import numpy as np, ml_dtypes
CORES = [16,32,48,64,80]
N = 5
BF = ml_dtypes.bfloat16
def gentries(a):
    return np.ascontiguousarray(a.reshape(8, 16, -1).transpose(0, 2, 1)).reshape(8, -1)
def gtable(e):
    e = np.asarray(e); return np.ascontiguousarray(e.reshape(8, -1, 16).transpose(0, 2, 1)).reshape(128, -1).astype(np.int32)
V, M, KK, RO, S, TH = 2048, 192, 512, 5, 2, 11
W = V + M * RO
def parts(rng):
    c = rng.integers(-60, 61, (N, 8, 8, V)); s = rng.integers(5, 36, (N, 8, 8, V))
    x = np.stack([c + s, s - c], axis=3).reshape(N, 8, 16, V)
    nb = rng.integers(0, V, (N, 8, 16, V))
    sh = (N, 8, 8, KK // 2); cut = rng.random(sh) < 0.25; h = rng.integers(-60, 61, sh); big = rng.integers(60, 128, (4,) + sh)
    k0 = np.stack([np.where(cut, h, big[0]), big[1]], axis=3).reshape(N, 8, 16, KK // 2)
    k1 = np.stack([big[2], np.where(cut, -h, big[3])], axis=3).reshape(N, 8, 16, KK // 2)
    k = np.stack([k0, k1], axis=-1).reshape(N, 8, 16, KK)
    z = rng.integers(-127, 128, (N, 8, 16, M)); p = rng.integers(0, V, (N, 8, M))
    p = np.where(rng.random(p.shape) < 0.15, p[..., ::-1], p)
    return x, nb, k, z, p, rng.integers(-127, 128, (N, 8, 16))
def distinct(rng):
    return np.argsort(rng.random((8, V)), axis=1)[:, :M]
def pack(x, nb, k, z, p, w):
    b = lambda a: np.ascontiguousarray(a.reshape(N, 128, -1)).astype(np.float32).astype(BF)
    return {"xc": b(x), "nb": np.ascontiguousarray(nb.reshape(N, 128, V)).astype(np.int32), "kc": b(k), "zi": b(z),
            "ps": np.stack([gtable(a) for a in p]), "wt": np.ascontiguousarray(w.reshape(N, 128, 1)).astype(np.int32)}
def setup_inputs(rng):
    return pack(*parts(rng))
def setup_inputs_spread(rng):
    x, nb, k, z, p, w = parts(rng)
    x = 127 - np.floor(255 * rng.random(x.shape) * rng.random((N, 8, 1, V)) ** rng.integers(0, 3, (N, 8, 1, V))).astype(np.int64)
    k = 127 - np.floor(255 * rng.random(k.shape) * rng.random((N, 8, 1, KK)) ** rng.integers(1, 4, (N, 8, 1, KK))).astype(np.int64)
    z = np.rint(z * rng.random((N, 8, 1, M)) ** 2).astype(np.int64); w = np.rint(w * rng.random((N, 8, 16)) ** 2).astype(np.int64)
    p[:, ::2] = np.floor(V * rng.random((N, 4, M)) ** 3).astype(np.int64)
    return pack(x, nb, k, z, np.minimum(p, V - 1), w)
def setup_inputs_ends(rng):
    x, nb, k, z, p, w = parts(rng)
    sg = lambda sh: np.where(rng.random(sh) < 0.5, 127, -127)
    def recs(n, a, b):
        h = rng.random((N, 8, 1, n)); return np.where(h < a, 127, np.where(h < b, -127, sg((N, 8, 16, n))))
    x = recs(V, 0.35, 0.5); k = recs(KK, 0.5, 0.6); w = sg((N, 8, 16)); z = sg((N, 8, 16, M))
    x[..., V - 1] = 127; x[..., V - 2] = 127; x[:, ::2, :, 0] = 127; x[:, 1::2, :, 0] = -127
    for i in (1, M - 1): z[..., i] = w
    for i in (0, M - 2): z[..., i] = -w
    for u in ((16 * 127 * 127) & (KK - 1), (-16 * 127 * 127) & (KK - 1)): k[..., u] = 127; k[..., u ^ 1] = -127
    e = np.where(rng.random(nb.shape) < 0.5, 0, V - 1); nb = np.where(rng.random((N, 8, 1, V)) < 0.72, e, nb)
    nb[..., 0] = np.where(np.arange(16) % 3 == 0, 0, V - 1); nb[..., V - 1] = np.where(np.arange(16) % 4 == 3, V - 1, 0); nb[..., V - 2] = np.where(np.arange(16) % 2 == 0, 0, V - 1)
    p = np.where(rng.random(p.shape) < 0.93, np.where(rng.random(p.shape) < 0.5, 0, V - 1), p); p[..., M - 1] = V - 2
    d = np.argsort(rng.random((8, V - 2)), axis=1)[:, :M] + 1; d[::2, 0] = V - 1; d[::2, M - 1] = 0; d[1::2, 0] = 0; d[1::2, M - 1] = V - 1
    p[N - 1] = d
    return pack(x, nb, k, z, p, w)
def setup_inputs_corners(rng):
    x, nb, k, z, p, w = parts(rng); v = np.arange(V); i = np.arange(M)
    for r in range(N):
        for g in range(8):
            m = (g + r) % 8; o = (3 * g + r) % 8
            if m == 0: nb[r, g] = v
            elif m == 1: nb[r, g] = (v + 1) & (V - 1)
            elif m == 2: nb[r, g] = 0
            elif m == 3: nb[r, g] = V - 1
            elif m == 4: nb[r, g, ::2] = v; nb[r, g, 1::4] = 0; nb[r, g, 3::4] = V - 1
            elif m == 5: nb[r, g] = (v - 1) & (V - 1)
            elif m == 6: nb[r, g] = int(rng.integers(0, V))
            if o < 7: p[r, g] = ((V - 1 + i // 2) & (V - 1), 0 * i + V - 1, 0 * i, i, V - M + i, i // 16, V - 1 - i)[o]
    h = rng.random((N, 8, 1, V)); x = np.where(h < 0.05, -127, np.where(h < 0.1, 127, np.where(h < 0.15, 0, x)))
    h = rng.random((N, 8, 1, KK)); k = np.where(h < 0.1, -127, np.where(h < 0.3, 127, k))
    z[:, 0] = 0; z[:, 3] = 0; z[:, 5] = np.where(rng.random((N, 16, M)) < 0.5, 127, -127); w[:, 2] = 0; w[:, 6] = 127
    return pack(x, nb, k, z, p, w)
def setup_inputs_crowd(rng):
    x, nb, k, z, p, w = parts(rng)
    for r in range(N):
        d = distinct(rng)
        for g in range(8):
            one = (0, V - 1, int(rng.integers(0, V)))[int(rng.integers(0, 3))]
            m = 0 if r == 0 else 3 if r in (1, 3) else (g + r) % 4
            if m == 3: p[r, g] = d[g]
            elif m == 2: p[r, g] = rng.choice(np.array([one, (one + 1) & (V - 1), (one + 7) & (V - 1)]), M)
            else:
                p[r, g] = one
                if m == 1: p[r, g, (0, M - 1)[int(rng.integers(0, 2))]] = (one + 1) & (V - 1)
    p[3, 0, M - 1] = p[3, 0, 0]
    few = rng.integers(0, V, (N, 4)); few[:, 0] = 0; few[:, 1] = V - 1
    for r in range(N):
        for g in (1, 5): nb[r, g] = few[r][rng.integers(0, 4, (16, V))]
    x[:, 6] = np.where(rng.random((N, 16, V)) < 0.02, -127, 127); k[:, 6] = np.where(rng.random((N, 16, KK)) < 0.02, -127, 127)
    return pack(x, nb, k, z, p, w)
def setup_inputs_ties(rng):
    x, nb, k, z, p, w = parts(rng)
    h = rng.random(x.shape); x = np.where(h < 0.2, -1, np.where(h < 0.5, 0, 1))
    h = rng.random(k.shape); k = np.where(h < 0.1, -1, np.where(h < 0.25, 0, np.where(h < 0.4, 1, 127)))
    nb[:, ::2, 8:] = nb[:, ::2, :8]
    return pack(x, nb, k, rng.integers(-3, 4, z.shape), p, rng.integers(-2, 3, w.shape))
def check_inputs(d):
    bad = []
    for key, lo, hi in (("xc", -127, 127), ("nb", 0, V - 1), ("kc", -127, 127), ("zi", -127, 127), ("ps", 0, V - 1), ("wt", -127, 127)):
        a = np.asarray(d[key]).astype(np.float64)
        if not (np.min(a) >= lo and np.max(a) <= hi): bad.append("range of " + key)
        elif np.any(a != np.floor(a)): bad.append("whole numbers in " + key)
    return bad
def relist(child, xa, xb, a, b, other):
    c = child[:, np.arange(16) ^ 1][:, :, None, :]
    oa = np.add.reduce(xa + c >= 0, axis=1, dtype=np.int32); ob = np.add.reduce(xb + c >= 0, axis=1, dtype=np.int32)
    s = np.maximum(oa, ob)
    return np.where(s < TH, other[:, None, :], np.where(ob > oa, b, a)), s
def reference(xc, nb, kc, zi, ps, wt):
    whole = lambda a: a.astype(np.float32).astype(np.int32).reshape(N, 8, 16, -1)
    X = np.zeros((N, 8, 16, W), np.int32); X[..., :V] = whole(xc)
    L = np.zeros((N, 8, 16, W), np.int64); L[..., :V] = nb.reshape(N, 8, 16, V)
    sib = np.tile(np.arange(W), (N, 8, 1)); K = whole(kc); w = wt.astype(np.int64).reshape(N, 8, 16, 1)
    z = whole(zi); p = np.stack([gentries(a) for a in ps]).astype(np.int64); A = np.zeros(N, np.int64)
    before = np.arange(M)[:, None] > np.arange(M)[None, :]
    for t in range(RO):
        n = V + M * t + np.arange(M)
        for r in range(N):
            q = (r + S * t) % N; pp = p[r]; zz = z[r]
            act = ~np.any((pp[:, :, None] == pp[:, None, :]) & before, axis=2)
            u = (np.add.reduce(w[q] * zz, axis=1) + A[q]) & (KK - 1)
            xp = np.take_along_axis(X[q], pp[:, None, :], 2)
            C = np.minimum(xp, np.take_along_axis(K[q], u[:, None, :], 2)); E = np.minimum(xp, np.take_along_axis(K[q], (u ^ 1)[:, None, :], 2))
            a = np.take_along_axis(L[q], pp[:, None, :], 2)
            for g in range(8):
                m = act[g]; X[q, g][:, pp[g, m]] = C[g][:, m]; X[q, g][:, n[m]] = E[g][:, m]; sib[q, g][pp[g, m]] = n[m]
            b = np.take_along_axis(sib[q], a.reshape(8, 16 * M), 1).reshape(8, 16, M)
            xa = np.take_along_axis(X[q], a.reshape(8, 1, 16 * M), 2).reshape(8, 16, 16, M)
            xb = np.take_along_axis(X[q], b.reshape(8, 1, 16 * M), 2).reshape(8, 16, 16, M)
            lc, sc = relist(C, xa, xb, a, b, np.tile(n, (8, 1))); le, se = relist(E, xa, xb, a, b, pp)
            for g in range(8):
                m = act[g]; L[q, g][:, pp[g, m]] = lc[g][:, m]; L[q, g][:, n[m]] = le[g][:, m]
            A[q] = np.sum(act)
            top = np.argmax(sc, axis=1)
            p[r] = np.where(act, np.take_along_axis(lc, top[:, None, :], 1)[:, 0], (pp + 1) & (V - 1))
            z[r] = np.where(act[:, None, :], (zz + C) >> 1, zz)
    return {"yx": X.reshape(N, 128, W).astype(np.float32).astype(BF), "yn": L.reshape(N, 128, W).astype(np.float32)}

@@ -1,0 +1,612 @@
+import math
+from concourse.mybir import AluOpType as OP, ActivationFunctionType as AF
+
+V, M, KK, RO, ST = 2048, 192, 512, 5, 2
+W = V + M * RO
+ALT = W
+MAGIC = 12582912.0
+LN2 = math.log(2.0)
+KD = (8, 8, 8, 8, 8)
+AV = 160
+CH = ((0, 64), (64, 128), (128, 192))
+K2 = 4
+KU = 15
+K1 = 1
+CUT = 2
+EG = 0
+BM = False
+EARLY = False
+
+SCRATCH = {
+    "X": ("sbuf", [128, W], "bfloat16"), "L": ("sbuf", [128, W + W - M], "float32"), "SB": ("sbuf", [128, W], "bfloat16"),
+    "NS": ("sbuf", [128, M], "bfloat16"), "ID": ("sbuf", [128, W - M], "float32"), "NB": ("sbuf", [128, V], "int32"),
+    "K0": ("sbuf", [128, KK], "bfloat16"), "K1": ("sbuf", [128, KK], "bfloat16"),
+    "psi": ("sbuf", [128, 12], "int32"), "wti": ("sbuf", [128, 1], "int32"), "wf": ("sbuf", [128, 1], "float32"),
+    "J": ("sbuf", [128, M], "bfloat16"), "Jg": ("sbuf", [128, 128], "bfloat16"), "J16": ("sbuf", [128, M], "float32"),
+    "pc": ("sbuf", [128, 128], "int32"), "pc2": ("sbuf", [128, 128], "int32"), "ci": ("sbuf", [128, 4], "int32"),
+    "cf": ("sbuf", [128, 12], "float32"), "cG": ("sbuf", [128, 12], "int32"), "cGu": ("sbuf", [128, 12], "uint16"),
+    "nG": ("sbuf", [128, 12 * RO], "float32"), "mask": ("sbuf", [128, M], "float32"), "thr": ("sbuf", [128, M], "float32"),
+    "gx": ("sbuf", [128, M], "float16"), "wG": ("sbuf", [128, 12], "float32"),
+    "I32": ("sbuf", [128, 128], "float32"), "on32": ("sbuf", [128, 128], "float32"),
+    "CKC": ("sbuf", [128, 2 * M], "bfloat16"), "CKb": ("sbuf", [128, 2 * M], "float32"),
+    "CKE0": ("sbuf", [128, 2 * M], "float32"), "CKE1": ("sbuf", [128, 2 * M], "float32"), "q4": ("sbuf", [128, M], "bfloat16"),
+    "pGf": ("sbuf", [128, 16], "float32"), "EQ": ("sbuf", [128, 12 * M], "bfloat16"),
+    "dup": ("sbuf", [128, M], "bfloat16"), "act": ("sbuf", [128, M], "bfloat16"), "act4": ("sbuf", [128, M], "bfloat16"),
+    "cnt": ("sbuf", [128, 1], "float32"), "of": ("sbuf", [128, 36], "float32"), "ou": ("sbuf", [128, 24], "uint16"),
+    "ui": ("sbuf", [128, 24], "int32"), "uu": ("sbuf", [128, 12], "uint16"),
+    "Ku": ("sbuf", [128, 2 * M], "bfloat16"), "CE": ("sbuf", [128, 2 * M], "bfloat16"),
+    "ab": ("sbuf", [128, 2 * M], "uint16"), "bv": ("sbuf", [128, M], "float16"),
+    "av": ("sbuf", [128, M], "float32"), "xp": ("sbuf", [128, M], "bfloat16"),
+    "sg": ("sbuf", [128, 16 * M], "bfloat16"), "xab": ("sbuf", [128, 32 * M], "bfloat16"),
+    "cC": ("sbuf", [128, 32 * M], "bfloat16"), "cE": ("sbuf", [128, 32 * M], "bfloat16"),
+    "NC": ("sbuf", [128, M], "float32"), "NE": ("sbuf", [128, M], "float32"),
+    "k1": ("sbuf", [128, M], "float32"), "k2": ("sbuf", [128, M], "float32"),
+    "rC": ("sbuf", [128, M], "bfloat16"), "rE": ("sbuf", [128, M], "bfloat16"), "vv": ("sbuf", [128, M], "bfloat16"),
+    "ec": ("sbuf", [128, M], "float32"), "mk": ("sbuf", [128, M], "float16"),
+    "dm": ("sbuf", [128, M], "bfloat16"), "zy": ("sbuf", [128, M], "float32"),
+}
+for _n in ("I", "nI", "Ih", "I256", "Pm", "nPm", "Bk", "TT", "t1", "t2"):
+    SCRATCH[_n] = ("sbuf", [128, 128], "bfloat16")
+for _n in ("Z1", "Z16", "Z8", "Zd", "Zw"):
+    SCRATCH[_n] = ("sbuf", [128, 144], "bfloat16")
+for _t in range(RO):
+    SCRATCH["mp%d" % _t] = ("sbuf", [128, M + 12], "uint16")
+    SCRATCH["mz%d" % _t] = ("sbuf", [128, M], "bfloat16")
+for _t in range(RO - 1):
+    SCRATCH["sp%d" % _t] = ("sbuf", [128, M + 12], "uint16")
+    SCRATCH["sz%d" % _t] = ("sbuf", [128, M], "bfloat16")
+for _b in range(8):
+    SCRATCH["P%d" % _b] = ("psum", [128, 512], "float32")
+
+DMAS = ["dps", "dwt", "dzi", "dkc", "dxc", "dnb0", "dnb1", "dnb2", "dnb3", "dyx", "dyn0", "dyn1"]
+SEMAPHORES = ["sV", "sA", "sP", "sG", "sent"] + DMAS + ["ap%d" % t for t in range(1, RO)] + ["az%d" % t for t in range(1, RO)]
+
+
+def rank_program(g, core, T, topo):
+    rank = T.rank_of(core)
+    if rank is None:
+        return
+    n_ranks = len(T.cores)
+    nxt = T.cores[(rank + ST) % n_ranks]
+    rid, pid, _se = topo.addr(nxt)
+    emask = topo.mask(core, nxt)
+    n_eng = len(topo.engines(core, nxt))
+    n_in = len(topo.engines(T.cores[(rank - ST) % n_ranks], core))
+
+    Q = {"V": g.vector, "A": g.scalar, "P": g.tensor, "G": g, "S": g.sync}
+    count = {"sV": 0, "sA": 0, "sP": 0, "sG": 0}
+    seen = {e: {} for e in Q}
+    clock = {}
+    wrote, read = {}, {}
+
+    def need(e, ev):
+        s, val = ev
+        if seen[e].get(s, 0) >= val:
+            return
+        Q[e].wait_ge(T.sem[s], val)
+        for s2, v2 in clock.get(ev, {}).items():
+            if seen[e].get(s2, 0) < v2:
+                seen[e][s2] = v2
+        seen[e][s] = val
+
+    def order(e, own, r, w):
+        evs = {}
+
+        def add(ev, same_ok):
+            if ev[0] == own and same_ok:
+                return
+            evs[ev[0]] = max(evs.get(ev[0], 0), ev[1])
+        for k in r:
+            if k in wrote:
+                add(wrote[k], e == "P")
+            if k[0] == "P" and k[1:].isdigit():
+                for ev in read.get(k, []):
+                    add(ev, True)
+        for k in w:
+            if k in wrote:
+                add(wrote[k], e == "P")
+            for ev in read.get(k, []):
+                add(ev, e == "P")
+        for s in sorted(evs, key=lambda s: s == own):
+            need(e, (s, evs[s]))
+
+    def done(e, ev, r, w):
+        clock[ev] = dict(seen[e])
+        for k in r:
+            read.setdefault(k, []).append(ev)
+        for k in w:
+            wrote[k] = ev
+            read[k] = []
+
+    def op(e, call, r, w):
+        s = "s" + e
+        order(e, s, r, w)
+        count[s] += 1
+        call().then_inc(T.sem[s], 1)
+        done(e, (s, count[s]), r, w)
+
+    def dma(e, sem, out, in_, r, w):
+        order(e, sem, r, w)
+        Q[e].dma_start(out, in_).then_inc(T.sem[sem], 16)
+        done(e, (sem, 16), r, w)
+
+    def send(src, dst, sem, r):
+        order("G", "sent", r, [])
+        g.remote_dma(T[dst][:], T[src][:], T.sem[sem], T.sem["sent"], pid, rid, emask)
+
+    v, a, pe = g.vector, g.scalar, g.tensor
+
+    def ts(out, in0, s1, s2, o0, o1, r, w):
+        if s2 is None:
+            op("V", lambda: v.tensor_scalar(out, in0, s1, None, o0), r, w)
+        else:
+            op("V", lambda: v.tensor_scalar(out, in0, s1, s2, o0, o1), r, w)
+
+    def tt(out, in0, in1, o, r, w):
+        op("V", lambda: v.tensor_tensor(out, in0, in1, o), r, w)
+
+    def cp(out, in_, r, w):
+        op("V", lambda: v.tensor_copy(out, in_), r, w)
+
+    def ms(out, val, w):
+        op("V", lambda: v.memset(out, val), [], w)
+
+    def ac(out, in_, r, w, f=AF.Identity, bias=0.0, scale=1.0, acc=None):
+        op("A", lambda: a.activation(out, in_, f, bias, scale, accum_out=acc), r, w)
+
+    def ag(out, in_, r, w):
+        op("A", lambda: a.activation(out, in_, AF.Copy), r, w)
+
+    def mm(out, lhsT, rhs, st, sp, r, w):
+        op("P", lambda: pe.matmul(out, lhsT, rhs, st, sp), r, w)
+
+    def io(out, pat, base, cm, w, flt=True):
+        if flt:
+            op("G", lambda: g.iota(out, pat, base, cm, allow_small_or_imprecise_dtypes=True), [], w)
+        else:
+            op("G", lambda: g.iota(out, pat, base, cm), [], w)
+
+    def sel(Z, k):
+        return T[Z][:, 15 - k:143 - k]
+
+    def to_list(out, Z, src, keys, bank):
+        for m in range(16):
+            mm(out, sel(Z, m), src[:, m:M:16], m == 0, m == 15, keys + [Z], [bank])
+
+    P = [T["P%d" % b] for b in range(8)]
+    col = lambda j: T.cf[:, j:j + 1]
+    J128, J144 = T.J[:, 0:128], T.J[:, 0:144]
+    for t in range(1, RO):
+        wrote["mp%d" % t] = ("ap%d" % t, n_in)
+        wrote["mz%d" % t] = ("az%d" % t, n_in)
+
+    dma("S", "dps", T.psi[:], T.ps[:], [], ["psi"])
+    dma("A", "dwt", T.wti[:], T.wt[:], [], ["wti"])
+    dma("A", "dzi", T.mz0[:], T.zi[:], [], ["mz0"])
+    dma("S", "dkc", T.K0[:], T.kc[:], [], ["K0"])
+    dma("S", "dxc", T.X[:, 0:V], T.xc[:], [], ["X"])
+    for j in range(4):
+        dma("S", "dnb%d" % j, T.NB[:, 512 * j:512 * j + 512], T.nb[:, 512 * j:512 * j + 512], [], ["NB%d" % j])
+    io(T.pc[:], [[1, 128]], 0, 1, ["pc"], False)
+    io(T.J[:], [[1, M]], 0, 0, ["J"])
+    io(T.Jg[:], [[16, 8], [0, 16]], 0, 0, ["Jg"])
+    io(T.J16[:], [[0, 12], [1, 16]], 0, 0, ["J16"])
+    io(T.cG[:], [[1, 12]], 0, 0, ["cG"], False)
+    io(T.nG[:], [[16, 12 * RO]], V, 1, ["nG"])
+    io(T.L[:, ALT:ALT + V - 1], [[1, V - 1]], 1, 0, ["ALT"])
+    io(T.L[:, ALT + V - 1:ALT + W - M], [[1, W - M - V + 1]], 0, 0, ["ALT2"])
+    io(T.L[:, V:W], [[0, W - V]], 0, 0, ["Ln"])
+    ts(T.ci[:, 0:1], T.pc[:, 0:1], 15, None, OP.bitwise_and, None, ["pc"], ["ci0"])
+    ts(T.ci[:, 1:2], T.pc[:, 0:1], 1, None, OP.bitwise_and, None, ["pc"], ["ci1"])
+    cp(col(0), T.pc[:, 0:1], ["pc"], ["c0"])
+    ts(T.pc2[:], T.pc[:], 4, None, OP.arith_shift_right, None, ["pc"], ["pc2"])
+    cp(col(1), T.ci[:, 0:1], ["ci0"], ["c1"])
+    ts(col(8), T.ci[:, 1:2], -2.0, 1.0, OP.mult, OP.add, ["ci1"], ["c8"])
+    cp(T.SB[:, 0:128], T.pc2[:], ["pc2"], ["SB"])
+    tt(col(2), col(0), col(1), OP.subtract, ["c0", "c1"], ["c2"])
+    tt(col(4), col(0), col(8), OP.add, ["c0", "c8"], ["c4"])
+    ac(T.thr[:], T.J[:], ["J"], ["thr"], AF.Exp, 96 * LN2 + math.log(1.25), -LN2)
+    ts(T.I[:], J128, col(0), None, OP.is_equal, None, ["J", "c0"], ["I"])
+    ts(col(3), col(2), 15.0, None, OP.add, None, ["c2"], ["c3"])
+    ts(T.Bk[:], T.Jg[:], col(2), None, OP.is_equal, None, ["Jg", "c2"], ["Bk"])
+    ts(T.mask[:], T.J16[:], col(1), None, OP.is_equal, None, ["J16", "c1"], ["mask"])
+    cp(T.cGu[:], T.cG[:], ["cG"], ["cGu"])
+    ts(T.Z1[:], J144, col(3), None, OP.is_equal, None, ["J", "c3"], ["Z1"])
+    ts(T.Zd[:], J144, col(3), W / 16.0, OP.is_equal, OP.mult, ["J", "c3"], ["Zd"])
+    ts(T.nG[:], T.nG[:], col(2), None, OP.subtract, None, ["nG", "c2"], ["nG"])
+    ts(T.nPm[:], J128, col(4), -1.0, OP.is_equal, OP.mult, ["J", "c4"], ["nPm"])
+    ts(T.wG[:], T.nG[:, 0:12], -float(V), None, OP.add, None, ["nG"], ["wG"])
+    ac(T.wG[:], T.wG[:], ["wG"], ["wG"], AF.Exp, 95 * LN2, -LN2)
+    ts(T.I256[:], J128, col(0), 256.0, OP.is_equal, OP.mult, ["J", "c0"], ["I256"])
+    w0 = 128
+    while w0 < W:
+        w1 = min(2 * w0, W)
+        ac(T.SB[:, w0:w1], T.SB[:, 0:w1 - w0], ["SB"], ["SB"], AF.Identity, w0 / 16.0)
+        if w0 == 128:
+            ag(T.K1[:, 0:KK:2], T.K0[:, 1:KK:2], ["K0"], ["K1a"])
+            ag(T.K1[:, 1:KK:2], T.K0[:, 0:KK:2], ["K0"], ["K1b"])
+        w0 = w1
+    cp(T.wf[:], T.wti[:], ["wti"], ["wf"])
+    cp(T.pGf[:, 0:12], T.psi[:], ["psi"], ["pGf"])
+    ts(T.Zw[:], J144, col(3), T.wf[:], OP.is_equal, OP.mult, ["J", "c3", "wf"], ["Zw"])
+    tt(T.gx[:], T.pGf[:, 0:12].indirect(T.cGu[:, 0:12]), T.mask[:], OP.mult, ["pGf", "cGu", "mask"], ["gx"])
+    cp(T.mp0[:, M:M + 12], T.psi[:], ["psi"], ["mp0g"])
+    mm(P[6][:, 0:M], T.Bk[:], T.gx[:], True, True, ["Bk", "gx"], ["P6"])
+
+    def cuts_pe(t):
+        if t > 0:
+            mm(P[7][:, 16:17], T.on32[:], T.cnt[:], True, True, ["on32", "cnt"], ["P7"])
+        to_list(P[7][:, 0:12], "Zw", T["mz%d" % t], ["mz%d" % t], "P7")
+
+    def cuts_v(t, step):
+        if step == 0:
+            if t > 0:
+                ts(T.ui[:, 0:12], P[7][:, 0:12], P[7][:, 16:17], 262144.0, OP.add, OP.add, ["P7"], ["ui0"])
+            else:
+                ts(T.ui[:, 0:12], P[7][:, 0:12], 262144.0, None, OP.add, None, ["P7"], ["ui0"])
+        elif step == 1:
+            ts(T.ui[:, 12:24], T.ui[:, 0:12], KK - 1, None, OP.bitwise_and, None, ["ui0"], ["ui1"])
+        else:
+            cp(T.uu[:], T.ui[:, 12:24], ["ui1"], ["uu"])
+
+    def cuts_a():
+        ag(T.Ku[:, 0:M], T.K0[:].indirect(T.uu[:, 0:12]), ["K0", "uu"], ["Ku0"])
+        ag(T.Ku[:, M:2 * M], T.K1[:].indirect(T.uu[:, 0:12]), ["K1a", "K1b", "uu"], ["Ku1"])
+
+    cuts_pe(0)
+    cp(T.mp0[:, 0:M], P[6][:, 0:M], ["P6", "mp0g"], ["mp0"])
+    cuts_v(0, 0)
+    ts(T.Z16[:], J144, col(3), 16.0, OP.is_equal, OP.mult, ["J", "c3"], ["Z16"])
+    cuts_v(0, 1)
+    ts(T.Z8[:], J144, col(3), 8.0, OP.is_equal, OP.mult, ["J", "c3"], ["Z8"])
+    cuts_v(0, 2)
+    cuts_a()
+    ag(T.NS[:], T.SB[:, V:V + M], ["SB"], ["NS"])
+    ts(T.Pm[:], J128, col(4), None, OP.is_equal, None, ["J", "c4"], ["Pm"])
+    ts(T.nI[:], J128, col(0), -1.0, OP.is_equal, OP.mult, ["J", "c0"], ["nI"])
+    ts(T.Ih[:], J128, col(0), 0.5, OP.is_equal, OP.mult, ["J", "c0"], ["Ih"])
+    ts(T.t1[:], J128, col(0), 65536.0, OP.is_gt, OP.mult, ["J", "c0"], ["t1"])
+    ts(T.t2[:], J128, col(0), -1024.0, OP.is_equal, OP.mult, ["J", "c0"], ["t2"])
+    ms(T.CKC[:, 0:M], -31.25, ["CKCa"])
+    ms(T.CKC[:, M:2 * M], -32.0, ["CKCb"])
+    ms(T.q4[:], -0.25, ["q4"])
+    tt(T.t1[:], T.t1[:], T.Bk[:], OP.mult, ["t1", "Bk"], ["t1"])
+    tt(T.t2[:], T.t2[:], T.Bk[:], OP.add, ["t2", "Bk"], ["t2"])
+    ts(col(6), col(1), KD[0] - 0.5, 128.0, OP.is_ge, OP.mult, ["c1"], ["c6"])
+    ts(col(7), col(1), KD[RO - 1] - 0.5, 128.0, OP.is_ge, OP.mult, ["c1"], ["c7"])
+    tt(T.TT[:], T.t1[:], T.t2[:], OP.add, ["t1", "t2"], ["TT"])
+    ac(T.I32[:], T.I[:], ["I"], ["I32"])
+    ac(T.on32[:], T.I[:], ["I"], ["on32"], AF.Identity, 1.0 / 16, 0.0)
+    ac(T.CKb[:], T.CKC[:], ["CKCa", "CKCb"], ["CKb"], AF.Identity, 0.25)
+    ac(T.CKE0[:], T.CKb[:], ["CKb", "c6"], ["CKE0"], AF.Identity, col(6))
+    ac(T.CKE1[:], T.CKb[:], ["CKb", "c7"], ["CKE1"], AF.Identity, col(7))
+
+    XA, XB = ["xa0", "xa1", "xa2"], ["xb0", "xb1", "xb2"]
+    LK = ["L0", "L1", "L2", "L3", "Ln"]
+    H = ((0, 128, 6), (128, 192, 5))
+    carry = []
+
+    for t in range(RO):
+        last = t == RO - 1
+        n0 = V + M * t
+        n1 = n0 + M
+        mp, mz = T["mp%d" % t], T["mz%d" % t]
+        kp, kz = "mp%d" % t, "mz%d" % t
+        pG = mp[:, M:M + 12]
+        C, E = T.CE[:, 0:M], T.CE[:, M:2 * M]
+        kd = KD[t]
+
+        if t > 0:
+            cp(T.pGf[:, 0:12], pG, [kp], ["pGf"])
+            ag(T.xp[:], T.X[:, 0:n0].indirect(pG), ["X", "Xn", kp], ["xp"])
+        for c in range(12):
+            e0 = c * M
+            ts(T.EQ[:, e0:e0 + M - 16 * c], mp[:, 16 * c:M], T.pGf[:, c:c + 1], T.wG[:, c:c + 1], OP.is_equal, OP.mult,
+               [kp, "pGf", "wG"], ["EQ%d" % c])
+            mm(P[5][:, 16 * c:M], T.Bk[:], T.EQ[:, e0:e0 + M - 16 * c], c == 0, c == 11, ["Bk", "EQ%d" % c], ["P5"])
+        if carry:
+            carry.pop(0)()
+        tt(T.dup[:], P[5][:, 0:M], T.thr[:], OP.is_ge, ["P5", "thr"], ["dup"])
+        to_list(P[6][:, 0:12], "Zd", T.dup, ["dup"], "P6")
+        ac(T.act[:], T.dup[:], ["dup"], ["act", "cnt"], AF.Identity, 1.0, -1.0, T.cnt[:])
+        while carry:
+            carry.pop(0)()
+        ac(T.act4[:], T.dup[:], ["dup"], ["act4"], AF.Identity, 4096.0, -4096.0)
+        if t > 0:
+            cp(T.ab[:, 0:M], T.L[:, 0:n0].indirect(pG), LK + [kp], ["a"])
+        tt(T.of[:, 24:36], P[6][:, 0:12], T.nG[:, 12 * t:12 * t + 12], OP.min, ["P6", "nG"], ["of2"])
+        tt(T.of[:, 0:12], P[6][:, 0:12], T.pGf[:, 0:12], OP.add, ["P6", "pGf"], ["of0"])
+        tt(T.of[:, 12:24], T.of[:, 24:36], T.pGf[:, 0:12], OP.max, ["of2", "pGf"], ["of1"])
+        cp(T.ou[:], T.of[:, 0:24], ["of0", "of1"], ["ou"])
+        off, offv = T.ou[:, 12:24], T.ou[:, 0:12]
+
+        def a_values():
+            ac(T.av[:], T.L[:, 0:ALT + n0].indirect(offv), LK + ["ALT", "ALT2", "ou"], ["av"], AF.Identity, 0.0, 1.0 / 4096)
+
+        def gat_s(j):
+            i0, i1 = CH[j]
+            ag(T.sg[:, 16 * i0:16 * i1], T.SB[:, 0:n1].indirect(T.ab[:, i0:i1]), ["SB", "a"], ["sg%d" % j])
+
+        def sib_pe(j):
+            i0, i1 = CH[j]
+            bank = 5 + j % 2
+            for k in range(16):
+                mm(P[bank][:, 0:i1 - i0], sel("Z1", k), T.sg[:, 16 * i0 + k:16 * i1:16], k == 0, k == 15, ["Z1", "sg%d" % j], ["P%d" % bank])
+
+        def sib_v(j):
+            i0, i1 = CH[j]
+            bank = 5 + j % 2
+            ts(T.ab[:, M + i0:M + i1], P[bank][:, 0:i1 - i0], col(2), None, OP.subtract, None, ["P%d" % bank, "c2"], ["b%d" % j])
+
+        def gat_b(j):
+            i0, i1 = CH[j]
+            ag(T.xab[:, 16 * (M + i0):16 * (M + i1)], T.X[:, 0:n1].indirect(T.ab[:, M + i0:M + i1]), ["X", "Xn", "b%d" % j], ["xb%d" % j])
+
+        cp(T.SB[:, 0:n1].indirect(off), T.NS[:], ["NS", "ou"], ["SB"])
+        if t > 0:
+            a_values()
+            gat_s(0)
+        if t == 0:
+            tt(C, T.X[:, 0:n0].indirect(pG), T.Ku[:, 0:M], OP.min, ["X", kp, "Ku0"], ["C"])
+            tt(E, T.X[:, 0:n0].indirect(pG), T.Ku[:, M:2 * M], OP.min, ["X", kp, "Ku1"], ["E"])
+        else:
+            tt(C, T.xp[:], P[1][:, 0:M], OP.min, ["xp", "P1"], ["C"])
+            tt(E, T.xp[:], P[1][:, M:2 * M], OP.min, ["xp", "P1"], ["E"])
+        mm(P[0][:, 0:M], T.nPm[:], C, True, False, ["nPm", "C"], ["P0"])
+        mm(P[0][:, 0:M], T.I256[:], T.dup[:], False, True, ["I256", "dup"], ["P0"])
+        mm(P[0][:, M:2 * M], T.nPm[:], E, True, True, ["nPm", "E"], ["P0"])
+        if not last:
+            mm(P[7][:, 0:M], T.I[:], C, True, False, ["I", "C"], ["P7"])
+            mm(P[7][:, 0:M], T.nI[:], mz[:], False, True, ["nI", kz], ["P7"])
+        cp(T.X[:, 0:n1].indirect(off), C, ["C", "ou"], ["X"])
+        if not last:
+            tt(T.dm[:], P[7][:, 0:M], T.act[:], OP.mult, ["P7", "act"], ["dm"])
+            mm(P[7][:, 0:M], T.I[:], T.q4[:], True, False, ["I", "q4"], ["P7"])
+            mm(P[7][:, 0:M], T.I[:], mz[:], False, False, ["I", kz], ["P7"])
+            mm(P[7][:, 0:M], T.Ih[:], T.dm[:], False, True, ["Ih", "dm"], ["P7"])
+        tt(T.X[:, n0:n1], E, T.act[:], OP.mult, ["E", "act", "X"], ["Xn"])
+        if last:
+            dma("S", "dyx", T.yx[:], T.X[:], ["X", "Xn"], [])
+        if t == 0:
+            for j in range(3):
+                cp(T.L[:, 512 * j:512 * j + 512], T.NB[:, 512 * j:512 * j + 512], ["NB%d" % j], ["L%d" % j])
+            cp(T.ab[:, 0:M], T.NB[:].indirect(pG), ["NB0", "NB1", "NB2", "NB3", kp], ["a"])
+            cp(T.L[:, 1536:V], T.NB[:, 1536:V], ["NB3"], ["L3"])
+            gat_s(0)
+
+        sib_pe(0)
+        gat_s(1)
+        if not last:
+            ac(T.zy[:], P[7][:, 0:M], ["P7"], ["zy"], AF.Identity, MAGIC)
+        if t == 0:
+            a_values()
+        if not last:
+            ac(T["sz%d" % t][:], T.zy[:], ["zy"], ["sz%d" % t], AF.Identity, -MAGIC)
+            send("sz%d" % t, "mz%d" % (t + 1), "az%d" % (t + 1), ["sz%d" % t])
+        if t == 0:
+            io(T.ID[:], [[1, W - M]], 0, 0, ["ID"])
+        mm(P[1][:, 0:M], T.I[:], T.CKC[:, 0:M], True, False, ["I", "CKCa"], ["P1"])
+        mm(P[1][:, 0:M], T.I256[:], T.dup[:], False, False, ["I256", "dup"], ["P1"])
+        mm(P[1][:, 0:M], T.I32[:], T.av[:], False, False, ["I32", "av"], ["P1"])
+        cke = "CKE1" if last else "CKE0"
+        mm(P[2][:, 0:2 * M], T.I32[:], T[cke][:], True, False, ["I32", cke], ["P2"])
+        mm(P[2][:, 0:M], T.I32[:], T.av[:], False, False, ["I32", "av"], ["P2"])
+        half = AV // 2
+        cp(T.xab[:, 0:16 * half], T.X[:, 0:n1].indirect(T.ab[:, 0:half]), ["X", "Xn", "a"], ["xa2"])
+        sib_v(0)
+        sib_pe(1)
+        cp(T.xab[:, 16 * half:16 * AV], T.X[:, 0:n1].indirect(T.ab[:, half:AV]), ["X", "Xn", "a"], ["xa0"])
+        sib_v(1)
+        if AV < M:
+            ag(T.xab[:, 16 * AV:16 * M], T.X[:, 0:n1].indirect(T.ab[:, AV:M]), ["X", "Xn", "a"], ["xa1"])
+        gat_s(2)
+        gat_b(0)
+        ac(T.NC[:], T.L[:, ALT + M * t:ALT + M * t + M], ["ALT"], ["NC"], AF.Identity, 130.0 + (V - 1 - 1024) / 4096.0, 1.0 / 4096)
+        gat_b(1)
+
+        ks = list(range(kd, 16))
+        npre = min(3, len(ks) // 2)
+        todo = [((ks[2 * u], s), (ks[2 * u + 1], s)) for s in (0, 1) for u in range(npre)]
+        todo += [((k, 0), (k, 1)) for k in ks[2 * npre:]]
+        st = {"staged": [], "signed": [], "n": 0, "red": 0}
+
+        def stage():
+            if not todo:
+                return
+            unit = todo.pop(0)
+            slot = kd + st["n"]
+            bank = (3, 4, 1)[st["n"] % 3]
+            st["n"] += 1
+            kb = "P%d" % bank
+            if unit[0][0] == unit[1][0]:
+                mm(P[bank][:, 0:2 * M], T.I[:], T.xab[:, unit[0][0]:32 * M:16], True, False, ["I"] + XA + XB, [kb])
+                mm(P[bank][:, 0:M], T.Pm[:], E, False, False, ["Pm", "E"], [kb])
+                mm(P[bank][:, M:2 * M], T.Pm[:], E, False, True, ["Pm", "E"], [kb])
+            else:
+                for h, (k, s) in enumerate(unit):
+                    mm(P[bank][:, M * h:M * h + M], T.Pm[:], E, True, False, ["Pm", "E"], [kb])
+                    mm(P[bank][:, M * h:M * h + M], T.I[:], T.xab[:, 16 * M * s + k:16 * M * (s + 1):16], False, True,
+                       ["I"] + (XB if s else XA), [kb])
+            st["staged"].append((unit, slot, bank))
+
+        def sign():
+            if not st["staged"]:
+                return
+            unit, slot, bank = st["staged"].pop(0)
+            ac(T.cE[:, 2 * M * slot:2 * M * (slot + 1)], P[bank][:, 0:2 * M], ["P%d" % bank], ["cE%d" % slot], AF.Sign, 0.5)
+            st["signed"].append((unit, slot))
+
+        def red(unit, slot, Z, keys):
+            st["red"] += 1
+            o = 2 * M * slot
+            if unit[0][0] == unit[1][0]:
+                mm(P[2][:, 0:2 * M], sel(Z, unit[0][0]), T.cE[:, o:o + 2 * M], False, st["red"] == 16, [Z] + keys, ["P2"])
+            else:
+                for h, (k, s) in enumerate(unit):
+                    mm(P[2][:, M * s:M * s + M], sel(Z, k), T.cE[:, o + M * h:o + M * h + M], False, st["red"] == 16 and h == 1,
+                       [Z] + keys, ["P2"])
+
+        def red_a():
+            if st["signed"]:
+                unit, slot = st["signed"].pop(0)
+                red(unit, slot, "Z8", ["cE%d" % slot])
+
+        def step():
+            sign()
+            stage()
+            if len(st["signed"]) > 1 or not st["staged"]:
+                red_a()
+
+        def e_a(k):
+            o = 2 * M * k
+            tt(T.cE[:, o:o + M], T.xab[:, k:16 * M:16], P[0][:, M:2 * M], OP.is_ge, XA + ["P0"], ["cEa%d" % k])
+
+        def e_on_v(k):
+            o = 2 * M * k
+            if k >= EG:
+                e_a(k)
+            tt(T.cE[:, o + M:o + 2 * M], T.xab[:, 16 * M + k:32 * M:16], P[0][:, M:2 * M], OP.is_ge, XB + ["P0"], ["cE%d" % k])
+            red(((k, 0), (k, 1)), k, "Z16", ["cEa%d" % k, "cE%d" % k])
+
+        def b_scores(j):
+            i0, i1 = CH[j]
+            if BM and j == 1:
+                i0 = 0
+            b = H[j // 2][2]
+            for k in range(16):
+                o = 2 * M * k + M
+                key = "cCb%d_%d" % (j, k)
+                tt(T.cC[:, o + i0:o + i1], T.xab[:, 16 * (M + i0) + k:16 * (M + i1):16], P[0][:, i0:i1], OP.is_ge,
+                   ["xb0", "xb%d" % j, "P0"], [key])
+                mm(P[b][:, i0:i1], sel("Z16", k), T.cC[:, o + i0:o + i1], False, j > 0 and k == 15, ["Z16", key], ["P%d" % b])
+                if j == 1 and k == K1:
+                    tt(T.k1[:], P[1][:, 0:M], T.NC[:], OP.max, ["P1", "NC"], ["k1"])
+                    stage()
+                if j == 2 and k == 2:
+                    sign()
+                    if not last:
+                        f_arg(0)
+                    sign()
+
+        def f_max(h):
+            i0, i1, b = H[h]
+            tt(P[b][:, i0:i1], P[b][:, i0:i1], T.k1[:, i0:i1], OP.max, ["P%d" % b, "k1"], ["P%d" % b])
+
+        def f_exp(h):
+            i0, i1, b = H[h]
+            if not last:
+                ac(T.vv[:, i0:i1], P[b][:, i0:i1], ["P%d" % b], ["vv%d" % h], AF.Exp, -176 * LN2, LN2)
+            ag(T.rC[:, i0:i1], P[b][:, i0:i1], ["P%d" % b], ["rC%d" % h])
+
+        def f_arg(h):
+            i0, i1, b = H[h]
+            mm(P[6][:, M + i0:M + i1], T.TT[:], T.vv[:, i0:i1], True, True, ["TT", "vv%d" % h], ["P6"])
+            ac(P[6][:, M + i0:M + i1], P[6][:, M + i0:M + i1], ["P6"], ["P6"], AF.Sign, 0.0, -1.0)
+
+        def f_sub(h):
+            i0, i1, b = H[h]
+            tt(T.ec[:, i0:i1], P[b][:, i0:i1], T.rC[:, i0:i1], OP.subtract, ["P%d" % b, "rC%d" % h], ["ec%d" % h])
+
+        def f_min(h):
+            i0, i1, b = H[h]
+            tt(T.mk[:, i0:i1], P[6][:, M + i0:M + i1], T.ec[:, i0:i1], OP.min, ["P6", "ec%d" % h], ["mk%d" % h])
+            mm(P[7][:, i0:i1], T.Bk[:], T.mk[:, i0:i1], True, True, ["Bk", "mk%d" % h], ["P7"])
+
+        for k in range(16):
+            o = 2 * M * k
+            tt(T.cC[:, o:o + M], T.xab[:, k:16 * M:16], P[0][:, 0:M], OP.is_ge, XA + ["P0"], ["cCa%d" % k])
+            mm(P[1][:, 0:M], sel("Z16", k), T.cC[:, o:o + M], False, k == 15, ["Z16", "cCa%d" % k], ["P1"])
+            if k == KU and not last:
+                cuts_pe(t + 1)
+            if k == K2:
+                sib_pe(2)
+            if k == K2 + 4:
+                sib_v(2)
+                gat_b(2)
+                ts(T.bv[:], T.ab[:, M:2 * M], -1024.0, 1.0 / 4096, OP.add, OP.mult, ["b0", "b1", "b2"], ["bv"])
+            if k == K2 + 5:
+                for (i0, i1, b) in H:
+                    mm(P[b][:, i0:i1], T.I[:], T.CKC[:, M + i0:M + i1], True, False, ["I", "CKCb"], ["P%d" % b])
+                    mm(P[b][:, i0:i1], T.I[:], T.bv[:, i0:i1], False, False, ["I", "bv"], ["P%d" % b])
+                mm(P[2][:, M:2 * M], T.I[:], T.bv[:], False, False, ["I", "bv"], ["P2"])
+            if k in (0, 10):
+                stage()
+        for k in range(EG // 2):
+            e_a(k)
+        if not BM:
+            b_scores(0)
+        for k in range(EG // 2, EG):
+            e_a(k)
+        b_scores(1)
+        if not last:
+            cuts_v(t + 1, 0)
+        f_max(0)
+        if not last:
+            cuts_v(t + 1, 1)
+        f_exp(0)
+        b_scores(2)
+        stage()
+        f_sub(0)
+        if not last:
+            f_min(0)
+        f_max(1)
+        f_exp(1)
+        if not last:
+            f_arg(1)
+            red_a()
+            cuts_v(t + 1, 2)
+        f_sub(1)
+        if not last:
+            sp = "sp%d" % t
+            ts(T[sp][:, 0:128], P[7][:, 0:128], 4096.0, 15 * 4096.0 + 1024.0, OP.mult, OP.add, ["P7"], [sp + "a"])
+            f_min(1)
+            to_list(P[7][:, M:M + 12], "Z1", T.mk, ["mk0", "mk1"], "P7")
+            sign()
+            stage()
+            red_a()
+            e_on_v(0)
+            ts(T[sp][:, 128:M + 12], P[7][:, 128:M + 12], 4096.0, 15 * 4096.0 + 1024.0, OP.mult, OP.add, ["P7"], [sp])
+            send(sp, "mp%d" % (t + 1), "ap%d" % (t + 1), [sp, sp + "a"])
+        ts(T.L[:, 0:n1].indirect(off), T.ec[:], 4096.0, 1024.0, OP.mult, OP.add, ["ec0", "ec1", "ou"], LK)
+        if last:
+            dma("S", "dyn0", T.yn[:, 0:n0], T.L[:, 0:n0], LK[:4], [])
+            stage()
+            red_a()
+            red_a()
+            e_on_v(0)
+        for k in range(1, kd):
+            step()
+            e_on_v(k)
+            if k == CUT and not last:
+                cuts_a()
+        while st["staged"] or st["signed"] or todo:
+            step()
+        if not last:
+            ag(P[1][:, 0:2 * M], T.Ku[:], ["Ku0", "Ku1"], ["P1"])
+            ag(T.NS[:], T.SB[:, n1:n1 + M], ["SB"], ["NS"])
+        ac(T.NE[:], T.ID[:, 0:n0].indirect(pG), ["ID", kp], ["NE"], AF.Identity, 130.0, 1.0 / 4096)
+
+        def e_max():
+            tt(T.k2[:], P[2][:, 0:M], T.NE[:], OP.max, ["P2", "NE"], ["k2"])
+            tt(P[2][:, M:2 * M], P[2][:, M:2 * M], T.k2[:], OP.max, ["P2", "k2"], ["P2"])
+            ac(T.rE[:], P[2][:, M:2 * M], ["P2"], ["rE"], AF.Identity, -0.25)
+
+        def e_end(n0=n0, n1=n1):
+            tt(P[2][:, M:2 * M], P[2][:, M:2 * M], T.rE[:], OP.subtract, ["P2", "rE"], ["P2"])
+            tt(T.L[:, n0:n1], P[2][:, M:2 * M], T.act4[:], OP.mult, ["P2", "act4", "Ln"], ["Ln"])
+
+        if last:
+            e_max()
+            e_end()
+            dma("A", "dyn1", T.yn[:, n0:n1], T.L[:, n0:n1], ["Ln"], [])
+        elif EARLY:
+            e_max()
+            carry.append(e_end)
+        else:
+            carry.extend([e_max, e_end])
+
+    g.wait_ge(T.sem["sent"], 2 * (RO - 1) * n_eng)
+    for s in ("sV", "sA", "sP", "sG"):
+        need("G", (s, count[s]))
+    for s in ("dyx", "dyn0", "dyn1"):
+        need("G", (s, 16))

@@ -4,22 +4,32 @@ from concourse.mybir import AluOpType as OP, ActivationFunctionType as AF
 V, M, KK, RO, ST = 2048, 192, 512, 5, 2
 W = V + M * RO
 ALT = W
+TOP = 95 * 4096
 MAGIC = 12582912.0
 LN2 = math.log(2.0)
-KD = (8, 8, 8, 8, 8)
-AV = 160
+KD = (10, 10, 10, 10, 10)
+AV = 176
 CH = ((0, 64), (64, 128), (128, 192))
-K2 = 4
+K2 = -2
 KU = 15
 K1 = 1
 CUT = 2
+KM = 4
+KA = 12
+F1 = 1
+F2 = 3
 EG = 0
+SO = True
+PRE = (3, 9)
+PRE3 = 0
+ZE = False
+S2 = True
 BM = False
-EARLY = False
+EARLY = True
 
 SCRATCH = {
-    "X": ("sbuf", [128, W], "bfloat16"), "L": ("sbuf", [128, W + W - M], "float32"), "SB": ("sbuf", [128, W], "bfloat16"),
-    "NS": ("sbuf", [128, M], "bfloat16"), "ID": ("sbuf", [128, W - M], "float32"), "NB": ("sbuf", [128, V], "int32"),
+    "X": ("sbuf", [128, W], "bfloat16"), "L": ("sbuf", [128, W], "float32"), "SB": ("sbuf", [128, W], "bfloat16"),
+    "NS": ("sbuf", [128, M], "bfloat16"), "ID": ("sbuf", [128, W + W - M], "float32"), "NB": ("sbuf", [128, V], "int32"),
     "K0": ("sbuf", [128, KK], "bfloat16"), "K1": ("sbuf", [128, KK], "bfloat16"),
     "psi": ("sbuf", [128, 12], "int32"), "wti": ("sbuf", [128, 1], "int32"), "wf": ("sbuf", [128, 1], "float32"),
     "J": ("sbuf", [128, M], "bfloat16"), "Jg": ("sbuf", [128, 128], "bfloat16"), "J16": ("sbuf", [128, M], "float32"),
@@ -27,16 +37,15 @@ SCRATCH = {
     "cf": ("sbuf", [128, 12], "float32"), "cG": ("sbuf", [128, 12], "int32"), "cGu": ("sbuf", [128, 12], "uint16"),
     "nG": ("sbuf", [128, 12 * RO], "float32"), "mask": ("sbuf", [128, M], "float32"), "thr": ("sbuf", [128, M], "float32"),
     "gx": ("sbuf", [128, M], "float16"), "wG": ("sbuf", [128, 12], "float32"),
-    "I32": ("sbuf", [128, 128], "float32"), "on32": ("sbuf", [128, 128], "float32"),
-    "CKC": ("sbuf", [128, 2 * M], "bfloat16"), "CKb": ("sbuf", [128, 2 * M], "float32"),
-    "CKE0": ("sbuf", [128, 2 * M], "float32"), "CKE1": ("sbuf", [128, 2 * M], "float32"), "q4": ("sbuf", [128, M], "bfloat16"),
+    "on32": ("sbuf", [128, 128], "float32"), "CKC": ("sbuf", [128, 2 * M], "bfloat16"),
+    "CKE0": ("sbuf", [128, 2 * M], "float16"), "CKE1": ("sbuf", [128, 2 * M], "float16"), "q4": ("sbuf", [128, M], "bfloat16"),
     "pGf": ("sbuf", [128, 16], "float32"), "EQ": ("sbuf", [128, 12 * M], "bfloat16"),
     "dup": ("sbuf", [128, M], "bfloat16"), "act": ("sbuf", [128, M], "bfloat16"), "act4": ("sbuf", [128, M], "bfloat16"),
-    "cnt": ("sbuf", [128, 1], "float32"), "of": ("sbuf", [128, 36], "float32"), "ou": ("sbuf", [128, 24], "uint16"),
+    "cnt": ("sbuf", [128, 1], "float32"), "of": ("sbuf", [128, 48], "float32"), "ou": ("sbuf", [128, 24], "uint16"),
     "ui": ("sbuf", [128, 24], "int32"), "uu": ("sbuf", [128, 12], "uint16"),
     "Ku": ("sbuf", [128, 2 * M], "bfloat16"), "CE": ("sbuf", [128, 2 * M], "bfloat16"),
     "ab": ("sbuf", [128, 2 * M], "uint16"), "bv": ("sbuf", [128, M], "float16"),
-    "av": ("sbuf", [128, M], "float32"), "xp": ("sbuf", [128, M], "bfloat16"),
+    "av": ("sbuf", [128, M], "float16"), "xp": ("sbuf", [128, M], "bfloat16"),
     "sg": ("sbuf", [128, 16 * M], "bfloat16"), "xab": ("sbuf", [128, 32 * M], "bfloat16"),
     "cC": ("sbuf", [128, 32 * M], "bfloat16"), "cE": ("sbuf", [128, 32 * M], "bfloat16"),
     "NC": ("sbuf", [128, M], "float32"), "NE": ("sbuf", [128, M], "float32"),
@@ -130,9 +139,9 @@ def rank_program(g, core, T, topo):
         Q[e].dma_start(out, in_).then_inc(T.sem[sem], 16)
         done(e, (sem, 16), r, w)
 
-    def send(src, dst, sem, r):
+    def send(src, dst, sem, r, c0=0, c1=M):
         order("G", "sent", r, [])
-        g.remote_dma(T[dst][:], T[src][:], T.sem[sem], T.sem["sent"], pid, rid, emask)
+        g.remote_dma(T[dst][:, c0:c1], T[src][:, c0:c1], T.sem[sem], T.sem["sent"], pid, rid, emask)
 
     v, a, pe = g.vector, g.scalar, g.tensor
 
@@ -177,7 +186,7 @@ def rank_program(g, core, T, topo):
     col = lambda j: T.cf[:, j:j + 1]
     J128, J144 = T.J[:, 0:128], T.J[:, 0:144]
     for t in range(1, RO):
-        wrote["mp%d" % t] = ("ap%d" % t, n_in)
+        wrote["mp%d" % t] = ("ap%d" % t, 2 * n_in)
         wrote["mz%d" % t] = ("az%d" % t, n_in)
 
     dma("S", "dps", T.psi[:], T.ps[:], [], ["psi"])
@@ -193,9 +202,9 @@ def rank_program(g, core, T, topo):
     io(T.J16[:], [[0, 12], [1, 16]], 0, 0, ["J16"])
     io(T.cG[:], [[1, 12]], 0, 0, ["cG"], False)
     io(T.nG[:], [[16, 12 * RO]], V, 1, ["nG"])
-    io(T.L[:, ALT:ALT + V - 1], [[1, V - 1]], 1, 0, ["ALT"])
-    io(T.L[:, ALT + V - 1:ALT + W - M], [[1, W - M - V + 1]], 0, 0, ["ALT2"])
-    io(T.L[:, V:W], [[0, W - V]], 0, 0, ["Ln"])
+    io(T.ID[:, 0:W], [[1, W]], 0, 0, ["ID"])
+    io(T.ID[:, ALT:ALT + V - 1], [[1, V - 1]], TOP + 1, 0, ["ALT"])
+    io(T.ID[:, ALT + V - 1:ALT + W - M], [[1, W - M - V + 1]], TOP, 0, ["ALT2"])
     ts(T.ci[:, 0:1], T.pc[:, 0:1], 15, None, OP.bitwise_and, None, ["pc"], ["ci0"])
     ts(T.ci[:, 1:2], T.pc[:, 0:1], 1, None, OP.bitwise_and, None, ["pc"], ["ci1"])
     cp(col(0), T.pc[:, 0:1], ["pc"], ["c0"])
@@ -267,7 +276,7 @@ def rank_program(g, core, T, topo):
     ts(T.Ih[:], J128, col(0), 0.5, OP.is_equal, OP.mult, ["J", "c0"], ["Ih"])
     ts(T.t1[:], J128, col(0), 65536.0, OP.is_gt, OP.mult, ["J", "c0"], ["t1"])
     ts(T.t2[:], J128, col(0), -1024.0, OP.is_equal, OP.mult, ["J", "c0"], ["t2"])
-    ms(T.CKC[:, 0:M], -31.25, ["CKCa"])
+    ms(T.CKC[:, 0:M], -31.0, ["CKCa"])
     ms(T.CKC[:, M:2 * M], -32.0, ["CKCb"])
     ms(T.q4[:], -0.25, ["q4"])
     tt(T.t1[:], T.t1[:], T.Bk[:], OP.mult, ["t1", "Bk"], ["t1"])
@@ -275,11 +284,9 @@ def rank_program(g, core, T, topo):
     ts(col(6), col(1), KD[0] - 0.5, 128.0, OP.is_ge, OP.mult, ["c1"], ["c6"])
     ts(col(7), col(1), KD[RO - 1] - 0.5, 128.0, OP.is_ge, OP.mult, ["c1"], ["c7"])
     tt(T.TT[:], T.t1[:], T.t2[:], OP.add, ["t1", "t2"], ["TT"])
-    ac(T.I32[:], T.I[:], ["I"], ["I32"])
     ac(T.on32[:], T.I[:], ["I"], ["on32"], AF.Identity, 1.0 / 16, 0.0)
-    ac(T.CKb[:], T.CKC[:], ["CKCa", "CKCb"], ["CKb"], AF.Identity, 0.25)
-    ac(T.CKE0[:], T.CKb[:], ["CKb", "c6"], ["CKE0"], AF.Identity, col(6))
-    ac(T.CKE1[:], T.CKb[:], ["CKb", "c7"], ["CKE1"], AF.Identity, col(7))
+    ts(T.CKE0[:], T.CKC[:], col(6), 0.25, OP.add, OP.add, ["CKCa", "CKCb", "c6"], ["CKE0"])
+    ts(T.CKE1[:], T.CKC[:], col(7), 0.25, OP.add, OP.add, ["CKCa", "CKCb", "c7"], ["CKE1"])
 
     XA, XB = ["xa0", "xa1", "xa2"], ["xb0", "xb1", "xb2"]
     LK = ["L0", "L1", "L2", "L3", "Ln"]
@@ -306,6 +313,8 @@ def rank_program(g, core, T, topo):
             mm(P[5][:, 16 * c:M], T.Bk[:], T.EQ[:, e0:e0 + M - 16 * c], c == 0, c == 11, ["Bk", "EQ%d" % c], ["P5"])
         if carry:
             carry.pop(0)()
+        if t > 0:
+            tt(C, T.xp[:], P[1][:, 0:M], OP.min, ["xp", "P1"], ["C"])
         tt(T.dup[:], P[5][:, 0:M], T.thr[:], OP.is_ge, ["P5", "thr"], ["dup"])
         to_list(P[6][:, 0:12], "Zd", T.dup, ["dup"], "P6")
         ac(T.act[:], T.dup[:], ["dup"], ["act", "cnt"], AF.Identity, 1.0, -1.0, T.cnt[:])
@@ -314,14 +323,21 @@ def rank_program(g, core, T, topo):
         ac(T.act4[:], T.dup[:], ["dup"], ["act4"], AF.Identity, 4096.0, -4096.0)
         if t > 0:
             cp(T.ab[:, 0:M], T.L[:, 0:n0].indirect(pG), LK + [kp], ["a"])
+            tt(E, T.xp[:], P[1][:, M:2 * M], OP.min, ["xp", "P1"], ["E"])
         tt(T.of[:, 24:36], P[6][:, 0:12], T.nG[:, 12 * t:12 * t + 12], OP.min, ["P6", "nG"], ["of2"])
-        tt(T.of[:, 0:12], P[6][:, 0:12], T.pGf[:, 0:12], OP.add, ["P6", "pGf"], ["of0"])
+        tt(T.of[:, 36:48], P[6][:, 0:12], T.pGf[:, 0:12], OP.add, ["P6", "pGf"], ["of3"])
         tt(T.of[:, 12:24], T.of[:, 24:36], T.pGf[:, 0:12], OP.max, ["of2", "pGf"], ["of1"])
-        cp(T.ou[:], T.of[:, 0:24], ["of0", "of1"], ["ou"])
+        tt(T.of[:, 0:12], T.of[:, 36:48], T.nG[:, 12 * t:12 * t + 12], OP.max, ["of3", "nG"], ["of0"])
+        cp(T.ou[:, 12:24], T.of[:, 12:24], ["of1"], ["ou"])
+        cp(T.ou[:, 0:12], T.of[:, 0:12], ["of0"], ["on"])
         off, offv = T.ou[:, 12:24], T.ou[:, 0:12]
 
         def a_values():
-            ac(T.av[:], T.L[:, 0:ALT + n0].indirect(offv), LK + ["ALT", "ALT2", "ou"], ["av"], AF.Identity, 0.0, 1.0 / 4096)
+            ts(T.av[:], T.ab[:, 0:M], -1024.0, 1.0 / 4096, OP.add, OP.mult, ["a"], ["av"])
+
+        def other_c():
+            ac(T.NC[:], T.ID[:, 0:ALT + n0].indirect(offv), ["ID", "ALT", "ALT2", "on"], ["NC"], AF.Identity, 129.75, 1.0 / 4096)
+            ac(T.NE[:], T.ID[:, 0:n0].indirect(pG), ["ID", kp], ["NE"], AF.Identity, 130.0, 1.0 / 4096)
 
         def gat_s(j):
             i0, i1 = CH[j]
@@ -344,14 +360,11 @@ def rank_program(g, core, T, topo):
 
         cp(T.SB[:, 0:n1].indirect(off), T.NS[:], ["NS", "ou"], ["SB"])
         if t > 0:
-            a_values()
+            other_c()
             gat_s(0)
         if t == 0:
             tt(C, T.X[:, 0:n0].indirect(pG), T.Ku[:, 0:M], OP.min, ["X", kp, "Ku0"], ["C"])
             tt(E, T.X[:, 0:n0].indirect(pG), T.Ku[:, M:2 * M], OP.min, ["X", kp, "Ku1"], ["E"])
-        else:
-            tt(C, T.xp[:], P[1][:, 0:M], OP.min, ["xp", "P1"], ["C"])
-            tt(E, T.xp[:], P[1][:, M:2 * M], OP.min, ["xp", "P1"], ["E"])
         mm(P[0][:, 0:M], T.nPm[:], C, True, False, ["nPm", "C"], ["P0"])
         mm(P[0][:, 0:M], T.I256[:], T.dup[:], False, True, ["I256", "dup"], ["P0"])
         mm(P[0][:, M:2 * M], T.nPm[:], E, True, True, ["nPm", "E"], ["P0"])
@@ -375,37 +388,41 @@ def rank_program(g, core, T, topo):
             gat_s(0)
 
         sib_pe(0)
-        gat_s(1)
+        if not ZE:
+            gat_s(1)
         if not last:
             ac(T.zy[:], P[7][:, 0:M], ["P7"], ["zy"], AF.Identity, MAGIC)
-        if t == 0:
-            a_values()
         if not last:
             ac(T["sz%d" % t][:], T.zy[:], ["zy"], ["sz%d" % t], AF.Identity, -MAGIC)
             send("sz%d" % t, "mz%d" % (t + 1), "az%d" % (t + 1), ["sz%d" % t])
-        if t == 0:
-            io(T.ID[:], [[1, W - M]], 0, 0, ["ID"])
+        if ZE:
+            gat_s(1)
         mm(P[1][:, 0:M], T.I[:], T.CKC[:, 0:M], True, False, ["I", "CKCa"], ["P1"])
-        mm(P[1][:, 0:M], T.I256[:], T.dup[:], False, False, ["I256", "dup"], ["P1"])
-        mm(P[1][:, 0:M], T.I32[:], T.av[:], False, False, ["I32", "av"], ["P1"])
         cke = "CKE1" if last else "CKE0"
-        mm(P[2][:, 0:2 * M], T.I32[:], T[cke][:], True, False, ["I32", cke], ["P2"])
-        mm(P[2][:, 0:M], T.I32[:], T.av[:], False, False, ["I32", "av"], ["P2"])
+        mm(P[2][:, 0:2 * M], T.I[:], T[cke][:], True, False, ["I", cke], ["P2"])
         half = AV // 2
         cp(T.xab[:, 0:16 * half], T.X[:, 0:n1].indirect(T.ab[:, 0:half]), ["X", "Xn", "a"], ["xa2"])
         sib_v(0)
         sib_pe(1)
+        a_values()
+        mm(P[1][:, 0:M], T.I[:], T.av[:], False, False, ["I", "av"], ["P1"])
+        mm(P[2][:, 0:M], T.I[:], T.av[:], False, False, ["I", "av"], ["P2"])
         cp(T.xab[:, 16 * half:16 * AV], T.X[:, 0:n1].indirect(T.ab[:, half:AV]), ["X", "Xn", "a"], ["xa0"])
         sib_v(1)
+        if SO:
+            gat_s(2)
+            sib_pe(2)
         if AV < M:
             ag(T.xab[:, 16 * AV:16 * M], T.X[:, 0:n1].indirect(T.ab[:, AV:M]), ["X", "Xn", "a"], ["xa1"])
-        gat_s(2)
+        if not SO:
+            gat_s(2)
         gat_b(0)
-        ac(T.NC[:], T.L[:, ALT + M * t:ALT + M * t + M], ["ALT"], ["NC"], AF.Identity, 130.0 + (V - 1 - 1024) / 4096.0, 1.0 / 4096)
+        if t == 0:
+            other_c()
         gat_b(1)
 
         ks = list(range(kd, 16))
-        npre = min(3, len(ks) // 2)
+        npre = min(len(PRE) + PRE3, len(ks) // 2)
         todo = [((ks[2 * u], s), (ks[2 * u + 1], s)) for s in (0, 1) for u in range(npre)]
         todo += [((k, 0), (k, 1)) for k in ks[2 * npre:]]
         st = {"staged": [], "signed": [], "n": 0, "red": 0}
@@ -415,7 +432,7 @@ def rank_program(g, core, T, topo):
                 return
             unit = todo.pop(0)
             slot = kd + st["n"]
-            bank = (3, 4, 1)[st["n"] % 3]
+            bank = (3, 4, 1)[st["n"]] if st["n"] < 3 else 4 - st["n"] % 2
             st["n"] += 1
             kb = "P%d" % bank
             if unit[0][0] == unit[1][0]:
@@ -461,11 +478,15 @@ def rank_program(g, core, T, topo):
             o = 2 * M * k
             tt(T.cE[:, o:o + M], T.xab[:, k:16 * M:16], P[0][:, M:2 * M], OP.is_ge, XA + ["P0"], ["cEa%d" % k])
 
-        def e_on_v(k):
+        def e_on_v(k, now=True):
             o = 2 * M * k
-            if k >= EG:
+            if EG <= k < kd - 1:
                 e_a(k)
             tt(T.cE[:, o + M:o + 2 * M], T.xab[:, 16 * M + k:32 * M:16], P[0][:, M:2 * M], OP.is_ge, XB + ["P0"], ["cE%d" % k])
+            if now:
+                e_red(k)
+
+        def e_red(k):
             red(((k, 0), (k, 1)), k, "Z16", ["cEa%d" % k, "cE%d" % k])
 
         def b_scores(j):
@@ -481,12 +502,20 @@ def rank_program(g, core, T, topo):
                 mm(P[b][:, i0:i1], sel("Z16", k), T.cC[:, o + i0:o + i1], False, j > 0 and k == 15, ["Z16", key], ["P%d" % b])
                 if j == 1 and k == K1:
                     tt(T.k1[:], P[1][:, 0:M], T.NC[:], OP.max, ["P1", "NC"], ["k1"])
-                    stage()
-                if j == 2 and k == 2:
+                    if PRE3:
+                        stage()
+                if j == 2 and k == 0:
                     sign()
                     if not last:
-                        f_arg(0)
+                        cuts_v(t + 1, 0)
+                if j == 2 and k == KM:
+                    f_max(0)
+                    f_exp(0)
                     sign()
+                if j == 2 and k == KM + 2 and not last:
+                    cuts_v(t + 1, 1)
+                if j == 2 and k == KA and not last:
+                    f_arg(0)
 
         def f_max(h):
             i0, i1, b = H[h]
@@ -500,8 +529,12 @@ def rank_program(g, core, T, topo):
 
         def f_arg(h):
             i0, i1, b = H[h]
-            mm(P[6][:, M + i0:M + i1], T.TT[:], T.vv[:, i0:i1], True, True, ["TT", "vv%d" % h], ["P6"])
-            ac(P[6][:, M + i0:M + i1], P[6][:, M + i0:M + i1], ["P6"], ["P6"], AF.Sign, 0.0, -1.0)
+            mm(P[7 - h][:, 256 + i0:256 + i1], T.TT[:], T.vv[:, i0:i1], True, True, ["TT", "vv%d" % h], ["P%d" % (7 - h)])
+
+        def f_win(h):
+            i0, i1, b = H[h]
+            at = P[7 - h][:, 256 + i0:256 + i1]
+            ts(at, at, 0.0, None, OP.is_lt, None, ["P%d" % (7 - h)], ["P%d" % (7 - h)])
 
         def f_sub(h):
             i0, i1, b = H[h]
@@ -509,7 +542,7 @@ def rank_program(g, core, T, topo):
 
         def f_min(h):
             i0, i1, b = H[h]
-            tt(T.mk[:, i0:i1], P[6][:, M + i0:M + i1], T.ec[:, i0:i1], OP.min, ["P6", "ec%d" % h], ["mk%d" % h])
+            tt(T.mk[:, i0:i1], P[7 - h][:, 256 + i0:256 + i1], T.ec[:, i0:i1], OP.mult, ["P%d" % (7 - h), "ec%d" % h], ["mk%d" % h])
             mm(P[7][:, i0:i1], T.Bk[:], T.mk[:, i0:i1], True, True, ["Bk", "mk%d" % h], ["P7"])
 
         for k in range(16):
@@ -518,7 +551,7 @@ def rank_program(g, core, T, topo):
             mm(P[1][:, 0:M], sel("Z16", k), T.cC[:, o:o + M], False, k == 15, ["Z16", "cCa%d" % k], ["P1"])
             if k == KU and not last:
                 cuts_pe(t + 1)
-            if k == K2:
+            if k == K2 and not SO:
                 sib_pe(2)
             if k == K2 + 4:
                 sib_v(2)
@@ -529,7 +562,7 @@ def rank_program(g, core, T, topo):
                     mm(P[b][:, i0:i1], T.I[:], T.CKC[:, M + i0:M + i1], True, False, ["I", "CKCb"], ["P%d" % b])
                     mm(P[b][:, i0:i1], T.I[:], T.bv[:, i0:i1], False, False, ["I", "bv"], ["P%d" % b])
                 mm(P[2][:, M:2 * M], T.I[:], T.bv[:], False, False, ["I", "bv"], ["P2"])
-            if k in (0, 10):
+            if k in PRE:
                 stage()
         for k in range(EG // 2):
             e_a(k)
@@ -538,74 +571,90 @@ def rank_program(g, core, T, topo):
         for k in range(EG // 2, EG):
             e_a(k)
         b_scores(1)
-        if not last:
-            cuts_v(t + 1, 0)
-        f_max(0)
-        if not last:
-            cuts_v(t + 1, 1)
-        f_exp(0)
         b_scores(2)
         stage()
+        if S2:
+            stage()
         f_sub(0)
-        if not last:
-            f_min(0)
+        e_a(KD[t] - 1)
         f_max(1)
         f_exp(1)
         if not last:
+            f_win(0)
             f_arg(1)
+            f_min(0)
+            sign()
             red_a()
+            stage()
             cuts_v(t + 1, 2)
+            sign()
+            cuts_a()
+            ag(P[1][:, 0:2 * M], T.Ku[:], ["Ku0", "Ku1"], ["P1"])
+            for k in range(F1):
+                e_on_v(k, False)
         f_sub(1)
         if not last:
             sp = "sp%d" % t
-            ts(T[sp][:, 0:128], P[7][:, 0:128], 4096.0, 15 * 4096.0 + 1024.0, OP.mult, OP.add, ["P7"], [sp + "a"])
+            f_win(1)
+            ts(T[sp][:, 0:128], P[7][:, 0:128], 4096.0, 1024.0, OP.mult, OP.add, ["P7"], [sp + "a"])
+            send(sp, "mp%d" % (t + 1), "ap%d" % (t + 1), [sp + "a"], 0, 128)
             f_min(1)
             to_list(P[7][:, M:M + 12], "Z1", T.mk, ["mk0", "mk1"], "P7")
             sign()
             stage()
             red_a()
-            e_on_v(0)
-            ts(T[sp][:, 128:M + 12], P[7][:, 128:M + 12], 4096.0, 15 * 4096.0 + 1024.0, OP.mult, OP.add, ["P7"], [sp])
-            send(sp, "mp%d" % (t + 1), "ap%d" % (t + 1), [sp, sp + "a"])
-        ts(T.L[:, 0:n1].indirect(off), T.ec[:], 4096.0, 1024.0, OP.mult, OP.add, ["ec0", "ec1", "ou"], LK)
+            for k in range(F1):
+                e_red(k)
+            for k in range(F1, F2):
+                e_on_v(k)
+            ts(T[sp][:, 128:M + 12], P[7][:, 128:M + 12], 4096.0, 1024.0, OP.mult, OP.add, ["P7"], [sp])
+            send(sp, "mp%d" % (t + 1), "ap%d" % (t + 1), [sp], 128, M + 12)
+
+        def c_list():
+            ts(T.L[:, 0:n1].indirect(off), T.ec[:], 4096.0, 1024.0, OP.mult, OP.add, ["ec0", "ec1", "ou"], LK)
+
         if last:
+            c_list()
             dma("S", "dyn0", T.yn[:, 0:n0], T.L[:, 0:n0], LK[:4], [])
+            sign()
+            sign()
             stage()
             red_a()
             red_a()
             e_on_v(0)
-        for k in range(1, kd):
+        k0 = 1 if last else F2
+        for k in range(k0, kd):
             step()
             e_on_v(k)
-            if k == CUT and not last:
-                cuts_a()
         while st["staged"] or st["signed"] or todo:
             step()
         if not last:
-            ag(P[1][:, 0:2 * M], T.Ku[:], ["Ku0", "Ku1"], ["P1"])
+            c_list()
             ag(T.NS[:], T.SB[:, n1:n1 + M], ["SB"], ["NS"])
-        ac(T.NE[:], T.ID[:, 0:n0].indirect(pG), ["ID", kp], ["NE"], AF.Identity, 130.0, 1.0 / 4096)
 
         def e_max():
             tt(T.k2[:], P[2][:, 0:M], T.NE[:], OP.max, ["P2", "NE"], ["k2"])
             tt(P[2][:, M:2 * M], P[2][:, M:2 * M], T.k2[:], OP.max, ["P2", "k2"], ["P2"])
             ac(T.rE[:], P[2][:, M:2 * M], ["P2"], ["rE"], AF.Identity, -0.25)
 
-        def e_end(n0=n0, n1=n1):
+        def e_sub():
             tt(P[2][:, M:2 * M], P[2][:, M:2 * M], T.rE[:], OP.subtract, ["P2", "rE"], ["P2"])
+
+        def e_end(n0=n0, n1=n1):
             tt(T.L[:, n0:n1], P[2][:, M:2 * M], T.act4[:], OP.mult, ["P2", "act4", "Ln"], ["Ln"])
 
         if last:
             e_max()
+            e_sub()
             e_end()
             dma("A", "dyn1", T.yn[:, n0:n1], T.L[:, n0:n1], ["Ln"], [])
         elif EARLY:
             e_max()
-            carry.append(e_end)
+            carry.extend([e_sub, e_end])
         else:
-            carry.extend([e_max, e_end])
+            carry.extend([e_max, e_sub, e_end])
 
-    g.wait_ge(T.sem["sent"], 2 * (RO - 1) * n_eng)
+    g.wait_ge(T.sem["sent"], 3 * (RO - 1) * n_eng)
     for s in ("sV", "sA", "sP", "sG"):
         need("G", (s, count[s]))
     for s in ("dyx", "dyn0", "dyn1"):

@@ -1,62 +1,69 @@
 import math
-from concourse.mybir import AluOpType as OP, ActivationFunctionType as AF
+from concourse.mybir import AluOpType as OP, ActivationFunctionType as AF, AxisListType as AX
 
 V, M, KK, RO, ST = 2048, 192, 512, 5, 2
 W = V + M * RO
-ALT = W
-TOP = 95 * 4096
+ALT = W + M
+U = 4096.0
+OFF = 1536.0
+TOP = -103 * 4096
+BIG = 2097152.0
 MAGIC = 12582912.0
 LN2 = math.log(2.0)
-KD = (10, 10, 10, 10, 10)
-AV = 176
+KD = 12
+KDL = 10
+NPRE = 0
+S1 = 1
+S2 = 0
+S3 = 1
+S4 = 1
+EB = 6
+UA = 8
+UB = 8
+UL = 2
+UE = 4
+UX = 16
 CH = ((0, 64), (64, 128), (128, 192))
-K2 = -2
-KU = 15
-K1 = 1
-CUT = 2
-KM = 4
-KA = 12
-F1 = 1
-F2 = 3
-EG = 0
-SO = True
-PRE = (3, 9)
-PRE3 = 0
-ZE = False
-S2 = True
-BM = False
-EARLY = True
+XS = ((0, 64, "V"), (64, 128, "A"), (128, 192, "A"))
+CA = ((0, 128), (128, 192))
+BU = "V"
+LV = 3
+SV = 3008
+NSTRIP = 4
+PASSES = 6
+CYC, PEC, GATHER, SCATTER, HOP, OWN, FAR, DMA_US, DMA_BW = 0.83e-3, 0.5e-3, 1.56, 3.8, 0.1, 0.06, 2.3, 1.8, 200e3
 
 SCRATCH = {
-    "X": ("sbuf", [128, W], "bfloat16"), "L": ("sbuf", [128, W], "float32"), "SB": ("sbuf", [128, W], "bfloat16"),
-    "NS": ("sbuf", [128, M], "bfloat16"), "ID": ("sbuf", [128, W + W - M], "float32"), "NB": ("sbuf", [128, V], "int32"),
+    "X": ("sbuf", [128, W + M], "bfloat16"), "L": ("sbuf", [128, W + M], "float32"),
+    "XR": ("sbuf", [128, W], "float16"), "XO": ("sbuf", [128, W], "bfloat16"), "BT": ("sbuf", [128, M * RO], "bfloat16"),
+    "ID": ("sbuf", [128, ALT + W - M], "float32"), "NB": ("sbuf", [128, V], "int32"),
     "K0": ("sbuf", [128, KK], "bfloat16"), "K1": ("sbuf", [128, KK], "bfloat16"),
     "psi": ("sbuf", [128, 12], "int32"), "wti": ("sbuf", [128, 1], "int32"), "wf": ("sbuf", [128, 1], "float32"),
     "J": ("sbuf", [128, M], "bfloat16"), "Jg": ("sbuf", [128, 128], "bfloat16"), "J16": ("sbuf", [128, M], "float32"),
-    "pc": ("sbuf", [128, 128], "int32"), "pc2": ("sbuf", [128, 128], "int32"), "ci": ("sbuf", [128, 4], "int32"),
+    "pc": ("sbuf", [128, 2], "int32"), "ci": ("sbuf", [128, 4], "int32"),
     "cf": ("sbuf", [128, 12], "float32"), "cG": ("sbuf", [128, 12], "int32"), "cGu": ("sbuf", [128, 12], "uint16"),
-    "nG": ("sbuf", [128, 12 * RO], "float32"), "mask": ("sbuf", [128, M], "float32"), "thr": ("sbuf", [128, M], "float32"),
+    "nG": ("sbuf", [128, 12 * (RO + 1)], "float32"), "mask": ("sbuf", [128, M], "float32"), "thr": ("sbuf", [128, M], "float32"),
     "gx": ("sbuf", [128, M], "float16"), "wG": ("sbuf", [128, 12], "float32"),
-    "on32": ("sbuf", [128, 128], "float32"), "CKC": ("sbuf", [128, 2 * M], "bfloat16"),
-    "CKE0": ("sbuf", [128, 2 * M], "float16"), "CKE1": ("sbuf", [128, 2 * M], "float16"), "q4": ("sbuf", [128, M], "bfloat16"),
+    "hb": ("sbuf", [128, 16], "float32"), "wr": ("sbuf", [128, 16], "bfloat16"), "wm": ("sbuf", [128, 16], "float32"),
+    "on32": ("sbuf", [128, 128], "float32"), "I32": ("sbuf", [128, 128], "float32"), "CK": ("sbuf", [128, 2 * M], "bfloat16"),
+    "CKE0": ("sbuf", [128, 2 * M], "float16"), "CKE1": ("sbuf", [128, 2 * M], "float16"),
     "pGf": ("sbuf", [128, 16], "float32"), "EQ": ("sbuf", [128, 12 * M], "bfloat16"),
-    "dup": ("sbuf", [128, M], "bfloat16"), "act": ("sbuf", [128, M], "bfloat16"), "act4": ("sbuf", [128, M], "bfloat16"),
-    "cnt": ("sbuf", [128, 1], "float32"), "of": ("sbuf", [128, 48], "float32"), "ou": ("sbuf", [128, 24], "uint16"),
+    "dup": ("sbuf", [128, M], "bfloat16"), "zr": ("sbuf", [128, M], "float16"),
+    "cnt": ("sbuf", [128, 1], "float32"), "ou": ("sbuf", [128, 24], "uint16"),
     "ui": ("sbuf", [128, 24], "int32"), "uu": ("sbuf", [128, 12], "uint16"),
     "Ku": ("sbuf", [128, 2 * M], "bfloat16"), "CE": ("sbuf", [128, 2 * M], "bfloat16"),
-    "ab": ("sbuf", [128, 2 * M], "uint16"), "bv": ("sbuf", [128, M], "float16"),
-    "av": ("sbuf", [128, M], "float16"), "xp": ("sbuf", [128, M], "bfloat16"),
-    "sg": ("sbuf", [128, 16 * M], "bfloat16"), "xab": ("sbuf", [128, 32 * M], "bfloat16"),
+    "ab": ("sbuf", [128, 2 * M], "uint16"), "bv": ("sbuf", [128, M], "float16"), "av": ("sbuf", [128, M], "float16"),
+    "xo": ("sbuf", [128, M], "float16"), "xp": ("sbuf", [128, M], "bfloat16"),
+    "xr": ("sbuf", [128, 16 * M], "float16"), "xab": ("sbuf", [128, 32 * M], "bfloat16"),
     "cC": ("sbuf", [128, 32 * M], "bfloat16"), "cE": ("sbuf", [128, 32 * M], "bfloat16"),
     "NC": ("sbuf", [128, M], "float32"), "NE": ("sbuf", [128, M], "float32"),
     "k1": ("sbuf", [128, M], "float32"), "k2": ("sbuf", [128, M], "float32"),
     "rC": ("sbuf", [128, M], "bfloat16"), "rE": ("sbuf", [128, M], "bfloat16"), "vv": ("sbuf", [128, M], "bfloat16"),
-    "ec": ("sbuf", [128, M], "float32"), "mk": ("sbuf", [128, M], "float16"),
-    "dm": ("sbuf", [128, M], "bfloat16"), "zy": ("sbuf", [128, M], "float32"),
+    "ec": ("sbuf", [128, M], "float32"), "mk": ("sbuf", [128, M], "float16"), "zy": ("sbuf", [128, M], "float32"),
 }
-for _n in ("I", "nI", "Ih", "I256", "Pm", "nPm", "Bk", "TT", "t1", "t2"):
+for _n in ("I", "nI", "Ih", "I256", "IU", "nBI", "nIc", "Pm", "nPm", "Bk", "TT", "t1", "t2"):
     SCRATCH[_n] = ("sbuf", [128, 128], "bfloat16")
-for _n in ("Z1", "Z16", "Z8", "Zd", "Zw"):
+for _n in ("Z1", "Z16", "Z8", "Zc", "Zd", "Zw", "Zb", "nZb"):
     SCRATCH[_n] = ("sbuf", [128, 144], "bfloat16")
 for _t in range(RO):
     SCRATCH["mp%d" % _t] = ("sbuf", [128, M + 12], "uint16")
@@ -71,6 +78,50 @@ DMAS = ["dps", "dwt", "dzi", "dkc", "dxc", "dnb0", "dnb1", "dnb2", "dnb3", "dyx"
 SEMAPHORES = ["sV", "sA", "sP", "sG", "sent"] + DMAS + ["ap%d" % t for t in range(1, RO)] + ["az%d" % t for t in range(1, RO)]
 
 
+def place(order, queue, busy, after, edges):
+    start = [0.0] * len(queue)
+    slots = {}
+    for i in order:
+        t = 0.0
+        for j, gap in edges[i]:
+            t = max(t, start[j] + busy[j] + after[j] + gap)
+        s = slots.setdefault(queue[i], [])
+        lo, hi = 0, len(s)
+        while lo < hi:
+            mid = (lo + hi) // 2
+            if s[mid][1] <= t:
+                lo = mid + 1
+            else:
+                hi = mid
+        while lo < len(s) and s[lo][0] < t + busy[i] - 1e-9:
+            t = max(t, s[lo][1])
+            lo += 1
+        s.insert(lo, (t, t + busy[i]))
+        start[i] = t
+    return start
+
+
+def schedule(queue, busy, after, before):
+    n = len(queue)
+    behind = [[] for _ in range(n)]
+    for i in range(n):
+        for j, gap in before[i]:
+            behind[j].append((i, gap + after[j]))
+    rest = [0.0] * n
+    for i in reversed(range(n)):
+        rest[i] = busy[i] + max([after[i]] + [gap + rest[j] for j, gap in behind[i]])
+    best = None
+    none = [0.0] * n
+    for _ in range(PASSES):
+        start = place(sorted(range(n), key=lambda i: (-rest[i], i)), queue, busy, after, before)
+        end = max(start[i] + busy[i] + after[i] for i in range(n))
+        if best is None or end < best[0]:
+            best = (end, start)
+        back = place(sorted(range(n), key=lambda i: (-start[i] - busy[i], -i)), queue, busy, none, behind)
+        rest = [back[i] + busy[i] for i in range(n)]
+    return sorted(range(n), key=lambda i: (best[1][i], i))
+
+
 def rank_program(g, core, T, topo):
     rank = T.rank_of(core)
     if rank is None:
@@ -83,10 +134,349 @@ def rank_program(g, core, T, topo):
     n_in = len(topo.engines(T.cores[(rank - ST) % n_ranks], core))
 
     Q = {"V": g.vector, "A": g.scalar, "P": g.tensor, "G": g, "S": g.sync}
+    calls = []
+    wrote, read, opened, units = {}, {}, {}, {}
+
+    def note(e, call, busy, r, w, after=0.0, event=None, adds=False, group=None):
+        deps = {}
+        for k in r:
+            if k[0] == "~":
+                for j in wrote.get(k[1:], []):
+                    deps.setdefault(j, False)
+                continue
+            for j in wrote.get(k, []):
+                deps[j] = True
+            if k[0] == "P" and k[1:].isdigit():
+                for j in read.get(k, []):
+                    if calls[j][0] != e:
+                        deps[j] = True
+        for k in w:
+            for j in (wrote[k][:1] if adds else wrote.get(k, []) + read.get(k, [])):
+                if e != "G":
+                    deps[j] = True
+        i = len(calls)
+        calls.append([e, call, busy, after, deps, event, group])
+        for k in r:
+            read.setdefault(k, []).append(i)
+        for k in w:
+            if adds:
+                wrote[k].append(i)
+            else:
+                wrote[k] = [i]
+                read[k] = []
+        return i
+
+    def cyc(n, kind):
+        return {"": max(64, n) * CYC, "h": max(64, n / 2) * CYC, "d": max(64, 2 * n) * CYC, "g": 0.06 + n * GATHER * CYC,
+                "s": 0.05 + n * SCATTER * CYC}[kind]
+
+    def dma(e, sem, out, in_, nbytes, r, w):
+        t = nbytes / DMA_BW + 0.2
+        note(e, lambda: Q[e].dma_start(out, in_), t if e == "S" else 0.05, r, w, DMA_US, (sem, 16))
+
+    def send(src, dst, sem, val, r, w, c0, c1, adds=False):
+        note("G", lambda: g.remote_dma(T[dst][:, c0:c1], T[src][:, c0:c1], T.sem[sem], T.sem["sent"], pid, rid, emask), 0.3, r, w,
+             FAR + (c1 - c0) * 0.005, (sem, val), adds)
+
+    v, a, pe = g.vector, g.scalar, g.tensor
+
+    def ts(out, in0, s1, s2, o0, o1, r, w, n=64, kind=""):
+        if s2 is None:
+            note("V", lambda: v.tensor_scalar(out, in0, s1, None, o0), cyc(n, kind), r, w)
+        else:
+            note("V", lambda: v.tensor_scalar(out, in0, s1, s2, o0, o1), cyc(n, kind), r, w)
+
+    def tt(out, in0, in1, o, r, w, n=64, kind=""):
+        note("V", lambda: v.tensor_tensor(out, in0, in1, o), cyc(n, kind), r, w)
+
+    def cp(out, in_, r, w, n=64, kind=""):
+        note("V", lambda: v.tensor_copy(out, in_), cyc(n, kind), r, w)
+
+    def ms(out, val, w, n=64):
+        note("V", lambda: v.memset(out, val), cyc(n, "h"), [], w)
+
+    def ac(out, in_, r, w, f=AF.Identity, bias=0.0, scale=1.0, acc=None, n=64, kind=""):
+        note("A", lambda: a.activation(out, in_, f, bias, scale, accum_out=acc), cyc(n, kind) + (0.14 if acc is not None else 0), r, w)
+
+    def ag(out, in_, r, w, n=64, kind=""):
+        note("A", lambda: a.activation(out, in_, AF.Copy), cyc(n, kind), r, w)
+
+    def mm(out, lhsT, rhs, st, r, bank, n, unit=None):
+        if st:
+            opened[bank] = len(calls)
+        units[len(calls)] = unit
+        note("P", lambda stop: pe.matmul(out, lhsT, rhs, st, stop), max(64, n) * PEC, r, [bank], adds=not st, group=opened[bank])
+
+    def io(out, pat, base, cm, w, n, flt=True):
+        if flt:
+            note("G", lambda: g.iota(out, pat, base, cm, allow_small_or_imprecise_dtypes=True), 0.13 + 2 * n * CYC, [], w)
+        else:
+            note("G", lambda: g.iota(out, pat, base, cm), 0.13 + 2 * n * CYC, [], w)
+
+    def sel(Z, k):
+        return T[Z][:, 15 - k:143 - k]
+
+    def to_list(out, Z, src, keys, bank, first=True):
+        for m in range(16):
+            mm(out, sel(Z, m), src[:, m:M:16], first and m == 0, keys + [Z], bank, 12, ("list", len(calls) - m))
+
+    P = [T["P%d" % b] for b in range(8)]
+    col = lambda j: T.cf[:, j:j + 1]
+    J128, J144 = T.J[:, 0:128], T.J[:, 0:144]
+
+    dma("S", "dps", T.psi[:], T.ps[:], 6144, [], ["psi", "ld"])
+    dma("A", "dwt", T.wti[:], T.wt[:], 512, [], ["wti"])
+    dma("A", "dzi", T.mz0[:], T.zi[:], 256 * M, [], ["mz0"])
+    dma("S", "dkc", T.K0[:], T.kc[:], 256 * KK, [], ["K0"])
+    dma("S", "dxc", T.X[:, 0:V], T.xc[:], 256 * V, [], ["X"])
+    for j in range(4):
+        dma("S", "dnb%d" % j, T.NB[:, 512 * j:512 * j + 512], T.nb[:, 512 * j:512 * j + 512], 512 * 512, [], ["NB%d" % j])
+    io(T.pc[:], [[1, 2]], 0, 1, ["pc"], 2, False)
+    io(T.J[:], [[1, M]], 0, 0, ["J"], M)
+    io(T.Jg[:], [[16, 8], [0, 16]], 0, 0, ["Jg"], 128)
+    io(T.J16[:], [[0, 12], [1, 16]], 0, 0, ["J16"], M)
+    io(T.cG[:], [[1, 12]], 0, 0, ["cG"], 12, False)
+    io(T.nG[:], [[16, 12 * (RO + 1)]], V, 1, ["nG"], 72)
+    io(T.ID[:, 0:W], [[1, W]], 0, 0, ["ID"], W)
+    io(T.ID[:, W:ALT], [[0, M]], 110 * 4096, 0, ["ID2"], M)
+    io(T.ID[:, ALT:ALT + V - 1], [[1, V - 1]], TOP + 1, 0, ["ALT"], V)
+    io(T.ID[:, ALT + V - 1:ALT + W - M], [[1, W - M - V + 1]], TOP, 0, ["ALT2"], W - M - V)
+    ts(T.ci[:, 0:1], T.pc[:, 0:1], 15, None, OP.bitwise_and, None, ["pc"], ["ci0"])
+    ts(T.ci[:, 1:2], T.pc[:, 0:1], 1, None, OP.bitwise_and, None, ["pc"], ["ci1"])
+    cp(col(0), T.pc[:, 0:1], ["pc"], ["c0"])
+    cp(col(1), T.ci[:, 0:1], ["ci0"], ["c1"])
+    ts(col(8), T.ci[:, 1:2], -2.0, 1.0, OP.mult, OP.add, ["ci1"], ["c8"])
+    tt(col(2), col(0), col(1), OP.subtract, ["c0", "c1"], ["c2"])
+    tt(col(4), col(0), col(8), OP.add, ["c0", "c8"], ["c4"])
+    ts(col(3), col(2), 15.0, None, OP.add, None, ["c2"], ["c3"])
+    ts(col(6), col(1), KD - 0.5, 128.0, OP.is_ge, OP.mult, ["c1"], ["c6"])
+    ts(col(7), col(1), KDL - 0.5, 128.0, OP.is_ge, OP.mult, ["c1"], ["c7"])
+    for name, c, wgt in (("I", 0, 1.0), ("nI", 0, -1.0), ("Ih", 0, 0.5), ("I256", 0, 256.0), ("IU", 0, U), ("nBI", 0, -BIG),
+                         ("nIc", 0, -1.0 / 2048), ("t2", 0, -1024.0), ("I32", 0, 1.0), ("Pm", 4, 1.0), ("nPm", 4, -1.0)):
+        ts(T[name][:], J128, col(c), wgt, OP.is_equal, OP.mult, ["J", "c%d" % c], [name], 128, "" if name == "I32" else "h")
+    for name, wgt in (("Z1", 1.0), ("Zd", ALT / 16.0), ("Z16", 16 * U), ("Z8", 8 * U), ("Zc", 32.0)):
+        ts(T[name][:], J144, col(3), wgt, OP.is_equal, OP.mult, ["J", "c3"], [name], 144, "h")
+    ts(T.Bk[:], T.Jg[:], col(2), None, OP.is_equal, None, ["Jg", "c2"], ["Bk"])
+    ts(T.mask[:], T.J16[:], col(1), None, OP.is_equal, None, ["J16", "c1"], ["mask"], M)
+    ac(T.thr[:], T.J[:], ["J"], ["thr"], AF.Exp, 96 * LN2 + math.log(1.25), -LN2, n=1800)
+    ts(T.nG[:], T.nG[:], col(2), None, OP.subtract, None, ["nG", "c2"], ["nG"], 72)
+    ts(T.wG[:], T.nG[:, 0:12], -float(V), None, OP.add, None, ["nG"], ["wG"])
+    ac(T.wG[:], T.wG[:], ["wG", "thr"], ["wG"], AF.Exp, 95 * LN2, -LN2)
+    ts(T.t1[:], J128, col(0), 65536.0, OP.is_gt, OP.mult, ["J", "c0"], ["t1"])
+    tt(T.t1[:], T.t1[:], T.Bk[:], OP.mult, ["t1", "Bk"], ["t1"], 128, "d")
+    tt(T.t2[:], T.t2[:], T.Bk[:], OP.add, ["t2", "Bk"], ["t2"], 128, "d")
+    tt(T.TT[:], T.t1[:], T.t2[:], OP.add, ["t1", "t2"], ["TT"], 128, "d")
+    ac(T.on32[:], T.I[:], ["I"], ["on32"], AF.Identity, 1.0 / 16, 0.0, n=128)
+    ms(T.CK[:, 0:M], -31.0, ["CKa"], M)
+    ms(T.CK[:, M:2 * M], -32.0, ["CKb"], M)
+    ts(T.CKE0[:], T.CK[:], col(6), OFF / U, OP.add, OP.add, ["CKa", "CKb", "c6"], ["CKE0"], 2 * M, "h")
+    ts(T.CKE1[:], T.CK[:], col(7), OFF / U, OP.add, OP.add, ["CKa", "CKb", "c7"], ["CKE1"], 2 * M, "h")
+    ts(T.hb[:], T.J[:, 0:16], col(1), 0.5, OP.is_equal, OP.mult, ["J", "c1"], ["hb"])
+    ag(T.BT[:, 0:1], T.hb[:, 11:12], ["hb"], ["BT"])
+    for e in range(10):
+        w0, w1 = 1 << e, min(2 << e, M * RO)
+        ac(T.BT[:, w0:w1], T.BT[:, 0:w1 - w0], ["BT", "hb"], ["BT"], AF.Identity, T.hb[:, e:e + 1], n=w1 - w0)
+    ac(T.wr[:], T.J[:, 0:16], ["J", "thr"], ["wr"], AF.Exp, 2 * LN2, LN2)
+    for j, wj in ((12, -16384.0), (13, 4.0), (14, 2.0), (15, 0.0)):
+        ms(T.wr[:, j:j + 1], wj, ["wr"])
+    tt(T.wm[:], T.wr[:], T.hb[:], OP.mult, ["wr", "hb"], ["wm"])
+    note("V", lambda: v.tensor_reduce(col(5), T.wm[:], AX.X, OP.add), cyc(16, ""), ["wm"], ["c5"])
+    ts(T.Zb[:], J144, col(3), col(5), OP.is_equal, OP.mult, ["J", "c3", "c5"], ["Zb"], 144, "h")
+    ts(T.nZb[:], T.Zb[:], -1.0, None, OP.mult, None, ["Zb"], ["nZb"], 144, "h")
+    ag(T.K1[:, 0:KK:2], T.K0[:, 1:KK:2], ["K0"], ["K1a"], 256)
+    ag(T.K1[:, 1:KK:2], T.K0[:, 0:KK:2], ["K0"], ["K1b"], 256)
+    cp(T.wf[:], T.wti[:], ["wti"], ["wf"])
+    ts(T.Zw[:], J144, col(3), T.wf[:], OP.is_equal, OP.mult, ["J", "c3", "wf"], ["Zw"], 144, "h")
+    cp(T.cGu[:], T.cG[:], ["cG"], ["cGu"])
+    cp(T.pGf[:, 0:12], T.psi[:], ["psi"], ["pGf"])
+    tt(T.gx[:], T.pGf[:, 0:12].indirect(T.cGu[:, 0:12]), T.mask[:], OP.mult, ["pGf", "cGu", "mask"], ["gx"], M, "g")
+    cp(T.mp0[:, M:M + 12], T.psi[:], ["psi"], ["mp0g"])
+    mm(P[6][:, 0:M], T.Bk[:], T.gx[:], True, ["Bk", "gx"], "P6", M)
+    cp(T.mp0[:, 0:M], P[6][:, 0:M], ["P6", "mp0g"], ["mp0"], M)
+    for j in range(4):
+        (cp if j < LV else ag)(T.L[:, 512 * j:512 * j + 512], T.NB[:, 512 * j:512 * j + 512], ["NB%d" % j], ["L%d" % j], 512)
+
+    def cuts(t):
+        if t > 0:
+            mm(P[7][:, 16:17], T.on32[:], T.cnt[:], True, ["on32", "cnt"], "P7", 256)
+        to_list(P[7][:, 0:12], "Zw", T["mz%d" % t], ["mz%d" % t], "P7")
+        if t > 0:
+            ts(T.ui[:, 0:12], P[7][:, 0:12], P[7][:, 16:17], 262144.0, OP.add, OP.add, ["P7"], ["ui0"])
+        else:
+            ts(T.ui[:, 0:12], P[7][:, 0:12], 262144.0, None, OP.add, None, ["P7"], ["ui0"])
+        ts(T.ui[:, 12:24], T.ui[:, 0:12], KK - 1, None, OP.bitwise_and, None, ["ui0"], ["ui1"])
+        ag(T.uu[:], T.ui[:, 12:24], ["ui1"], ["uu"])
+        ag(T.Ku[:, 0:M], T.K0[:].indirect(T.uu[:, 0:12]), ["K0", "uu"], ["Ku0"], M, "g")
+        ag(T.Ku[:, M:2 * M], T.K1[:].indirect(T.uu[:, 0:12]), ["K1a", "K1b", "uu"], ["Ku1"], M, "g")
+
+    cuts(0)
+    XB = ["xb0", "xb1", "xb2"]
+    XA = ["xa%d" % i0 for i0, i1, e in XS]
+    xa_keys = lambda c0, c1: ["xa%d" % i0 for i0, i1, e in XS if i0 < c1 and i1 > c0]
+    LK = ["L0", "L1", "L2", "L3", "Ln"]
+    H = ((0, 128, 6), (128, 192, 5))
+
+    for t in range(RO):
+        last = t == RO - 1
+        n0 = V + M * t
+        n1 = n0 + M
+        mp, mz = T["mp%d" % t], T["mz%d" % t]
+        kp, kz, sp = "mp%d" % t, "mz%d" % t, "sp%d" % t
+        pG = mp[:, M:M + 12]
+        C, E = T.CE[:, 0:M], T.CE[:, M:2 * M]
+        off, offv = T.ou[:, 12:24], T.ou[:, 0:12]
+        kd = KDL if last else KD
+
+        if t > 0:
+            cp(T.pGf[:, 0:12], pG, [kp] + ["~L0"] * S1, ["pGf"])
+        for c in range(12):
+            e0 = c * M
+            ts(T.EQ[:, e0:e0 + M - 16 * c], mp[:, 16 * c:M], T.pGf[:, c:c + 1], T.wG[:, c:c + 1], OP.is_equal, OP.mult,
+               [kp, "pGf", "wG"], ["EQ%d" % c], M - 16 * c, "h")
+            mm(P[5][:, 16 * c:M], T.Bk[:], T.EQ[:, e0:e0 + M - 16 * c], c == 0, ["Bk", "EQ%d" % c], "P5", M - 16 * c, ("eq", t, c // UE))
+        tt(T.dup[:], P[5][:, 0:M], T.thr[:], OP.is_ge, ["P5", "thr"], ["dup"], M)
+        mm(P[7][:, 0:12], T.I32[:], T.pGf[:, 0:12], True, ["I32", "pGf"], "P7", 256)
+        to_list(P[7][:, 0:12], "Zd", T.dup, ["dup"], "P7", False)
+        ac(P[3][:, 0:M], T.dup[:], ["dup"], ["P3", "cnt"], AF.Identity, 1.0, -1.0, T.cnt[:], M)
+        tt(off, P[7][:, 0:12], T.nG[:, 12 * RO:12 * RO + 12], OP.min, ["P7", "nG"], ["ou"])
+        tt(offv, P[7][:, 0:12], T.nG[:, 12 * t:12 * t + 12], OP.max, ["P7", "nG"], ["ov"])
+        ag(P[1][:, 0:2 * M], T.Ku[:], ["Ku0", "Ku1"], ["P1"], 2 * M)
+        ac(T.xo[:], T.X[:, 0:n0].indirect(pG), ["X", "Xn", kp], ["xo"], AF.Identity, OFF - 0.25, n=M, kind="g")
+        ac(T.xp[:], T.xo[:], ["xo"], ["xp"], AF.Identity, -OFF, n=M)
+        tt(C, T.xp[:], P[1][:, 0:M], OP.min, ["xp", "P1"], ["C"], M)
+        tt(E, T.xp[:], P[1][:, M:2 * M], OP.min, ["xp", "P1"], ["E"], M)
+        mm(P[0][:, 0:2 * M], T.nPm[:], T.CE[:], True, ["nPm", "C", "E"], "P0", 2 * M)
+        if t > 0:
+            ag(T.ab[:, 0:M], T.L[:, 0:n0].indirect(pG), LK + [kp], ["a"], M, "g")
+        else:
+            cp(T.ab[:, 0:M], T.NB[:].indirect(pG), ["NB0", "NB1", "NB2", "NB3", kp], ["a"], M, "g")
+        ac(T.av[:], T.ab[:, 0:M], ["a"], ["av"], AF.Identity, -OFF, n=M)
+        tt(T.X[:, n0:n1], E, P[3][:, 0:M], OP.mult, ["E", "P3"], ["Xn"], M)
+        tt(T.X[:, 0:W + M].indirect(off), C, T.BT[:, M * t:M * t + M], OP.add, ["C", "BT", "ou"] + ["~Ln"] * (S4 * (t > 0)), ["X", "Xn"], M, "s")
+        if not last:
+            mm(P[7][:, 0:M], T.I[:], C, True, ["I", "C"], "P7", M)
+            mm(P[7][:, 0:M], T.nI[:], mz[:], False, ["nI", kz], "P7", M)
+            mm(P[7][:, 0:M], T.nBI[:], T.dup[:], False, ["nBI", "dup"], "P7", M)
+            ac(T.zr[:], P[7][:, 0:M], ["P7"], ["zr"], AF.Relu, 511.5, n=M)
+            mm(P[4][:, 0:M], T.I[:], mz[:], True, ["I", kz], "P4", M)
+            mm(P[4][:, 0:M], T.I256[:], T.dup[:], False, ["I256", "dup"], "P4", M)
+            mm(P[4][:, 0:M], T.Ih[:], T.zr[:], False, ["Ih", "zr"], "P4", M)
+            ac(T.zy[:], P[4][:, 0:M], ["P4"], ["zy"], AF.Identity, MAGIC - 256, n=M)
+            ac(T["sz%d" % t][:], T.zy[:], ["zy"], ["sz%d" % t], AF.Identity, -MAGIC, n=M)
+            send("sz%d" % t, "mz%d" % (t + 1), "az%d" % (t + 1), n_in, ["sz%d" % t], ["mz%d" % (t + 1)], 0, M)
+            cuts(t + 1)
+        ac(T.NC[:], T.ID[:, 0:ALT + n0].indirect(offv), ["ID", "ID2", "ALT", "ALT2", "ov"], ["NC"], AF.Identity, 322.75, -1.0 / 2048,
+           n=M, kind="g")
+        ac(T.NE[:], T.ID[:, 0:ALT].indirect(off), ["ID", "ID2", "ou"], ["NE"], AF.Identity, 130 * U, n=M, kind="g")
+        if last:
+            for j in range(NSTRIP):
+                j0, j1 = W // NSTRIP * j, W // NSTRIP * (j + 1)
+                if j0 < SV:
+                    ts(T.XR[:, j0:j1], T.X[:, j0:j1], OFF - 0.25, None, OP.add, None, ["X", "Xn"], ["XR%d" % j], j1 - j0, "h")
+                    ts(T.XO[:, j0:j1], T.XR[:, j0:j1], -OFF, None, OP.add, None, ["XR%d" % j], ["XO%d" % j], j1 - j0, "h")
+                else:
+                    ac(T.XR[:, j0:j1], T.X[:, j0:j1], ["X", "Xn"], ["XR%d" % j], AF.Identity, OFF - 0.25, n=j1 - j0)
+                    ac(T.XO[:, j0:j1], T.XR[:, j0:j1], ["XR%d" % j], ["XO%d" % j], AF.Identity, -OFF, n=j1 - j0)
+            dma("S", "dyx", T.yx[:], T.XO[:], 256 * W, ["XO%d" % j for j in range(NSTRIP)], [])
+
+        for i0, i1, e in XS:
+            (cp if e == "V" else ag)(T.xab[:, 16 * i0:16 * i1], T.X[:, 0:n1].indirect(T.ab[:, i0:i1]), ["X", "Xn", "a"] + ["~av"] * (S3 * (e == "A")), ["xa%d" % i0],
+                                     16 * (i1 - i0), "g")
+        for j, (i0, i1) in enumerate(CH):
+            kb, Pb = "P%d" % (5 + j % 2), P[5 + j % 2][:, 0:i1 - i0]
+            ts(T.xr[:, 16 * i0:16 * i1], T.xab[:, 16 * i0:16 * i1], OFF - 0.25, None, OP.add, None, xa_keys(i0, i1), ["xr%d" % j],
+               16 * (i1 - i0), "h")
+            for k in range(16):
+                mm(Pb, sel("Zb", k), T.xab[:, 16 * i0 + k:16 * i1:16], k == 0, ["Zb"] + xa_keys(i0, i1) + ["~P%d" % (6 - j % 2)] * (S2 * (j > 0)), kb, i1 - i0,
+                   ("xt", t, j, k // UX))
+            for k in range(16):
+                mm(Pb, sel("nZb", k), T.xr[:, 16 * i0 + k:16 * i1:16], False, ["nZb", "xr%d" % j], kb, i1 - i0, ("xr", t, j, k // UX))
+            tt(T.bv[:, i0:i1], Pb, T.av[:, i0:i1], OP.max, [kb, "av"], ["bv%d" % j], i1 - i0)
+            if BU == "A":
+                ac(T.ab[:, M + i0:M + i1], T.bv[:, i0:i1], ["bv%d" % j], ["b%d" % j], AF.Identity, OFF, n=i1 - i0)
+            else:
+                ts(T.ab[:, M + i0:M + i1], T.bv[:, i0:i1], OFF, None, OP.add, None, ["bv%d" % j], ["b%d" % j])
+            ag(T.xab[:, 16 * (M + i0):16 * (M + i1)], T.X[:, 0:n1].indirect(T.ab[:, M + i0:M + i1]), ["X", "Xn", "b%d" % j], ["xb%d" % j],
+               16 * (i1 - i0), "g")
+
+        mm(P[1][:, 0:M], T.nIc[:], T.av[:], True, ["nIc", "av"], "P1", M)
+        for i0, i1 in CA:
+            for k in range(16):
+                o, key = 2 * M * k, "cCa%d_%d" % (k, i0)
+                tt(T.cC[:, o + i0:o + i1], T.xab[:, 16 * i0 + k:16 * i1:16], P[0][:, i0:i1], OP.is_ge, xa_keys(i0, i1) + ["P0"], [key], i1 - i0)
+                mm(P[1][:, i0:i1], sel("Zc", k), T.cC[:, o + i0:o + i1], False, ["Zc", key], "P1", i1 - i0, ("ca", t, i0, k // UA))
+        tt(T.k1[:], P[1][:, 0:M], T.NC[:], OP.max, ["P1", "NC"], ["k1"], M)
+        for i0, i1, b in H:
+            mm(P[b][:, i0:i1], T.nIc[:], T.bv[:, i0:i1], True, ["nIc"] + (["bv0", "bv1"] if i0 == 0 else ["bv2"]), "P%d" % b, i1 - i0)
+        for j, (i0, i1) in enumerate(CH):
+            b = H[j // 2][2]
+            for k in range(16):
+                o, key = 2 * M * k + M, "cCb%d_%d" % (j, k)
+                tt(T.cC[:, o + i0:o + i1], T.xab[:, 16 * (M + i0) + k:16 * (M + i1):16], P[0][:, i0:i1], OP.is_ge, ["xb%d" % j, "P0"], [key])
+                mm(P[b][:, i0:i1], sel("Zc", k), T.cC[:, o + i0:o + i1], False, ["Zc", key], "P%d" % b, i1 - i0,
+                   ("cb", t, j, k // (UL if j == 2 else UB)))
+        for h, (i0, i1, b) in enumerate(H):
+            kb, Pb, n = "P%d" % b, P[b][:, i0:i1], i1 - i0
+            tt(Pb, Pb, T.k1[:, i0:i1], OP.max, [kb, "k1"], [kb], n)
+            if not last:
+                ac(T.vv[:, i0:i1], Pb, [kb], ["vv%d" % h], AF.Exp, -200 * LN2, LN2 / 2, n=n)
+            ag(T.rC[:, i0:i1], Pb, [kb], ["rC%d" % h], n)
+            tt(T.ec[:, i0:i1], Pb, T.rC[:, i0:i1], OP.subtract, [kb, "rC%d" % h], ["ec%d" % h], n)
+            if not last:
+                kw, Pw = "P%d" % (7 - h), P[7 - h][:, 256 + i0:256 + i1]
+                mm(Pw, T.TT[:], T.vv[:, i0:i1], True, ["TT", "vv%d" % h], kw, n)
+                ac(Pw, Pw, [kw], [kw], AF.Sign, 0.0, -1.0, n=n)
+                tt(T.mk[:, i0:i1], Pw, T.ec[:, i0:i1], OP.min, [kw, "ec%d" % h], ["mk%d" % h], n)
+                mm(P[7][:, i0:i1], T.Bk[:], T.mk[:, i0:i1], True, ["Bk", "mk%d" % h], "P7", n)
+                if h == 1:
+                    to_list(P[7][:, M:M + 12], "Z1", T.mk, ["mk0", "mk1"], "P7")
+                    i1 = M + 12
+                ac(T[sp][:, i0:i1], P[7][:, i0:i1], ["P7"], [sp + "_%d" % h], AF.Identity, OFF - 15 * 2048, -2048.0, n=i1 - i0)
+                send(sp, "mp%d" % (t + 1), "ap%d" % (t + 1), 2 * n_in, [sp + "_%d" % h], ["mp%d" % (t + 1)], i0, i1, h == 1)
+        ts(T.L[:, 0:W + M].indirect(off), T.ec[:], -2048.0, OFF, OP.mult, OP.add, ["ec0", "ec1", "ou"], LK, M, "s")
+        if last:
+            dma("S", "dyn0", T.yn[:, 0:n0], T.L[:, 0:n0], 512 * n0, LK[:4], [])
+
+        PE, KE = (P[2][:, 0:M], P[EB][:, M:2 * M]), ("P2", "P%d" % EB)
+        for s, val, keys in ((0, T.av, ["av"]), (1, T.bv, ["bv0", "bv1", "bv2"])):
+            mm(PE[s], T.IU[:], T["CKE1" if last else "CKE0"][:, M * s:M * s + M], EB != 2 or s == 0, ["IU", "CKE0", "CKE1"], KE[s], M)
+            mm(PE[s], T.I[:], val[:], False, ["I"] + keys, KE[s], M)
+        halves = [(k, 0) for k in range(kd, kd + 2 * NPRE)] + [(k, 1) for k in range(kd, kd + 2 * NPRE)]
+        halves += [(k, h) for k in range(kd + 2 * NPRE, 16) for h in (0, 1)]
+        for u in range(len(halves) // 2):
+            kb, o = "P%d" % (3 + u % 2), 2 * M * (kd + u)
+            for h, (k, s) in enumerate(halves[2 * u:2 * u + 2]):
+                Pb = P[3 + u % 2][:, M * h:M * h + M]
+                mm(Pb, T.Pm[:], E, True, ["Pm", "E"], kb, M, ("st", t, u, h))
+                mm(Pb, T.I[:], T.xab[:, 16 * M * s + k:16 * M * (s + 1):16], False, ["I"] + (XB if s else XA), kb, M, ("st", t, u, h))
+            ac(T.cE[:, o:o + 2 * M], P[3 + u % 2][:, 0:2 * M], [kb], ["cEs%d" % u], AF.Sign, 0.25, n=2 * M)
+            for h, (k, s) in enumerate(halves[2 * u:2 * u + 2]):
+                mm(PE[s], sel("Z8", k), T.cE[:, o + M * h:o + M * h + M], False, ["Z8", "cEs%d" % u], KE[s], M)
+        for k in range(kd):
+            for s in (0, 1):
+                o, key = 2 * M * k + M * s, "cE%d_%d" % (k, s)
+                tt(T.cE[:, o:o + M], T.xab[:, 16 * M * s + k:16 * M * (s + 1):16], P[0][:, M:2 * M], OP.is_ge, (XB if s else XA) + ["P0"], [key], M)
+                mm(PE[s], sel("Z16", k), T.cE[:, o:o + M], False, ["Z16", key], KE[s], M)
+        tt(T.k2[:], P[2][:, 0:M], T.NE[:], OP.max, ["P2", "NE"], ["k2"], M)
+        tt(PE[1], PE[1], T.k2[:], OP.max, [KE[1], "k2"], [KE[1]], M)
+        ac(T.rE[:], PE[1], [KE[1]], ["rE"], AF.Identity, -OFF, n=M)
+        tt(T.L[:, n0:n1], PE[1], T.rE[:], OP.subtract, [KE[1], "rE"], ["Ln"], M)
+        if last:
+            dma("A", "dyn1", T.yn[:, n0:n1], T.L[:, n0:n1], 512 * M, ["Ln"], [])
+
+    gap = lambda i, j: HOP if calls[i][0] != calls[j][0] or calls[j][5] else (0.0 if calls[i][0] == "P" or not calls[i][4][j] else OWN)
+    members = {}
+    for i in range(len(calls)):
+        members.setdefault(units.get(i) or i, []).append(i)
+    members = sorted(members.values(), key=lambda m: m[-1])
+    node = {i: q for q, m in enumerate(members) for i in m}
+    order = schedule([calls[m[0]][0] for m in members], [sum(calls[i][2] for i in m) for m in members], [calls[m[0]][3] for m in members],
+                     [list({node[j]: gap(i, j) for i in m for j in calls[i][4] if node[j] != q}.items()) for q, m in enumerate(members)])
+    order = [i for q in order for i in members[q]]
+    closes = {calls[i][6]: i for i in order if calls[i][6] is not None}
     count = {"sV": 0, "sA": 0, "sP": 0, "sG": 0}
     seen = {e: {} for e in Q}
-    clock = {}
-    wrote, read = {}, {}
+    clock, event = {}, {}
 
     def need(e, ev):
         s, val = ev
@@ -98,561 +488,26 @@ def rank_program(g, core, T, topo):
                 seen[e][s2] = v2
         seen[e][s] = val
 
-    def order(e, own, r, w):
+    for i in order:
+        e, call, _, _, deps, ev, group = calls[i]
         evs = {}
-
-        def add(ev, same_ok):
-            if ev[0] == own and same_ok:
-                return
-            evs[ev[0]] = max(evs.get(ev[0], 0), ev[1])
-        for k in r:
-            if k in wrote:
-                add(wrote[k], e == "P")
-            if k[0] == "P" and k[1:].isdigit():
-                for ev in read.get(k, []):
-                    add(ev, True)
-        for k in w:
-            if k in wrote:
-                add(wrote[k], e == "P")
-            for ev in read.get(k, []):
-                add(ev, e == "P")
-        for s in sorted(evs, key=lambda s: s == own):
+        for j in deps:
+            s, val = event[j]
+            if deps[j] and (s != "sP" or e != "P"):
+                evs[s] = max(evs.get(s, 0), val)
+        for s in sorted(evs, key=lambda s: s == "s" + e):
             need(e, (s, evs[s]))
-
-    def done(e, ev, r, w):
-        clock[ev] = dict(seen[e])
-        for k in r:
-            read.setdefault(k, []).append(ev)
-        for k in w:
-            wrote[k] = ev
-            read[k] = []
-
-    def op(e, call, r, w):
-        s = "s" + e
-        order(e, s, r, w)
-        count[s] += 1
-        call().then_inc(T.sem[s], 1)
-        done(e, (s, count[s]), r, w)
-
-    def dma(e, sem, out, in_, r, w):
-        order(e, sem, r, w)
-        Q[e].dma_start(out, in_).then_inc(T.sem[sem], 16)
-        done(e, (sem, 16), r, w)
-
-    def send(src, dst, sem, r, c0=0, c1=M):
-        order("G", "sent", r, [])
-        g.remote_dma(T[dst][:, c0:c1], T[src][:, c0:c1], T.sem[sem], T.sem["sent"], pid, rid, emask)
-
-    v, a, pe = g.vector, g.scalar, g.tensor
-
-    def ts(out, in0, s1, s2, o0, o1, r, w):
-        if s2 is None:
-            op("V", lambda: v.tensor_scalar(out, in0, s1, None, o0), r, w)
+        if ev is None:
+            count["s" + e] += 1
+            ev = ("s" + e, count["s" + e])
+            (call() if group is None else call(closes[group] == i)).then_inc(T.sem[ev[0]], 1)
+            clock[ev] = dict(seen[e])
+        elif e == "G":
+            call()
         else:
-            op("V", lambda: v.tensor_scalar(out, in0, s1, s2, o0, o1), r, w)
-
-    def tt(out, in0, in1, o, r, w):
-        op("V", lambda: v.tensor_tensor(out, in0, in1, o), r, w)
-
-    def cp(out, in_, r, w):
-        op("V", lambda: v.tensor_copy(out, in_), r, w)
-
-    def ms(out, val, w):
-        op("V", lambda: v.memset(out, val), [], w)
-
-    def ac(out, in_, r, w, f=AF.Identity, bias=0.0, scale=1.0, acc=None):
-        op("A", lambda: a.activation(out, in_, f, bias, scale, accum_out=acc), r, w)
-
-    def ag(out, in_, r, w):
-        op("A", lambda: a.activation(out, in_, AF.Copy), r, w)
-
-    def mm(out, lhsT, rhs, st, sp, r, w):
-        op("P", lambda: pe.matmul(out, lhsT, rhs, st, sp), r, w)
-
-    def io(out, pat, base, cm, w, flt=True):
-        if flt:
-            op("G", lambda: g.iota(out, pat, base, cm, allow_small_or_imprecise_dtypes=True), [], w)
-        else:
-            op("G", lambda: g.iota(out, pat, base, cm), [], w)
-
-    def sel(Z, k):
-        return T[Z][:, 15 - k:143 - k]
-
-    def to_list(out, Z, src, keys, bank):
-        for m in range(16):
-            mm(out, sel(Z, m), src[:, m:M:16], m == 0, m == 15, keys + [Z], [bank])
-
-    P = [T["P%d" % b] for b in range(8)]
-    col = lambda j: T.cf[:, j:j + 1]
-    J128, J144 = T.J[:, 0:128], T.J[:, 0:144]
-    for t in range(1, RO):
-        wrote["mp%d" % t] = ("ap%d" % t, 2 * n_in)
-        wrote["mz%d" % t] = ("az%d" % t, n_in)
-
-    dma("S", "dps", T.psi[:], T.ps[:], [], ["psi"])
-    dma("A", "dwt", T.wti[:], T.wt[:], [], ["wti"])
-    dma("A", "dzi", T.mz0[:], T.zi[:], [], ["mz0"])
-    dma("S", "dkc", T.K0[:], T.kc[:], [], ["K0"])
-    dma("S", "dxc", T.X[:, 0:V], T.xc[:], [], ["X"])
-    for j in range(4):
-        dma("S", "dnb%d" % j, T.NB[:, 512 * j:512 * j + 512], T.nb[:, 512 * j:512 * j + 512], [], ["NB%d" % j])
-    io(T.pc[:], [[1, 128]], 0, 1, ["pc"], False)
-    io(T.J[:], [[1, M]], 0, 0, ["J"])
-    io(T.Jg[:], [[16, 8], [0, 16]], 0, 0, ["Jg"])
-    io(T.J16[:], [[0, 12], [1, 16]], 0, 0, ["J16"])
-    io(T.cG[:], [[1, 12]], 0, 0, ["cG"], False)
-    io(T.nG[:], [[16, 12 * RO]], V, 1, ["nG"])
-    io(T.ID[:, 0:W], [[1, W]], 0, 0, ["ID"])
-    io(T.ID[:, ALT:ALT + V - 1], [[1, V - 1]], TOP + 1, 0, ["ALT"])
-    io(T.ID[:, ALT + V - 1:ALT + W - M], [[1, W - M - V + 1]], TOP, 0, ["ALT2"])
-    ts(T.ci[:, 0:1], T.pc[:, 0:1], 15, None, OP.bitwise_and, None, ["pc"], ["ci0"])
-    ts(T.ci[:, 1:2], T.pc[:, 0:1], 1, None, OP.bitwise_and, None, ["pc"], ["ci1"])
-    cp(col(0), T.pc[:, 0:1], ["pc"], ["c0"])
-    ts(T.pc2[:], T.pc[:], 4, None, OP.arith_shift_right, None, ["pc"], ["pc2"])
-    cp(col(1), T.ci[:, 0:1], ["ci0"], ["c1"])
-    ts(col(8), T.ci[:, 1:2], -2.0, 1.0, OP.mult, OP.add, ["ci1"], ["c8"])
-    cp(T.SB[:, 0:128], T.pc2[:], ["pc2"], ["SB"])
-    tt(col(2), col(0), col(1), OP.subtract, ["c0", "c1"], ["c2"])
-    tt(col(4), col(0), col(8), OP.add, ["c0", "c8"], ["c4"])
-    ac(T.thr[:], T.J[:], ["J"], ["thr"], AF.Exp, 96 * LN2 + math.log(1.25), -LN2)
-    ts(T.I[:], J128, col(0), None, OP.is_equal, None, ["J", "c0"], ["I"])
-    ts(col(3), col(2), 15.0, None, OP.add, None, ["c2"], ["c3"])
-    ts(T.Bk[:], T.Jg[:], col(2), None, OP.is_equal, None, ["Jg", "c2"], ["Bk"])
-    ts(T.mask[:], T.J16[:], col(1), None, OP.is_equal, None, ["J16", "c1"], ["mask"])
-    cp(T.cGu[:], T.cG[:], ["cG"], ["cGu"])
-    ts(T.Z1[:], J144, col(3), None, OP.is_equal, None, ["J", "c3"], ["Z1"])
-    ts(T.Zd[:], J144, col(3), W / 16.0, OP.is_equal, OP.mult, ["J", "c3"], ["Zd"])
-    ts(T.nG[:], T.nG[:], col(2), None, OP.subtract, None, ["nG", "c2"], ["nG"])
-    ts(T.nPm[:], J128, col(4), -1.0, OP.is_equal, OP.mult, ["J", "c4"], ["nPm"])
-    ts(T.wG[:], T.nG[:, 0:12], -float(V), None, OP.add, None, ["nG"], ["wG"])
-    ac(T.wG[:], T.wG[:], ["wG"], ["wG"], AF.Exp, 95 * LN2, -LN2)
-    ts(T.I256[:], J128, col(0), 256.0, OP.is_equal, OP.mult, ["J", "c0"], ["I256"])
-    w0 = 128
-    while w0 < W:
-        w1 = min(2 * w0, W)
-        ac(T.SB[:, w0:w1], T.SB[:, 0:w1 - w0], ["SB"], ["SB"], AF.Identity, w0 / 16.0)
-        if w0 == 128:
-            ag(T.K1[:, 0:KK:2], T.K0[:, 1:KK:2], ["K0"], ["K1a"])
-            ag(T.K1[:, 1:KK:2], T.K0[:, 0:KK:2], ["K0"], ["K1b"])
-        w0 = w1
-    cp(T.wf[:], T.wti[:], ["wti"], ["wf"])
-    cp(T.pGf[:, 0:12], T.psi[:], ["psi"], ["pGf"])
-    ts(T.Zw[:], J144, col(3), T.wf[:], OP.is_equal, OP.mult, ["J", "c3", "wf"], ["Zw"])
-    tt(T.gx[:], T.pGf[:, 0:12].indirect(T.cGu[:, 0:12]), T.mask[:], OP.mult, ["pGf", "cGu", "mask"], ["gx"])
-    cp(T.mp0[:, M:M + 12], T.psi[:], ["psi"], ["mp0g"])
-    mm(P[6][:, 0:M], T.Bk[:], T.gx[:], True, True, ["Bk", "gx"], ["P6"])
-
-    def cuts_pe(t):
-        if t > 0:
-            mm(P[7][:, 16:17], T.on32[:], T.cnt[:], True, True, ["on32", "cnt"], ["P7"])
-        to_list(P[7][:, 0:12], "Zw", T["mz%d" % t], ["mz%d" % t], "P7")
-
-    def cuts_v(t, step):
-        if step == 0:
-            if t > 0:
-                ts(T.ui[:, 0:12], P[7][:, 0:12], P[7][:, 16:17], 262144.0, OP.add, OP.add, ["P7"], ["ui0"])
-            else:
-                ts(T.ui[:, 0:12], P[7][:, 0:12], 262144.0, None, OP.add, None, ["P7"], ["ui0"])
-        elif step == 1:
-            ts(T.ui[:, 12:24], T.ui[:, 0:12], KK - 1, None, OP.bitwise_and, None, ["ui0"], ["ui1"])
-        else:
-            cp(T.uu[:], T.ui[:, 12:24], ["ui1"], ["uu"])
-
-    def cuts_a():
-        ag(T.Ku[:, 0:M], T.K0[:].indirect(T.uu[:, 0:12]), ["K0", "uu"], ["Ku0"])
-        ag(T.Ku[:, M:2 * M], T.K1[:].indirect(T.uu[:, 0:12]), ["K1a", "K1b", "uu"], ["Ku1"])
-
-    cuts_pe(0)
-    cp(T.mp0[:, 0:M], P[6][:, 0:M], ["P6", "mp0g"], ["mp0"])
-    cuts_v(0, 0)
-    ts(T.Z16[:], J144, col(3), 16.0, OP.is_equal, OP.mult, ["J", "c3"], ["Z16"])
-    cuts_v(0, 1)
-    ts(T.Z8[:], J144, col(3), 8.0, OP.is_equal, OP.mult, ["J", "c3"], ["Z8"])
-    cuts_v(0, 2)
-    cuts_a()
-    ag(T.NS[:], T.SB[:, V:V + M], ["SB"], ["NS"])
-    ts(T.Pm[:], J128, col(4), None, OP.is_equal, None, ["J", "c4"], ["Pm"])
-    ts(T.nI[:], J128, col(0), -1.0, OP.is_equal, OP.mult, ["J", "c0"], ["nI"])
-    ts(T.Ih[:], J128, col(0), 0.5, OP.is_equal, OP.mult, ["J", "c0"], ["Ih"])
-    ts(T.t1[:], J128, col(0), 65536.0, OP.is_gt, OP.mult, ["J", "c0"], ["t1"])
-    ts(T.t2[:], J128, col(0), -1024.0, OP.is_equal, OP.mult, ["J", "c0"], ["t2"])
-    ms(T.CKC[:, 0:M], -31.0, ["CKCa"])
-    ms(T.CKC[:, M:2 * M], -32.0, ["CKCb"])
-    ms(T.q4[:], -0.25, ["q4"])
-    tt(T.t1[:], T.t1[:], T.Bk[:], OP.mult, ["t1", "Bk"], ["t1"])
-    tt(T.t2[:], T.t2[:], T.Bk[:], OP.add, ["t2", "Bk"], ["t2"])
-    ts(col(6), col(1), KD[0] - 0.5, 128.0, OP.is_ge, OP.mult, ["c1"], ["c6"])
-    ts(col(7), col(1), KD[RO - 1] - 0.5, 128.0, OP.is_ge, OP.mult, ["c1"], ["c7"])
-    tt(T.TT[:], T.t1[:], T.t2[:], OP.add, ["t1", "t2"], ["TT"])
-    ac(T.on32[:], T.I[:], ["I"], ["on32"], AF.Identity, 1.0 / 16, 0.0)
-    ts(T.CKE0[:], T.CKC[:], col(6), 0.25, OP.add, OP.add, ["CKCa", "CKCb", "c6"], ["CKE0"])
-    ts(T.CKE1[:], T.CKC[:], col(7), 0.25, OP.add, OP.add, ["CKCa", "CKCb", "c7"], ["CKE1"])
-
-    XA, XB = ["xa0", "xa1", "xa2"], ["xb0", "xb1", "xb2"]
-    LK = ["L0", "L1", "L2", "L3", "Ln"]
-    H = ((0, 128, 6), (128, 192, 5))
-    carry = []
-
-    for t in range(RO):
-        last = t == RO - 1
-        n0 = V + M * t
-        n1 = n0 + M
-        mp, mz = T["mp%d" % t], T["mz%d" % t]
-        kp, kz = "mp%d" % t, "mz%d" % t
-        pG = mp[:, M:M + 12]
-        C, E = T.CE[:, 0:M], T.CE[:, M:2 * M]
-        kd = KD[t]
-
-        if t > 0:
-            cp(T.pGf[:, 0:12], pG, [kp], ["pGf"])
-            ag(T.xp[:], T.X[:, 0:n0].indirect(pG), ["X", "Xn", kp], ["xp"])
-        for c in range(12):
-            e0 = c * M
-            ts(T.EQ[:, e0:e0 + M - 16 * c], mp[:, 16 * c:M], T.pGf[:, c:c + 1], T.wG[:, c:c + 1], OP.is_equal, OP.mult,
-               [kp, "pGf", "wG"], ["EQ%d" % c])
-            mm(P[5][:, 16 * c:M], T.Bk[:], T.EQ[:, e0:e0 + M - 16 * c], c == 0, c == 11, ["Bk", "EQ%d" % c], ["P5"])
-        if carry:
-            carry.pop(0)()
-        if t > 0:
-            tt(C, T.xp[:], P[1][:, 0:M], OP.min, ["xp", "P1"], ["C"])
-        tt(T.dup[:], P[5][:, 0:M], T.thr[:], OP.is_ge, ["P5", "thr"], ["dup"])
-        to_list(P[6][:, 0:12], "Zd", T.dup, ["dup"], "P6")
-        ac(T.act[:], T.dup[:], ["dup"], ["act", "cnt"], AF.Identity, 1.0, -1.0, T.cnt[:])
-        while carry:
-            carry.pop(0)()
-        ac(T.act4[:], T.dup[:], ["dup"], ["act4"], AF.Identity, 4096.0, -4096.0)
-        if t > 0:
-            cp(T.ab[:, 0:M], T.L[:, 0:n0].indirect(pG), LK + [kp], ["a"])
-            tt(E, T.xp[:], P[1][:, M:2 * M], OP.min, ["xp", "P1"], ["E"])
-        tt(T.of[:, 24:36], P[6][:, 0:12], T.nG[:, 12 * t:12 * t + 12], OP.min, ["P6", "nG"], ["of2"])
-        tt(T.of[:, 36:48], P[6][:, 0:12], T.pGf[:, 0:12], OP.add, ["P6", "pGf"], ["of3"])
-        tt(T.of[:, 12:24], T.of[:, 24:36], T.pGf[:, 0:12], OP.max, ["of2", "pGf"], ["of1"])
-        tt(T.of[:, 0:12], T.of[:, 36:48], T.nG[:, 12 * t:12 * t + 12], OP.max, ["of3", "nG"], ["of0"])
-        cp(T.ou[:, 12:24], T.of[:, 12:24], ["of1"], ["ou"])
-        cp(T.ou[:, 0:12], T.of[:, 0:12], ["of0"], ["on"])
-        off, offv = T.ou[:, 12:24], T.ou[:, 0:12]
-
-        def a_values():
-            ts(T.av[:], T.ab[:, 0:M], -1024.0, 1.0 / 4096, OP.add, OP.mult, ["a"], ["av"])
-
-        def other_c():
-            ac(T.NC[:], T.ID[:, 0:ALT + n0].indirect(offv), ["ID", "ALT", "ALT2", "on"], ["NC"], AF.Identity, 129.75, 1.0 / 4096)
-            ac(T.NE[:], T.ID[:, 0:n0].indirect(pG), ["ID", kp], ["NE"], AF.Identity, 130.0, 1.0 / 4096)
-
-        def gat_s(j):
-            i0, i1 = CH[j]
-            ag(T.sg[:, 16 * i0:16 * i1], T.SB[:, 0:n1].indirect(T.ab[:, i0:i1]), ["SB", "a"], ["sg%d" % j])
-
-        def sib_pe(j):
-            i0, i1 = CH[j]
-            bank = 5 + j % 2
-            for k in range(16):
-                mm(P[bank][:, 0:i1 - i0], sel("Z1", k), T.sg[:, 16 * i0 + k:16 * i1:16], k == 0, k == 15, ["Z1", "sg%d" % j], ["P%d" % bank])
-
-        def sib_v(j):
-            i0, i1 = CH[j]
-            bank = 5 + j % 2
-            ts(T.ab[:, M + i0:M + i1], P[bank][:, 0:i1 - i0], col(2), None, OP.subtract, None, ["P%d" % bank, "c2"], ["b%d" % j])
-
-        def gat_b(j):
-            i0, i1 = CH[j]
-            ag(T.xab[:, 16 * (M + i0):16 * (M + i1)], T.X[:, 0:n1].indirect(T.ab[:, M + i0:M + i1]), ["X", "Xn", "b%d" % j], ["xb%d" % j])
-
-        cp(T.SB[:, 0:n1].indirect(off), T.NS[:], ["NS", "ou"], ["SB"])
-        if t > 0:
-            other_c()
-            gat_s(0)
-        if t == 0:
-            tt(C, T.X[:, 0:n0].indirect(pG), T.Ku[:, 0:M], OP.min, ["X", kp, "Ku0"], ["C"])
-            tt(E, T.X[:, 0:n0].indirect(pG), T.Ku[:, M:2 * M], OP.min, ["X", kp, "Ku1"], ["E"])
-        mm(P[0][:, 0:M], T.nPm[:], C, True, False, ["nPm", "C"], ["P0"])
-        mm(P[0][:, 0:M], T.I256[:], T.dup[:], False, True, ["I256", "dup"], ["P0"])
-        mm(P[0][:, M:2 * M], T.nPm[:], E, True, True, ["nPm", "E"], ["P0"])
-        if not last:
-            mm(P[7][:, 0:M], T.I[:], C, True, False, ["I", "C"], ["P7"])
-            mm(P[7][:, 0:M], T.nI[:], mz[:], False, True, ["nI", kz], ["P7"])
-        cp(T.X[:, 0:n1].indirect(off), C, ["C", "ou"], ["X"])
-        if not last:
-            tt(T.dm[:], P[7][:, 0:M], T.act[:], OP.mult, ["P7", "act"], ["dm"])
-            mm(P[7][:, 0:M], T.I[:], T.q4[:], True, False, ["I", "q4"], ["P7"])
-            mm(P[7][:, 0:M], T.I[:], mz[:], False, False, ["I", kz], ["P7"])
-            mm(P[7][:, 0:M], T.Ih[:], T.dm[:], False, True, ["Ih", "dm"], ["P7"])
-        tt(T.X[:, n0:n1], E, T.act[:], OP.mult, ["E", "act", "X"], ["Xn"])
-        if last:
-            dma("S", "dyx", T.yx[:], T.X[:], ["X", "Xn"], [])
-        if t == 0:
-            for j in range(3):
-                cp(T.L[:, 512 * j:512 * j + 512], T.NB[:, 512 * j:512 * j + 512], ["NB%d" % j], ["L%d" % j])
-            cp(T.ab[:, 0:M], T.NB[:].indirect(pG), ["NB0", "NB1", "NB2", "NB3", kp], ["a"])
-            cp(T.L[:, 1536:V], T.NB[:, 1536:V], ["NB3"], ["L3"])
-            gat_s(0)
-
-        sib_pe(0)
-        if not ZE:
-            gat_s(1)
-        if not last:
-            ac(T.zy[:], P[7][:, 0:M], ["P7"], ["zy"], AF.Identity, MAGIC)
-        if not last:
-            ac(T["sz%d" % t][:], T.zy[:], ["zy"], ["sz%d" % t], AF.Identity, -MAGIC)
-            send("sz%d" % t, "mz%d" % (t + 1), "az%d" % (t + 1), ["sz%d" % t])
-        if ZE:
-            gat_s(1)
-        mm(P[1][:, 0:M], T.I[:], T.CKC[:, 0:M], True, False, ["I", "CKCa"], ["P1"])
-        cke = "CKE1" if last else "CKE0"
-        mm(P[2][:, 0:2 * M], T.I[:], T[cke][:], True, False, ["I", cke], ["P2"])
-        half = AV // 2
-        cp(T.xab[:, 0:16 * half], T.X[:, 0:n1].indirect(T.ab[:, 0:half]), ["X", "Xn", "a"], ["xa2"])
-        sib_v(0)
-        sib_pe(1)
-        a_values()
-        mm(P[1][:, 0:M], T.I[:], T.av[:], False, False, ["I", "av"], ["P1"])
-        mm(P[2][:, 0:M], T.I[:], T.av[:], False, False, ["I", "av"], ["P2"])
-        cp(T.xab[:, 16 * half:16 * AV], T.X[:, 0:n1].indirect(T.ab[:, half:AV]), ["X", "Xn", "a"], ["xa0"])
-        sib_v(1)
-        if SO:
-            gat_s(2)
-            sib_pe(2)
-        if AV < M:
-            ag(T.xab[:, 16 * AV:16 * M], T.X[:, 0:n1].indirect(T.ab[:, AV:M]), ["X", "Xn", "a"], ["xa1"])
-        if not SO:
-            gat_s(2)
-        gat_b(0)
-        if t == 0:
-            other_c()
-        gat_b(1)
-
-        ks = list(range(kd, 16))
-        npre = min(len(PRE) + PRE3, len(ks) // 2)
-        todo = [((ks[2 * u], s), (ks[2 * u + 1], s)) for s in (0, 1) for u in range(npre)]
-        todo += [((k, 0), (k, 1)) for k in ks[2 * npre:]]
-        st = {"staged": [], "signed": [], "n": 0, "red": 0}
-
-        def stage():
-            if not todo:
-                return
-            unit = todo.pop(0)
-            slot = kd + st["n"]
-            bank = (3, 4, 1)[st["n"]] if st["n"] < 3 else 4 - st["n"] % 2
-            st["n"] += 1
-            kb = "P%d" % bank
-            if unit[0][0] == unit[1][0]:
-                mm(P[bank][:, 0:2 * M], T.I[:], T.xab[:, unit[0][0]:32 * M:16], True, False, ["I"] + XA + XB, [kb])
-                mm(P[bank][:, 0:M], T.Pm[:], E, False, False, ["Pm", "E"], [kb])
-                mm(P[bank][:, M:2 * M], T.Pm[:], E, False, True, ["Pm", "E"], [kb])
-            else:
-                for h, (k, s) in enumerate(unit):
-                    mm(P[bank][:, M * h:M * h + M], T.Pm[:], E, True, False, ["Pm", "E"], [kb])
-                    mm(P[bank][:, M * h:M * h + M], T.I[:], T.xab[:, 16 * M * s + k:16 * M * (s + 1):16], False, True,
-                       ["I"] + (XB if s else XA), [kb])
-            st["staged"].append((unit, slot, bank))
-
-        def sign():
-            if not st["staged"]:
-                return
-            unit, slot, bank = st["staged"].pop(0)
-            ac(T.cE[:, 2 * M * slot:2 * M * (slot + 1)], P[bank][:, 0:2 * M], ["P%d" % bank], ["cE%d" % slot], AF.Sign, 0.5)
-            st["signed"].append((unit, slot))
-
-        def red(unit, slot, Z, keys):
-            st["red"] += 1
-            o = 2 * M * slot
-            if unit[0][0] == unit[1][0]:
-                mm(P[2][:, 0:2 * M], sel(Z, unit[0][0]), T.cE[:, o:o + 2 * M], False, st["red"] == 16, [Z] + keys, ["P2"])
-            else:
-                for h, (k, s) in enumerate(unit):
-                    mm(P[2][:, M * s:M * s + M], sel(Z, k), T.cE[:, o + M * h:o + M * h + M], False, st["red"] == 16 and h == 1,
-                       [Z] + keys, ["P2"])
-
-        def red_a():
-            if st["signed"]:
-                unit, slot = st["signed"].pop(0)
-                red(unit, slot, "Z8", ["cE%d" % slot])
-
-        def step():
-            sign()
-            stage()
-            if len(st["signed"]) > 1 or not st["staged"]:
-                red_a()
-
-        def e_a(k):
-            o = 2 * M * k
-            tt(T.cE[:, o:o + M], T.xab[:, k:16 * M:16], P[0][:, M:2 * M], OP.is_ge, XA + ["P0"], ["cEa%d" % k])
-
-        def e_on_v(k, now=True):
-            o = 2 * M * k
-            if EG <= k < kd - 1:
-                e_a(k)
-            tt(T.cE[:, o + M:o + 2 * M], T.xab[:, 16 * M + k:32 * M:16], P[0][:, M:2 * M], OP.is_ge, XB + ["P0"], ["cE%d" % k])
-            if now:
-                e_red(k)
-
-        def e_red(k):
-            red(((k, 0), (k, 1)), k, "Z16", ["cEa%d" % k, "cE%d" % k])
-
-        def b_scores(j):
-            i0, i1 = CH[j]
-            if BM and j == 1:
-                i0 = 0
-            b = H[j // 2][2]
-            for k in range(16):
-                o = 2 * M * k + M
-                key = "cCb%d_%d" % (j, k)
-                tt(T.cC[:, o + i0:o + i1], T.xab[:, 16 * (M + i0) + k:16 * (M + i1):16], P[0][:, i0:i1], OP.is_ge,
-                   ["xb0", "xb%d" % j, "P0"], [key])
-                mm(P[b][:, i0:i1], sel("Z16", k), T.cC[:, o + i0:o + i1], False, j > 0 and k == 15, ["Z16", key], ["P%d" % b])
-                if j == 1 and k == K1:
-                    tt(T.k1[:], P[1][:, 0:M], T.NC[:], OP.max, ["P1", "NC"], ["k1"])
-                    if PRE3:
-                        stage()
-                if j == 2 and k == 0:
-                    sign()
-                    if not last:
-                        cuts_v(t + 1, 0)
-                if j == 2 and k == KM:
-                    f_max(0)
-                    f_exp(0)
-                    sign()
-                if j == 2 and k == KM + 2 and not last:
-                    cuts_v(t + 1, 1)
-                if j == 2 and k == KA and not last:
-                    f_arg(0)
-
-        def f_max(h):
-            i0, i1, b = H[h]
-            tt(P[b][:, i0:i1], P[b][:, i0:i1], T.k1[:, i0:i1], OP.max, ["P%d" % b, "k1"], ["P%d" % b])
-
-        def f_exp(h):
-            i0, i1, b = H[h]
-            if not last:
-                ac(T.vv[:, i0:i1], P[b][:, i0:i1], ["P%d" % b], ["vv%d" % h], AF.Exp, -176 * LN2, LN2)
-            ag(T.rC[:, i0:i1], P[b][:, i0:i1], ["P%d" % b], ["rC%d" % h])
-
-        def f_arg(h):
-            i0, i1, b = H[h]
-            mm(P[7 - h][:, 256 + i0:256 + i1], T.TT[:], T.vv[:, i0:i1], True, True, ["TT", "vv%d" % h], ["P%d" % (7 - h)])
-
-        def f_win(h):
-            i0, i1, b = H[h]
-            at = P[7 - h][:, 256 + i0:256 + i1]
-            ts(at, at, 0.0, None, OP.is_lt, None, ["P%d" % (7 - h)], ["P%d" % (7 - h)])
-
-        def f_sub(h):
-            i0, i1, b = H[h]
-            tt(T.ec[:, i0:i1], P[b][:, i0:i1], T.rC[:, i0:i1], OP.subtract, ["P%d" % b, "rC%d" % h], ["ec%d" % h])
-
-        def f_min(h):
-            i0, i1, b = H[h]
-            tt(T.mk[:, i0:i1], P[7 - h][:, 256 + i0:256 + i1], T.ec[:, i0:i1], OP.mult, ["P%d" % (7 - h), "ec%d" % h], ["mk%d" % h])
-            mm(P[7][:, i0:i1], T.Bk[:], T.mk[:, i0:i1], True, True, ["Bk", "mk%d" % h], ["P7"])
-
-        for k in range(16):
-            o = 2 * M * k
-            tt(T.cC[:, o:o + M], T.xab[:, k:16 * M:16], P[0][:, 0:M], OP.is_ge, XA + ["P0"], ["cCa%d" % k])
-            mm(P[1][:, 0:M], sel("Z16", k), T.cC[:, o:o + M], False, k == 15, ["Z16", "cCa%d" % k], ["P1"])
-            if k == KU and not last:
-                cuts_pe(t + 1)
-            if k == K2 and not SO:
-                sib_pe(2)
-            if k == K2 + 4:
-                sib_v(2)
-                gat_b(2)
-                ts(T.bv[:], T.ab[:, M:2 * M], -1024.0, 1.0 / 4096, OP.add, OP.mult, ["b0", "b1", "b2"], ["bv"])
-            if k == K2 + 5:
-                for (i0, i1, b) in H:
-                    mm(P[b][:, i0:i1], T.I[:], T.CKC[:, M + i0:M + i1], True, False, ["I", "CKCb"], ["P%d" % b])
-                    mm(P[b][:, i0:i1], T.I[:], T.bv[:, i0:i1], False, False, ["I", "bv"], ["P%d" % b])
-                mm(P[2][:, M:2 * M], T.I[:], T.bv[:], False, False, ["I", "bv"], ["P2"])
-            if k in PRE:
-                stage()
-        for k in range(EG // 2):
-            e_a(k)
-        if not BM:
-            b_scores(0)
-        for k in range(EG // 2, EG):
-            e_a(k)
-        b_scores(1)
-        b_scores(2)
-        stage()
-        if S2:
-            stage()
-        f_sub(0)
-        e_a(KD[t] - 1)
-        f_max(1)
-        f_exp(1)
-        if not last:
-            f_win(0)
-            f_arg(1)
-            f_min(0)
-            sign()
-            red_a()
-            stage()
-            cuts_v(t + 1, 2)
-            sign()
-            cuts_a()
-            ag(P[1][:, 0:2 * M], T.Ku[:], ["Ku0", "Ku1"], ["P1"])
-            for k in range(F1):
-                e_on_v(k, False)
-        f_sub(1)
-        if not last:
-            sp = "sp%d" % t
-            f_win(1)
-            ts(T[sp][:, 0:128], P[7][:, 0:128], 4096.0, 1024.0, OP.mult, OP.add, ["P7"], [sp + "a"])
-            send(sp, "mp%d" % (t + 1), "ap%d" % (t + 1), [sp + "a"], 0, 128)
-            f_min(1)
-            to_list(P[7][:, M:M + 12], "Z1", T.mk, ["mk0", "mk1"], "P7")
-            sign()
-            stage()
-            red_a()
-            for k in range(F1):
-                e_red(k)
-            for k in range(F1, F2):
-                e_on_v(k)
-            ts(T[sp][:, 128:M + 12], P[7][:, 128:M + 12], 4096.0, 1024.0, OP.mult, OP.add, ["P7"], [sp])
-            send(sp, "mp%d" % (t + 1), "ap%d" % (t + 1), [sp], 128, M + 12)
-
-        def c_list():
-            ts(T.L[:, 0:n1].indirect(off), T.ec[:], 4096.0, 1024.0, OP.mult, OP.add, ["ec0", "ec1", "ou"], LK)
-
-        if last:
-            c_list()
-            dma("S", "dyn0", T.yn[:, 0:n0], T.L[:, 0:n0], LK[:4], [])
-            sign()
-            sign()
-            stage()
-            red_a()
-            red_a()
-            e_on_v(0)
-        k0 = 1 if last else F2
-        for k in range(k0, kd):
-            step()
-            e_on_v(k)
-        while st["staged"] or st["signed"] or todo:
-            step()
-        if not last:
-            c_list()
-            ag(T.NS[:], T.SB[:, n1:n1 + M], ["SB"], ["NS"])
-
-        def e_max():
-            tt(T.k2[:], P[2][:, 0:M], T.NE[:], OP.max, ["P2", "NE"], ["k2"])
-            tt(P[2][:, M:2 * M], P[2][:, M:2 * M], T.k2[:], OP.max, ["P2", "k2"], ["P2"])
-            ac(T.rE[:], P[2][:, M:2 * M], ["P2"], ["rE"], AF.Identity, -0.25)
-
-        def e_sub():
-            tt(P[2][:, M:2 * M], P[2][:, M:2 * M], T.rE[:], OP.subtract, ["P2", "rE"], ["P2"])
-
-        def e_end(n0=n0, n1=n1):
-            tt(T.L[:, n0:n1], P[2][:, M:2 * M], T.act4[:], OP.mult, ["P2", "act4", "Ln"], ["Ln"])
-
-        if last:
-            e_max()
-            e_sub()
-            e_end()
-            dma("A", "dyn1", T.yn[:, n0:n1], T.L[:, n0:n1], ["Ln"], [])
-        elif EARLY:
-            e_max()
-            carry.extend([e_sub, e_end])
-        else:
-            carry.extend([e_max, e_sub, e_end])
+            call().then_inc(T.sem[ev[0]], 16)
+            clock[ev] = dict(seen[e])
+        event[i] = ev
 
     g.wait_ge(T.sem["sent"], 3 * (RO - 1) * n_eng)
     for s in ("sV", "sA", "sP", "sG"):

@@ -8,30 +8,35 @@ U = 4096.0
 OFF = 1536.0
 TOP = -103 * 4096
 BIG = 2097152.0
-MAGIC = 12582912.0
 LN2 = math.log(2.0)
-KD = 12
+KD = 11
 KDL = 10
-NPRE = 0
-S1 = 1
-S2 = 0
-S3 = 1
-S4 = 1
-EB = 6
-UA = 8
-UB = 8
-UL = 2
-UE = 4
-UX = 16
+NPRE = 1
 CH = ((0, 64), (64, 128), (128, 192))
 XS = ((0, 64, "V"), (64, 128, "A"), (128, 192, "A"))
 CA = ((0, 128), (128, 192))
-BU = "V"
-LV = 3
-SV = 3008
-NSTRIP = 4
-PASSES = 6
-CYC, PEC, GATHER, SCATTER, HOP, OWN, FAR, DMA_US, DMA_BW = 0.83e-3, 0.5e-3, 1.56, 3.8, 0.1, 0.06, 2.3, 1.8, 200e3
+H = ((0, 128, 6), (128, 192, 5))
+STRIP = ("V", "V", "V", "A")
+NBP = 1
+LV = 0
+BV = 5
+YF = 1
+EB = 6
+BM = 0
+SD = 0
+SK = 0
+AM = 0
+ONE = 0
+WV = 2
+SV = 0
+RV = 1
+EV = 0
+AV = 0
+CYC = 0.83e-3
+GUESS = ({"pe": 0.45e-3, "mm": 0.0, "act": 0.1, "gather": 1.4, "scatter": 3.8, "hop": 0.14, "own": 0.07, "far": 2.3, "dma": 1.8, "bw": 200e3},
+         {"pe": 0.43e-3, "mm": 0.0, "act": 0.1, "gather": 1.6, "scatter": 4.2, "hop": 0.11, "own": 0.1, "far": 1.6, "dma": 1.0, "bw": 400e3})
+MOVES = 30000
+SEED = 1
 
 SCRATCH = {
     "X": ("sbuf", [128, W + M], "bfloat16"), "L": ("sbuf", [128, W + M], "float32"),
@@ -48,7 +53,9 @@ SCRATCH = {
     "on32": ("sbuf", [128, 128], "float32"), "I32": ("sbuf", [128, 128], "float32"), "CK": ("sbuf", [128, 2 * M], "bfloat16"),
     "CKE0": ("sbuf", [128, 2 * M], "float16"), "CKE1": ("sbuf", [128, 2 * M], "float16"),
     "pGf": ("sbuf", [128, 16], "float32"), "EQ": ("sbuf", [128, 12 * M], "bfloat16"),
-    "dup": ("sbuf", [128, M], "bfloat16"), "zr": ("sbuf", [128, M], "float16"),
+    "dup": ("sbuf", [128, M], "bfloat16"), "zr": ("sbuf", [128, M], "float16"), "spare": ("sbuf", [128, M], "bfloat16"),
+    "thm": ("sbuf", [128, M], "float32"), "run": ("sbuf", [128, M], "bfloat16"), "dg": ("sbuf", [128, M], "bfloat16"),
+    "ds": ("sbuf", [128, M], "bfloat16"), "og": ("sbuf", [128, 48], "float32"), "pm": ("sbuf", [128, M], "float32"), "pn": ("sbuf", [128, M], "float32"),
     "cnt": ("sbuf", [128, 1], "float32"), "ou": ("sbuf", [128, 24], "uint16"),
     "ui": ("sbuf", [128, 24], "int32"), "uu": ("sbuf", [128, 12], "uint16"),
     "Ku": ("sbuf", [128, 2 * M], "bfloat16"), "CE": ("sbuf", [128, 2 * M], "bfloat16"),
@@ -59,7 +66,7 @@ SCRATCH = {
     "NC": ("sbuf", [128, M], "float32"), "NE": ("sbuf", [128, M], "float32"),
     "k1": ("sbuf", [128, M], "float32"), "k2": ("sbuf", [128, M], "float32"),
     "rC": ("sbuf", [128, M], "bfloat16"), "rE": ("sbuf", [128, M], "bfloat16"), "vv": ("sbuf", [128, M], "bfloat16"),
-    "ec": ("sbuf", [128, M], "float32"), "mk": ("sbuf", [128, M], "float16"), "zy": ("sbuf", [128, M], "float32"),
+    "ec": ("sbuf", [128, M], "float32"), "mk": ("sbuf", [128, M], "float16"),
 }
 for _n in ("I", "nI", "Ih", "I256", "IU", "nBI", "nIc", "Pm", "nPm", "Bk", "TT", "t1", "t2"):
     SCRATCH[_n] = ("sbuf", [128, 128], "bfloat16")
@@ -67,59 +74,105 @@ for _n in ("Z1", "Z16", "Z8", "Zc", "Zd", "Zw", "Zb", "nZb"):
     SCRATCH[_n] = ("sbuf", [128, 144], "bfloat16")
 for _t in range(RO):
     SCRATCH["mp%d" % _t] = ("sbuf", [128, M + 12], "uint16")
-    SCRATCH["mz%d" % _t] = ("sbuf", [128, M], "bfloat16")
+    SCRATCH["mz%d" % _t] = ("sbuf", [128, M], "float16" if _t else "bfloat16")
 for _t in range(RO - 1):
     SCRATCH["sp%d" % _t] = ("sbuf", [128, M + 12], "uint16")
-    SCRATCH["sz%d" % _t] = ("sbuf", [128, M], "bfloat16")
+    SCRATCH["sz%d" % _t] = ("sbuf", [128, M], "float16")
 for _b in range(8):
     SCRATCH["P%d" % _b] = ("psum", [128, 512], "float32")
 
-DMAS = ["dps", "dwt", "dzi", "dkc", "dxc", "dnb0", "dnb1", "dnb2", "dnb3", "dyx", "dyn0", "dyn1"]
+DMAS = ["dps", "dwt", "dzi", "dkc", "dxc", "dyx", "dyn0", "dyn1"] + ["dnb%d" % _j for _j in range(NBP)]
 SEMAPHORES = ["sV", "sA", "sP", "sG", "sent"] + DMAS + ["ap%d" % t for t in range(1, RO)] + ["az%d" % t for t in range(1, RO)]
+PLAN = {}
 
 
-def place(order, queue, busy, after, edges):
-    start = [0.0] * len(queue)
-    slots = {}
-    for i in order:
-        t = 0.0
-        for j, gap in edges[i]:
-            t = max(t, start[j] + busy[j] + after[j] + gap)
-        s = slots.setdefault(queue[i], [])
-        lo, hi = 0, len(s)
-        while lo < hi:
-            mid = (lo + hi) // 2
-            if s[mid][1] <= t:
-                lo = mid + 1
-            else:
-                hi = mid
-        while lo < len(s) and s[lo][0] < t + busy[i] - 1e-9:
-            t = max(t, s[lo][1])
-            lo += 1
-        s.insert(lo, (t, t + busy[i]))
-        start[i] = t
-    return start
-
-
-def schedule(queue, busy, after, before):
+def first_plan(queue, busy, tail, edges):
     n = len(queue)
-    behind = [[] for _ in range(n)]
-    for i in range(n):
-        for j, gap in before[i]:
-            behind[j].append((i, gap + after[j]))
-    rest = [0.0] * n
+    rest = [busy[i] + tail[i] for i in range(n)]
     for i in reversed(range(n)):
-        rest[i] = busy[i] + max([after[i]] + [gap + rest[j] for j, gap in behind[i]])
-    best = None
-    none = [0.0] * n
-    for _ in range(PASSES):
-        start = place(sorted(range(n), key=lambda i: (-rest[i], i)), queue, busy, after, before)
-        end = max(start[i] + busy[i] + after[i] for i in range(n))
-        if best is None or end < best[0]:
-            best = (end, start)
-        back = place(sorted(range(n), key=lambda i: (-start[i] - busy[i], -i)), queue, busy, none, behind)
-        rest = [back[i] + busy[i] for i in range(n)]
-    return sorted(range(n), key=lambda i: (best[1][i], i))
+        for j, gap in edges[i]:
+            rest[j] = max(rest[j], busy[j] + gap + rest[i])
+    start, slots = [0.0] * n, {}
+    for i in sorted(range(n), key=lambda i: (-rest[i], i)):
+        t = max([0.0] + [start[j] + busy[j] + gap for j, gap in edges[i]])
+        s = slots.setdefault(queue[i], [])
+        at = len(s)
+        while at and s[at - 1][1] > t:
+            at -= 1
+        while at < len(s) and s[at][0] < t + busy[i] - 1e-9:
+            t = max(t, s[at][1])
+            at += 1
+        s.insert(at, (t, t + busy[i]))
+        start[i] = t
+    return sorted(range(n), key=lambda i: (start[i], i))
+
+
+def replay(order, queue, busy, tail, edges):
+    end, why, free, ahead = [0.0] * len(order), [-1] * len(order), {}, {}
+    top, last = 0.0, -1
+    for i in order:
+        q = queue[i]
+        t, w = free.get(q, 0.0), ahead.get(q, -1)
+        for j, gap in edges[i]:
+            if end[j] + gap > t:
+                t, w = end[j] + gap, j
+        end[i] = free[q] = t = t + busy[i]
+        ahead[q], why[i] = i, w
+        if t + tail[i] > top:
+            top, last = t + tail[i], i
+    return top, why, last
+
+
+def schedule(queue, guesses):
+    n = len(queue)
+    before = [set(j for j, gap in e) for e in guesses[0][2]]
+    behind = [set() for _ in range(n)]
+    for i in range(n):
+        for j in before[i]:
+            behind[j].add(i)
+    state = [SEED]
+
+    def draw(k):
+        state[0] = (state[0] * 1103515245 + 12345) % 2147483648
+        return (state[0] >> 8) % k
+
+    order = first_plan(queue, *guesses[0])
+    runs = [replay(order, queue, *q) for q in guesses]
+    best = (sum(r[0] for r in runs), order)
+    now = best[0]
+    for move in range(MOVES):
+        top, why, i = runs[draw(len(runs))]
+        pairs = []
+        while i >= 0:
+            j = why[i]
+            if j >= 0 and queue[j] == queue[i] and j not in before[i]:
+                pairs.append((j, i))
+            i = j
+        if not pairs:
+            break
+        j, i = pairs[draw(len(pairs))]
+        lo, hi = order.index(j), order.index(i)
+        ahead, step = draw(2), (0, 0, 1, 2, 5)[draw(5)]
+        k = lo if ahead else hi
+        while step and 0 < k < n - 1:
+            k += -1 if ahead else 1
+            if queue[order[k]] == queue[i]:
+                lo, hi, step = min(lo, k), max(hi, k), step - 1
+        part = order[lo:hi + 1]
+        moved = {i if ahead else j}
+        for x in (reversed(part) if ahead else part):
+            if x in moved:
+                moved |= before[x] if ahead else behind[x]
+        if order[lo if ahead else hi] in moved:
+            continue
+        new = order[:lo] + [x for x in part if (x in moved) == ahead] + [x for x in part if (x in moved) != ahead] + order[hi + 1:]
+        tried = [replay(new, queue, *q) for q in guesses]
+        length = sum(r[0] for r in tried)
+        if length < now + 0.002 * draw(100) * (1 - move / MOVES):
+            now, order, runs = length, new, tried
+            if length < best[0]:
+                best = (length, new)
+    return best[1]
 
 
 def rank_program(g, core, T, topo):
@@ -137,7 +190,7 @@ def rank_program(g, core, T, topo):
     calls = []
     wrote, read, opened, units = {}, {}, {}, {}
 
-    def note(e, call, busy, r, w, after=0.0, event=None, adds=False, group=None):
+    def note(e, call, busy, r, w, after=lambda q: 0.0, event=None, adds=False, group=None):
         deps = {}
         for k in r:
             if k[0] == "~":
@@ -164,19 +217,22 @@ def rank_program(g, core, T, topo):
             else:
                 wrote[k] = [i]
                 read[k] = []
-        return i
+
+    def unit(*name):
+        units[len(calls)] = name
 
     def cyc(n, kind):
-        return {"": max(64, n) * CYC, "h": max(64, n / 2) * CYC, "d": max(64, 2 * n) * CYC, "g": 0.06 + n * GATHER * CYC,
-                "s": 0.05 + n * SCATTER * CYC}[kind]
+        if kind in ("g", "s"):
+            return lambda q: 0.06 + n * q["gather" if kind == "g" else "scatter"] * CYC
+        return lambda q: max(64, n * {"": 1, "h": 0.5, "d": 2}[kind]) * CYC
 
     def dma(e, sem, out, in_, nbytes, r, w):
-        t = nbytes / DMA_BW + 0.2
-        note(e, lambda: Q[e].dma_start(out, in_), t if e == "S" else 0.05, r, w, DMA_US, (sem, 16))
+        note(e, lambda: Q[e].dma_start(out, in_), lambda q: nbytes / q["bw"] + 0.2 if e == "S" else 0.05, r, w, lambda q: q["dma"], (sem, 16))
 
-    def send(src, dst, sem, val, r, w, c0, c1, adds=False):
-        note("G", lambda: g.remote_dma(T[dst][:, c0:c1], T[src][:, c0:c1], T.sem[sem], T.sem["sent"], pid, rid, emask), 0.3, r, w,
-             FAR + (c1 - c0) * 0.005, (sem, val), adds)
+    def send(src, dst, sem, val, r, c0, c1, slack=0.0, adds=False):
+        issue = 0.3 if read.get("far") else 2.3
+        note("G", lambda: g.remote_dma(T[dst][:, c0:c1], T[src][:, c0:c1], T.sem[sem], T.sem["sent"], pid, rid, emask), lambda q: issue,
+             r + ["far"], [dst], lambda q: q["far"] + slack + (c1 - c0) * 0.005, (sem, val), adds)
 
     v, a, pe = g.vector, g.scalar, g.tensor
 
@@ -192,45 +248,50 @@ def rank_program(g, core, T, topo):
     def cp(out, in_, r, w, n=64, kind=""):
         note("V", lambda: v.tensor_copy(out, in_), cyc(n, kind), r, w)
 
+    def scan(out, src, r, w, c0, c1, kind):
+        note("V", lambda: v.tensor_tensor_scan(out[:, c0:c1], T.run[:, c0:c1], src[:, c0:c1], 0.0, OP.mult, OP.add), cyc(c1 - c0, kind), r + ["run"], w)
+
     def ms(out, val, w, n=64):
         note("V", lambda: v.memset(out, val), cyc(n, "h"), [], w)
 
     def ac(out, in_, r, w, f=AF.Identity, bias=0.0, scale=1.0, acc=None, n=64, kind=""):
-        note("A", lambda: a.activation(out, in_, f, bias, scale, accum_out=acc), cyc(n, kind) + (0.14 if acc is not None else 0), r, w)
+        note("A", lambda: a.activation(out, in_, f, bias, scale, accum_out=acc), lambda q: q["act"] + cyc(n, kind)(q), r, w)
 
     def ag(out, in_, r, w, n=64, kind=""):
-        note("A", lambda: a.activation(out, in_, AF.Copy), cyc(n, kind), r, w)
+        note("A", lambda: a.activation(out, in_, AF.Copy), lambda q: q["act"] + cyc(n, kind)(q), r, w)
 
-    def mm(out, lhsT, rhs, st, r, bank, n, unit=None):
+    def mm(out, lhsT, rhs, st, r, bank, n):
         if st:
             opened[bank] = len(calls)
-        units[len(calls)] = unit
-        note("P", lambda stop: pe.matmul(out, lhsT, rhs, st, stop), max(64, n) * PEC, r, [bank], adds=not st, group=opened[bank])
+        note("P", lambda stop: pe.matmul(out, lhsT, rhs, st, stop), lambda q: q["mm"] + max(64, n) * q["pe"], r, [bank], adds=not st, group=opened[bank])
 
     def io(out, pat, base, cm, w, n, flt=True):
         if flt:
-            note("G", lambda: g.iota(out, pat, base, cm, allow_small_or_imprecise_dtypes=True), 0.13 + 2 * n * CYC, [], w)
+            note("G", lambda: g.iota(out, pat, base, cm, allow_small_or_imprecise_dtypes=True), lambda q: 0.13 + 2 * n * CYC, [], w)
         else:
-            note("G", lambda: g.iota(out, pat, base, cm), 0.13 + 2 * n * CYC, [], w)
+            note("G", lambda: g.iota(out, pat, base, cm), lambda q: 0.13 + 2 * n * CYC, [], w)
 
     def sel(Z, k):
         return T[Z][:, 15 - k:143 - k]
 
     def to_list(out, Z, src, keys, bank, first=True):
         for m in range(16):
-            mm(out, sel(Z, m), src[:, m:M:16], first and m == 0, keys + [Z], bank, 12, ("list", len(calls) - m))
+            unit("list", len(calls) - m)
+            mm(out, sel(Z, m), src[:, m:M:16], first and m == 0, keys + [Z], bank, 12)
 
     P = [T["P%d" % b] for b in range(8)]
     col = lambda j: T.cf[:, j:j + 1]
     J128, J144 = T.J[:, 0:128], T.J[:, 0:144]
 
-    dma("S", "dps", T.psi[:], T.ps[:], 6144, [], ["psi", "ld"])
+    dma("S", "dps", T.psi[:], T.ps[:], 6144, [], ["psi"])
     dma("A", "dwt", T.wti[:], T.wt[:], 512, [], ["wti"])
     dma("A", "dzi", T.mz0[:], T.zi[:], 256 * M, [], ["mz0"])
-    dma("S", "dkc", T.K0[:], T.kc[:], 256 * KK, [], ["K0"])
-    dma("S", "dxc", T.X[:, 0:V], T.xc[:], 256 * V, [], ["X"])
-    for j in range(4):
-        dma("S", "dnb%d" % j, T.NB[:, 512 * j:512 * j + 512], T.nb[:, 512 * j:512 * j + 512], 512 * 512, [], ["NB%d" % j])
+    dma("S", "dkc", T.K0[:], T.kc[:], 256 * KK, ["~psi"], ["K0"])
+    dma("S", "dxc", T.X[:, 0:V], T.xc[:], 256 * V, ["~K0"], ["X"])
+    for j in range(NBP):
+        w = V // NBP
+        dma("S", "dnb%d" % j, T.NB[:, w * j:w * j + w], T.nb[:, w * j:w * j + w], 512 * w, ["~X"],
+            ["NB%d" % q for q in range(4 * j // NBP, 4 * (j + 1) // NBP)])
     io(T.pc[:], [[1, 2]], 0, 1, ["pc"], 2, False)
     io(T.J[:], [[1, M]], 0, 0, ["J"], M)
     io(T.Jg[:], [[16, 8], [0, 16]], 0, 0, ["Jg"], 128)
@@ -262,6 +323,9 @@ def rank_program(g, core, T, topo):
     ts(T.nG[:], T.nG[:], col(2), None, OP.subtract, None, ["nG", "c2"], ["nG"], 72)
     ts(T.wG[:], T.nG[:, 0:12], -float(V), None, OP.add, None, ["nG"], ["wG"])
     ac(T.wG[:], T.wG[:], ["wG", "thr"], ["wG"], AF.Exp, 95 * LN2, -LN2)
+    if SD:
+        ts(T.thm[:], T.mask[:], -1e29, 1e29, OP.mult, OP.add, ["mask"], ["thm"], M)
+        tt(T.thm[:], T.thm[:], T.thr[:], OP.max, ["thm", "thr"], ["thm"], M, "d")
     ts(T.t1[:], J128, col(0), 65536.0, OP.is_gt, OP.mult, ["J", "c0"], ["t1"])
     tt(T.t1[:], T.t1[:], T.Bk[:], OP.mult, ["t1", "Bk"], ["t1"], 128, "d")
     tt(T.t2[:], T.t2[:], T.Bk[:], OP.add, ["t2", "Bk"], ["t2"], 128, "d")
@@ -272,12 +336,16 @@ def rank_program(g, core, T, topo):
     ts(T.CKE0[:], T.CK[:], col(6), OFF / U, OP.add, OP.add, ["CKa", "CKb", "c6"], ["CKE0"], 2 * M, "h")
     ts(T.CKE1[:], T.CK[:], col(7), OFF / U, OP.add, OP.add, ["CKa", "CKb", "c7"], ["CKE1"], 2 * M, "h")
     ts(T.hb[:], T.J[:, 0:16], col(1), 0.5, OP.is_equal, OP.mult, ["J", "c1"], ["hb"])
-    ag(T.BT[:, 0:1], T.hb[:, 11:12], ["hb"], ["BT"])
+    cp(T.BT[:, 0:1], T.hb[:, 11:12], ["hb"], ["BT"])
     for e in range(10):
         w0, w1 = 1 << e, min(2 << e, M * RO)
-        ac(T.BT[:, w0:w1], T.BT[:, 0:w1 - w0], ["BT", "hb"], ["BT"], AF.Identity, T.hb[:, e:e + 1], n=w1 - w0)
+        r, w = ["BT", "hb"] + ["BT8"] * (e > 8), ["BT" if e < 8 else "BT%d" % e]
+        if e < BV:
+            ts(T.BT[:, w0:w1], T.BT[:, 0:w1 - w0], T.hb[:, e:e + 1], None, OP.add, None, r, w, w1 - w0, "h")
+        else:
+            ac(T.BT[:, w0:w1], T.BT[:, 0:w1 - w0], r, w, AF.Identity, T.hb[:, e:e + 1], n=w1 - w0)
     ac(T.wr[:], T.J[:, 0:16], ["J", "thr"], ["wr"], AF.Exp, 2 * LN2, LN2)
-    for j, wj in ((12, -16384.0), (13, 4.0), (14, 2.0), (15, 0.0)):
+    for j, wj in ((12, -16384.0), (13, 4.0), (14, 0.0), (15, 0.0)):
         ms(T.wr[:, j:j + 1], wj, ["wr"])
     tt(T.wm[:], T.wr[:], T.hb[:], OP.mult, ["wr", "hb"], ["wm"])
     note("V", lambda: v.tensor_reduce(col(5), T.wm[:], AX.X, OP.add), cyc(16, ""), ["wm"], ["c5"])
@@ -301,45 +369,57 @@ def rank_program(g, core, T, topo):
             mm(P[7][:, 16:17], T.on32[:], T.cnt[:], True, ["on32", "cnt"], "P7", 256)
         to_list(P[7][:, 0:12], "Zw", T["mz%d" % t], ["mz%d" % t], "P7")
         if t > 0:
-            ts(T.ui[:, 0:12], P[7][:, 0:12], P[7][:, 16:17], 262144.0, OP.add, OP.add, ["P7"], ["ui0"])
+            ts(T.ui[:, 0:12], P[7][:, 0:12], P[7][:, 16:17], 4194304.0, OP.add, OP.add, ["P7"], ["ui0"])
         else:
             ts(T.ui[:, 0:12], P[7][:, 0:12], 262144.0, None, OP.add, None, ["P7"], ["ui0"])
         ts(T.ui[:, 12:24], T.ui[:, 0:12], KK - 1, None, OP.bitwise_and, None, ["ui0"], ["ui1"])
-        ag(T.uu[:], T.ui[:, 12:24], ["ui1"], ["uu"])
+        cp(T.uu[:], T.ui[:, 12:24], ["ui1"], ["uu"])
         ag(T.Ku[:, 0:M], T.K0[:].indirect(T.uu[:, 0:12]), ["K0", "uu"], ["Ku0"], M, "g")
         ag(T.Ku[:, M:2 * M], T.K1[:].indirect(T.uu[:, 0:12]), ["K1a", "K1b", "uu"], ["Ku1"], M, "g")
 
     cuts(0)
-    XB = ["xb0", "xb1", "xb2"]
-    XA = ["xa%d" % i0 for i0, i1, e in XS]
+    XA, XB = ["xa%d" % i0 for i0, i1, e in XS], ["xb0", "xb1", "xb2"]
     xa_keys = lambda c0, c1: ["xa%d" % i0 for i0, i1, e in XS if i0 < c1 and i1 > c0]
     LK = ["L0", "L1", "L2", "L3", "Ln"]
-    H = ((0, 128, 6), (128, 192, 5))
 
     for t in range(RO):
         last = t == RO - 1
         n0 = V + M * t
         n1 = n0 + M
         mp, mz = T["mp%d" % t], T["mz%d" % t]
-        kp, kz, sp = "mp%d" % t, "mz%d" % t, "sp%d" % t
+        kp, kz, sp, sz = "mp%d" % t, "mz%d" % t, "sp%d" % t, "sz%d" % t
         pG = mp[:, M:M + 12]
         C, E = T.CE[:, 0:M], T.CE[:, M:2 * M]
         off, offv = T.ou[:, 12:24], T.ou[:, 0:12]
         kd = KDL if last else KD
 
         if t > 0:
-            cp(T.pGf[:, 0:12], pG, [kp] + ["~L0"] * S1, ["pGf"])
+            cp(T.pGf[:, 0:12], pG, [kp, "~L0"], ["pGf"])
         for c in range(12):
             e0 = c * M
+            unit("eq", t, c // 4)
             ts(T.EQ[:, e0:e0 + M - 16 * c], mp[:, 16 * c:M], T.pGf[:, c:c + 1], T.wG[:, c:c + 1], OP.is_equal, OP.mult,
                [kp, "pGf", "wG"], ["EQ%d" % c], M - 16 * c, "h")
-            mm(P[5][:, 16 * c:M], T.Bk[:], T.EQ[:, e0:e0 + M - 16 * c], c == 0, ["Bk", "EQ%d" % c], "P5", M - 16 * c, ("eq", t, c // UE))
+            unit("eq sum", t, c // 4)
+            mm(P[5][:, 16 * c:M], T.Bk[:], T.EQ[:, e0:e0 + M - 16 * c], c == 0, ["Bk", "EQ%d" % c], "P5", M - 16 * c)
         tt(T.dup[:], P[5][:, 0:M], T.thr[:], OP.is_ge, ["P5", "thr"], ["dup"], M)
-        mm(P[7][:, 0:12], T.I32[:], T.pGf[:, 0:12], True, ["I32", "pGf"], "P7", 256)
-        to_list(P[7][:, 0:12], "Zd", T.dup, ["dup"], "P7", False)
-        ac(P[3][:, 0:M], T.dup[:], ["dup"], ["P3", "cnt"], AF.Identity, 1.0, -1.0, T.cnt[:], M)
-        tt(off, P[7][:, 0:12], T.nG[:, 12 * RO:12 * RO + 12], OP.min, ["P7", "nG"], ["ou"])
-        tt(offv, P[7][:, 0:12], T.nG[:, 12 * t:12 * t + 12], OP.max, ["P7", "nG"], ["ov"])
+        if SD:
+            tt(T.og[:, 0:12], T.nG[:, 12 * RO:12 * RO + 12], T.pGf[:, 0:12], OP.subtract, ["nG", "pGf"], ["og0"])
+            tt(T.dg[:], P[5][:, 0:M], T.thm[:], OP.is_ge, ["P5", "thm"], ["dg"], M)
+            scan(T.ds, T.dg, ["dg"], ["ds"], 0, M, "h")
+            tt(T.og[:, 12:24], T.ds[:, 15:M:16], T.og[:, 0:12], OP.mult, ["ds", "og0"], ["og1"])
+            tt(off, T.og[:, 12:24], T.pGf[:, 0:12], OP.add, ["og1", "pGf"], ["ou"])
+            ac(T.og[:, 24:36], T.pGf[:, 0:12], ["pGf"], ["og2"], AF.Identity, float(ALT))
+            tt(T.og[:, 36:48], T.ds[:, 15:M:16], T.og[:, 24:36], OP.mult, ["ds", "og2"], ["og3"])
+            tt(offv, T.og[:, 36:48], T.nG[:, 12 * t:12 * t + 12], OP.max, ["og3", "nG"], ["ov"])
+        else:
+            mm(P[7][:, 0:12], T.I32[:], T.pGf[:, 0:12], True, ["I32", "pGf"], "P7", 256)
+            to_list(P[7][:, 0:12], "Zd", T.dup, ["dup"], "P7", False)
+            tt(off, P[7][:, 0:12], T.nG[:, 12 * RO:12 * RO + 12], OP.min, ["P7", "nG"], ["ou"])
+            tt(offv, P[7][:, 0:12], T.nG[:, 12 * t:12 * t + 12], OP.max, ["P7", "nG"], ["ov"])
+        ac(P[3][:, 0:M], T.dup[:], ["dup"], ["P3"], AF.Identity, 1.0, -1.0, n=M)
+        if not last:
+            ac(T.spare[:], T.dup[:], ["dup"], ["cnt", "spare"], AF.Identity, 1.0, -1.0, T.cnt[:], M + 24)
         ag(P[1][:, 0:2 * M], T.Ku[:], ["Ku0", "Ku1"], ["P1"], 2 * M)
         ac(T.xo[:], T.X[:, 0:n0].indirect(pG), ["X", "Xn", kp], ["xo"], AF.Identity, OFF - 0.25, n=M, kind="g")
         ac(T.xp[:], T.xo[:], ["xo"], ["xp"], AF.Identity, -OFF, n=M)
@@ -347,132 +427,190 @@ def rank_program(g, core, T, topo):
         tt(E, T.xp[:], P[1][:, M:2 * M], OP.min, ["xp", "P1"], ["E"], M)
         mm(P[0][:, 0:2 * M], T.nPm[:], T.CE[:], True, ["nPm", "C", "E"], "P0", 2 * M)
         if t > 0:
-            ag(T.ab[:, 0:M], T.L[:, 0:n0].indirect(pG), LK + [kp], ["a"], M, "g")
+            (cp if AV else ag)(T.ab[:, 0:M], T.L[:, 0:n0].indirect(pG), LK + [kp], ["a"], M, "g")
         else:
             cp(T.ab[:, 0:M], T.NB[:].indirect(pG), ["NB0", "NB1", "NB2", "NB3", kp], ["a"], M, "g")
         ac(T.av[:], T.ab[:, 0:M], ["a"], ["av"], AF.Identity, -OFF, n=M)
         tt(T.X[:, n0:n1], E, P[3][:, 0:M], OP.mult, ["E", "P3"], ["Xn"], M)
-        tt(T.X[:, 0:W + M].indirect(off), C, T.BT[:, M * t:M * t + M], OP.add, ["C", "BT", "ou"] + ["~Ln"] * (S4 * (t > 0)), ["X", "Xn"], M, "s")
+        tt(T.X[:, 0:W + M].indirect(off), C, T.BT[:, M * t:M * t + M], OP.add, ["C", "BT", "ou"] + ["BT8", "BT9", "~Ln"] * (t > 0), ["X", "Xn"], M, "s")
         if not last:
-            mm(P[7][:, 0:M], T.I[:], C, True, ["I", "C"], "P7", M)
-            mm(P[7][:, 0:M], T.nI[:], mz[:], False, ["nI", kz], "P7", M)
-            mm(P[7][:, 0:M], T.nBI[:], T.dup[:], False, ["nBI", "dup"], "P7", M)
-            ac(T.zr[:], P[7][:, 0:M], ["P7"], ["zr"], AF.Relu, 511.5, n=M)
-            mm(P[4][:, 0:M], T.I[:], mz[:], True, ["I", kz], "P4", M)
-            mm(P[4][:, 0:M], T.I256[:], T.dup[:], False, ["I256", "dup"], "P4", M)
-            mm(P[4][:, 0:M], T.Ih[:], T.zr[:], False, ["Ih", "zr"], "P4", M)
-            ac(T.zy[:], P[4][:, 0:M], ["P4"], ["zy"], AF.Identity, MAGIC - 256, n=M)
-            ac(T["sz%d" % t][:], T.zy[:], ["zy"], ["sz%d" % t], AF.Identity, -MAGIC, n=M)
-            send("sz%d" % t, "mz%d" % (t + 1), "az%d" % (t + 1), n_in, ["sz%d" % t], ["mz%d" % (t + 1)], 0, M)
+            mm(P[4][:, 0:M], T.nI[:], mz[:], True, ["nI", kz], "P4", M)
+            mm(P[4][:, 0:M], T.I[:], C, False, ["I", "C"], "P4", M)
+            mm(P[4][:, 0:M], T.nBI[:], T.dup[:], False, ["nBI", "dup"], "P4", M)
+            ac(T.zr[:], P[4][:, 0:M], ["P4"], ["zr"], AF.Relu, 511.5 + (OFF if t else 0), n=M)
+            mm(P[5][:, 0:M], T.I[:], mz[:], True, ["I", kz], "P5", M)
+            mm(P[5][:, 0:M], T.I256[:], T.dup[:], False, ["I256", "dup"], "P5", M)
+            mm(P[5][:, 0:M], T.Ih[:], T.zr[:], False, ["Ih", "zr"], "P5", M)
+            ac(T[sz][:], P[5][:, 0:M], ["P5"], [sz], AF.Identity, (0 if t else OFF) - 256, n=M)
+            send(sz, "mz%d" % (t + 1), "az%d" % (t + 1), n_in, [sz], 0, M, 2.5)
             cuts(t + 1)
         ac(T.NC[:], T.ID[:, 0:ALT + n0].indirect(offv), ["ID", "ID2", "ALT", "ALT2", "ov"], ["NC"], AF.Identity, 322.75, -1.0 / 2048,
            n=M, kind="g")
         ac(T.NE[:], T.ID[:, 0:ALT].indirect(off), ["ID", "ID2", "ou"], ["NE"], AF.Identity, 130 * U, n=M, kind="g")
-        if last:
-            for j in range(NSTRIP):
-                j0, j1 = W // NSTRIP * j, W // NSTRIP * (j + 1)
-                if j0 < SV:
-                    ts(T.XR[:, j0:j1], T.X[:, j0:j1], OFF - 0.25, None, OP.add, None, ["X", "Xn"], ["XR%d" % j], j1 - j0, "h")
-                    ts(T.XO[:, j0:j1], T.XR[:, j0:j1], -OFF, None, OP.add, None, ["XR%d" % j], ["XO%d" % j], j1 - j0, "h")
-                else:
-                    ac(T.XR[:, j0:j1], T.X[:, j0:j1], ["X", "Xn"], ["XR%d" % j], AF.Identity, OFF - 0.25, n=j1 - j0)
-                    ac(T.XO[:, j0:j1], T.XR[:, j0:j1], ["XR%d" % j], ["XO%d" % j], AF.Identity, -OFF, n=j1 - j0)
-            dma("S", "dyx", T.yx[:], T.XO[:], 256 * W, ["XO%d" % j for j in range(NSTRIP)], [])
 
         for i0, i1, e in XS:
-            (cp if e == "V" else ag)(T.xab[:, 16 * i0:16 * i1], T.X[:, 0:n1].indirect(T.ab[:, i0:i1]), ["X", "Xn", "a"] + ["~av"] * (S3 * (e == "A")), ["xa%d" % i0],
+            (cp if e == "V" else ag)(T.xab[:, 16 * i0:16 * i1], T.X[:, 0:n1].indirect(T.ab[:, i0:i1]), ["X", "Xn", "a"], ["xa%d" % i0],
                                      16 * (i1 - i0), "g")
         for j, (i0, i1) in enumerate(CH):
-            kb, Pb = "P%d" % (5 + j % 2), P[5 + j % 2][:, 0:i1 - i0]
-            ts(T.xr[:, 16 * i0:16 * i1], T.xab[:, 16 * i0:16 * i1], OFF - 0.25, None, OP.add, None, xa_keys(i0, i1), ["xr%d" % j],
-               16 * (i1 - i0), "h")
+            kb, Pb, n = "P%d" % (5 + j % 2), P[5 + j % 2][:, 0:i1 - i0], i1 - i0
+            ts(T.xr[:, 16 * i0:16 * i1], T.xab[:, 16 * i0:16 * i1], OFF - 0.25, None, OP.add, None, xa_keys(i0, i1), ["xr%d" % j], 16 * n, "h")
             for k in range(16):
-                mm(Pb, sel("Zb", k), T.xab[:, 16 * i0 + k:16 * i1:16], k == 0, ["Zb"] + xa_keys(i0, i1) + ["~P%d" % (6 - j % 2)] * (S2 * (j > 0)), kb, i1 - i0,
-                   ("xt", t, j, k // UX))
+                unit("with bits", t, j)
+                mm(Pb, sel("Zb", k), T.xab[:, 16 * i0 + k:16 * i1:16], k == 0, ["Zb"] + xa_keys(i0, i1), kb, n)
             for k in range(16):
-                mm(Pb, sel("nZb", k), T.xr[:, 16 * i0 + k:16 * i1:16], False, ["nZb", "xr%d" % j], kb, i1 - i0, ("xr", t, j, k // UX))
-            tt(T.bv[:, i0:i1], Pb, T.av[:, i0:i1], OP.max, [kb, "av"], ["bv%d" % j], i1 - i0)
-            if BU == "A":
-                ac(T.ab[:, M + i0:M + i1], T.bv[:, i0:i1], ["bv%d" % j], ["b%d" % j], AF.Identity, OFF, n=i1 - i0)
-            else:
-                ts(T.ab[:, M + i0:M + i1], T.bv[:, i0:i1], OFF, None, OP.add, None, ["bv%d" % j], ["b%d" % j])
+                unit("without", t, j)
+                mm(Pb, sel("nZb", k), T.xr[:, 16 * i0 + k:16 * i1:16], False, ["nZb", "xr%d" % j], kb, n)
+            tt(T.ab[:, M + i0:M + i1], Pb, T.ab[:, i0:i1], OP.max, [kb, "a"], ["b%d" % j], n)
+            if i1 in (128, M):
+                c0 = 0 if i1 == 128 else 128
+                ts(T.bv[:, c0:i1], T.ab[:, M + c0:M + i1], -OFF, None, OP.add, None, ["b0", "b%d" % j],
+                   ["bv%d" % x for x in range(c0 // 64, j + 1)], i1 - c0, "h")
             ag(T.xab[:, 16 * (M + i0):16 * (M + i1)], T.X[:, 0:n1].indirect(T.ab[:, M + i0:M + i1]), ["X", "Xn", "b%d" % j], ["xb%d" % j],
-               16 * (i1 - i0), "g")
+               16 * n, "g")
+        if last:
+            for j, e in enumerate(STRIP):
+                j0, j1 = W // len(STRIP) * j, W // len(STRIP) * (j + 1)
+                if e == "V":
+                    ts(T.XR[:, j0:j1], T.X[:, j0:j1], OFF - 0.25, None, OP.add, None, ["X", "Xn", "~b0"], ["XR%d" % j], j1 - j0, "h")
+                    ts(T.XO[:, j0:j1], T.XR[:, j0:j1], -OFF, None, OP.add, None, ["XR%d" % j], ["XO%d" % j], j1 - j0, "h")
+                else:
+                    ac(T.XR[:, j0:j1], T.X[:, j0:j1], ["X", "Xn", "~b0"], ["XR%d" % j], AF.Identity, OFF - 0.25, n=j1 - j0)
+                    ac(T.XO[:, j0:j1], T.XR[:, j0:j1], ["XR%d" % j], ["XO%d" % j], AF.Identity, -OFF, n=j1 - j0)
+            dma("S", "dyx", T.yx[:], T.XO[:], 256 * W, ["XO%d" % j for j in range(len(STRIP))], ["yx"])
 
         mm(P[1][:, 0:M], T.nIc[:], T.av[:], True, ["nIc", "av"], "P1", M)
         for i0, i1 in CA:
             for k in range(16):
                 o, key = 2 * M * k, "cCa%d_%d" % (k, i0)
+                unit("a", t, i0, k // (4 if i0 else 2))
                 tt(T.cC[:, o + i0:o + i1], T.xab[:, 16 * i0 + k:16 * i1:16], P[0][:, i0:i1], OP.is_ge, xa_keys(i0, i1) + ["P0"], [key], i1 - i0)
-                mm(P[1][:, i0:i1], sel("Zc", k), T.cC[:, o + i0:o + i1], False, ["Zc", key], "P1", i1 - i0, ("ca", t, i0, k // UA))
+                if AM and i0 == 0:
+                    continue
+                unit("a sum", t, i0, k // 4)
+                c0 = 0 if AM else i0
+                mm(P[1][:, c0:i1], sel("Zc", k), T.cC[:, o + c0:o + i1], False, ["Zc", key, "cCa%d_0" % k], "P1", i1 - c0)
         tt(T.k1[:], P[1][:, 0:M], T.NC[:], OP.max, ["P1", "NC"], ["k1"], M)
         for i0, i1, b in H:
             mm(P[b][:, i0:i1], T.nIc[:], T.bv[:, i0:i1], True, ["nIc"] + (["bv0", "bv1"] if i0 == 0 else ["bv2"]), "P%d" % b, i1 - i0)
         for j, (i0, i1) in enumerate(CH):
-            b = H[j // 2][2]
+            h = int(i0 >= H[1][0])
+            b = H[h][2]
             for k in range(16):
                 o, key = 2 * M * k + M, "cCb%d_%d" % (j, k)
-                tt(T.cC[:, o + i0:o + i1], T.xab[:, 16 * (M + i0) + k:16 * (M + i1):16], P[0][:, i0:i1], OP.is_ge, ["xb%d" % j, "P0"], [key])
-                mm(P[b][:, i0:i1], sel("Zc", k), T.cC[:, o + i0:o + i1], False, ["Zc", key], "P%d" % b, i1 - i0,
-                   ("cb", t, j, k // (UL if j == 2 else UB)))
+                unit("b", t, j, k // (2 if i1 == M else 4))
+                tt(T.cC[:, o + i0:o + i1], T.xab[:, 16 * (M + i0) + k:16 * (M + i1):16], P[0][:, i0:i1], OP.is_ge, ["xb%d" % j, "P0"], [key], i1 - i0)
+                if BM and i1 != H[h][1]:
+                    continue
+                unit("b sum", t, j, k // (2 if i1 == M else 4))
+                c0 = H[h][0] if BM else i0
+                mm(P[b][:, c0:i1], sel("Zc", k), T.cC[:, o + c0:o + i1], False,
+                   ["Zc"] + ["cCb%d_%d" % (x, k) for x in range(j + 1) if CH[x][0] >= c0], "P%d" % b, i1 - c0)
         for h, (i0, i1, b) in enumerate(H):
             kb, Pb, n = "P%d" % b, P[b][:, i0:i1], i1 - i0
+            kw, Pw = "P%d" % (7 - h), P[7 - h][:, 256 + i0:256 + i1]
             tt(Pb, Pb, T.k1[:, i0:i1], OP.max, [kb, "k1"], [kb], n)
             if not last:
                 ac(T.vv[:, i0:i1], Pb, [kb], ["vv%d" % h], AF.Exp, -200 * LN2, LN2 / 2, n=n)
-            ag(T.rC[:, i0:i1], Pb, [kb], ["rC%d" % h], n)
+                mm(Pw, T.TT[:], T.vv[:, i0:i1], True, ["TT", "vv%d" % h], kw, n)
+            if RV > 1 - h:
+                ts(T.rC[:, i0:i1], Pb, 25165824.0, 25165824.0, OP.add, OP.subtract, [kb], ["rC%d" % h], n)
+            else:
+                ag(T.rC[:, i0:i1], Pb, [kb], ["rC%d" % h], n)
             tt(T.ec[:, i0:i1], Pb, T.rC[:, i0:i1], OP.subtract, [kb, "rC%d" % h], ["ec%d" % h], n)
             if not last:
-                kw, Pw = "P%d" % (7 - h), P[7 - h][:, 256 + i0:256 + i1]
-                mm(Pw, T.TT[:], T.vv[:, i0:i1], True, ["TT", "vv%d" % h], kw, n)
-                ac(Pw, Pw, [kw], [kw], AF.Sign, 0.0, -1.0, n=n)
-                tt(T.mk[:, i0:i1], Pw, T.ec[:, i0:i1], OP.min, [kw, "ec%d" % h], ["mk%d" % h], n)
+                if WV:
+                    ts(Pw, Pw, 0.0, 2.0, OP.is_lt, OP.mult, [kw], [kw], n)
+                else:
+                    ac(Pw, Pw, [kw], [kw], AF.Sign, 0.0, -1.0, n=n)
+                tt(T.mk[:, i0:i1], Pw, T.ec[:, i0:i1], OP.mult if WV else OP.min, [kw, "ec%d" % h], ["mk%d" % h], n)
                 mm(P[7][:, i0:i1], T.Bk[:], T.mk[:, i0:i1], True, ["Bk", "mk%d" % h], "P7", n)
-                if h == 1:
-                    to_list(P[7][:, M:M + 12], "Z1", T.mk, ["mk0", "mk1"], "P7")
-                    i1 = M + 12
-                ac(T[sp][:, i0:i1], P[7][:, i0:i1], ["P7"], [sp + "_%d" % h], AF.Identity, OFF - 15 * 2048, -2048.0, n=i1 - i0)
-                send(sp, "mp%d" % (t + 1), "ap%d" % (t + 1), 2 * n_in, [sp + "_%d" % h], ["mp%d" % (t + 1)], i0, i1, h == 1)
+                if SK:
+                    tt(T.pm[:, i0:i1], P[7][:, i0:i1], T.mask[:, i0:i1], OP.mult, ["P7", "mask"], ["pm%d" % h], n)
+                    scan(T.pn, T.pm, ["pm%d" % h], ["pn%d" % h], i0, i1, "")
+                    ac(T[sp][:, i0:i1], P[7][:, i0:i1], ["P7"], [sp + "_%d" % h], AF.Identity, OFF - 15 * 2048, -2048.0, n=i1 - i0)
+                    if h == 1:
+                        ac(T[sp][:, M:M + 12], T.pn[:, 15:M:16], ["pn0", "pn1"], [sp + "g"], AF.Identity, OFF - 15 * 2048, -2048.0)
+                        i1 = M + 12
+                else:
+                    if h == 1:
+                        to_list(P[7][:, M:M + 12], "Z1", T.mk, ["mk0", "mk1"], "P7")
+                        i1 = M + 12
+                    mul, add = (-1024.0, OFF) if WV else (-2048.0, OFF - 15 * 2048)
+                    if SV > 1 - h:
+                        ts(T[sp][:, i0:i1], P[7][:, i0:i1], mul, add, OP.mult, OP.add, ["P7"], [sp + "_%d" % h], i1 - i0)
+                    else:
+                        ac(T[sp][:, i0:i1], P[7][:, i0:i1], ["P7"], [sp + "_%d" % h], AF.Identity, add, mul, n=i1 - i0)
+                if not ONE:
+                    send(sp, "mp%d" % (t + 1), "ap%d" % (t + 1), 2 * n_in, [sp + "_%d" % h] + [sp + "g"] * h, i0, i1, 0.0, h == 1)
+                elif h == 1:
+                    send(sp, "mp%d" % (t + 1), "ap%d" % (t + 1), n_in, [sp + "_0", sp + "_1", sp + "g"], 0, i1)
         ts(T.L[:, 0:W + M].indirect(off), T.ec[:], -2048.0, OFF, OP.mult, OP.add, ["ec0", "ec1", "ou"], LK, M, "s")
         if last:
-            dma("S", "dyn0", T.yn[:, 0:n0], T.L[:, 0:n0], 512 * n0, LK[:4], [])
+            dma("S", "dyn0", T.yn[:, 0:n0], T.L[:, 0:n0], 512 * n0, LK[:4] + ["~yx"] * YF, [])
 
         PE, KE = (P[2][:, 0:M], P[EB][:, M:2 * M]), ("P2", "P%d" % EB)
-        for s, val, keys in ((0, T.av, ["av"]), (1, T.bv, ["bv0", "bv1", "bv2"])):
-            mm(PE[s], T.IU[:], T["CKE1" if last else "CKE0"][:, M * s:M * s + M], EB != 2 or s == 0, ["IU", "CKE0", "CKE1"], KE[s], M)
+        ck = T["CKE1" if last else "CKE0"]
+        if EB == 2:
+            mm(P[2][:, 0:2 * M], T.IU[:], ck[:], True, ["IU", "CKE0", "CKE1"], "P2", 2 * M)
+        for s, val, keys in ((0, T.av, ["av"]), (1, T.bv, ["bv%d" % j for j in range(len(CH))])):
+            if EB != 2:
+                mm(PE[s], T.IU[:], ck[:, M * s:M * s + M], True, ["IU", "CKE0", "CKE1"], KE[s], M)
             mm(PE[s], T.I[:], val[:], False, ["I"] + keys, KE[s], M)
-        halves = [(k, 0) for k in range(kd, kd + 2 * NPRE)] + [(k, 1) for k in range(kd, kd + 2 * NPRE)]
-        halves += [(k, h) for k in range(kd + 2 * NPRE, 16) for h in (0, 1)]
+
+        def e_sum(Z, pair, o, keys):
+            if EB == 2 and pair[0][0] == pair[1][0]:
+                mm(P[2][:, 0:2 * M], sel(Z, pair[0][0]), T.cE[:, o:o + 2 * M], False, [Z] + keys, "P2", 2 * M)
+            else:
+                for h, (k, s) in enumerate(pair):
+                    mm(PE[s], sel(Z, k), T.cE[:, o + M * h:o + M * h + M], False, [Z] + keys[h % len(keys):h % len(keys) + 1], KE[s], M)
+
+        halves = [(k, s) for s in (0, 1) for k in range(kd, kd + 2 * NPRE)] + [(k, s) for k in range(kd + 2 * NPRE, 16) for s in (0, 1)]
         for u in range(len(halves) // 2):
-            kb, o = "P%d" % (3 + u % 2), 2 * M * (kd + u)
-            for h, (k, s) in enumerate(halves[2 * u:2 * u + 2]):
-                Pb = P[3 + u % 2][:, M * h:M * h + M]
-                mm(Pb, T.Pm[:], E, True, ["Pm", "E"], kb, M, ("st", t, u, h))
-                mm(Pb, T.I[:], T.xab[:, 16 * M * s + k:16 * M * (s + 1):16], False, ["I"] + (XB if s else XA), kb, M, ("st", t, u, h))
-            ac(T.cE[:, o:o + 2 * M], P[3 + u % 2][:, 0:2 * M], [kb], ["cEs%d" % u], AF.Sign, 0.25, n=2 * M)
-            for h, (k, s) in enumerate(halves[2 * u:2 * u + 2]):
-                mm(PE[s], sel("Z8", k), T.cE[:, o + M * h:o + M * h + M], False, ["Z8", "cEs%d" % u], KE[s], M)
+            kb, o, pair, Pb = "P%d" % (3 + u % 2), 2 * M * (kd + u), halves[2 * u:2 * u + 2], P[3 + u % 2]
+            whole = pair[0][0] == pair[1][0]
+            if whole:
+                unit("lay", t, u)
+                mm(Pb[:, 0:2 * M], T.I[:], T.xab[:, pair[0][0]:32 * M:16], True, ["I"] + XA + XB, kb, 2 * M)
+            for h, (k, s) in enumerate(pair):
+                unit("lay", t, u)
+                mm(Pb[:, M * h:M * h + M], T.Pm[:], E, not whole, ["Pm", "E"], kb, M)
+                if not whole:
+                    unit("lay", t, u)
+                    mm(Pb[:, M * h:M * h + M], T.I[:], T.xab[:, 16 * M * s + k:16 * M * (s + 1):16], False, ["I"] + (XB if s else XA), kb, M)
+            ac(T.cE[:, o:o + 2 * M], Pb[:, 0:2 * M], [kb], ["cEs%d" % u], AF.Sign, 0.25, n=2 * M)
+            e_sum("Z8", pair, o, ["cEs%d" % u])
         for k in range(kd):
             for s in (0, 1):
                 o, key = 2 * M * k + M * s, "cE%d_%d" % (k, s)
                 tt(T.cE[:, o:o + M], T.xab[:, 16 * M * s + k:16 * M * (s + 1):16], P[0][:, M:2 * M], OP.is_ge, (XB if s else XA) + ["P0"], [key], M)
-                mm(PE[s], sel("Z16", k), T.cE[:, o:o + M], False, ["Z16", key], KE[s], M)
-        tt(T.k2[:], P[2][:, 0:M], T.NE[:], OP.max, ["P2", "NE"], ["k2"], M)
+            e_sum("Z16", ((k, 0), (k, 1)), 2 * M * k, ["cE%d_0" % k, "cE%d_1" % k])
+        tt(T.k2[:], PE[0], T.NE[:], OP.max, [KE[0], "NE"], ["k2"], M)
         tt(PE[1], PE[1], T.k2[:], OP.max, [KE[1], "k2"], [KE[1]], M)
-        ac(T.rE[:], PE[1], [KE[1]], ["rE"], AF.Identity, -OFF, n=M)
+        if EV:
+            ts(T.rE[:], PE[1], -OFF, None, OP.add, None, [KE[1]], ["rE"], M)
+        else:
+            ac(T.rE[:], PE[1], [KE[1]], ["rE"], AF.Identity, -OFF, n=M)
         tt(T.L[:, n0:n1], PE[1], T.rE[:], OP.subtract, [KE[1], "rE"], ["Ln"], M)
         if last:
             dma("A", "dyn1", T.yn[:, n0:n1], T.L[:, n0:n1], 512 * M, ["Ln"], [])
 
-    gap = lambda i, j: HOP if calls[i][0] != calls[j][0] or calls[j][5] else (0.0 if calls[i][0] == "P" or not calls[i][4][j] else OWN)
-    members = {}
-    for i in range(len(calls)):
-        members.setdefault(units.get(i) or i, []).append(i)
-    members = sorted(members.values(), key=lambda m: m[-1])
-    node = {i: q for q, m in enumerate(members) for i in m}
-    order = schedule([calls[m[0]][0] for m in members], [sum(calls[i][2] for i in m) for m in members], [calls[m[0]][3] for m in members],
-                     [list({node[j]: gap(i, j) for i in m for j in calls[i][4] if node[j] != q}.items()) for q, m in enumerate(members)])
-    order = [i for q in order for i in members[q]]
+    if not PLAN:
+        members = {}
+        for i in range(len(calls)):
+            members.setdefault(units.get(i, i), []).append(i)
+        members = sorted(members.values(), key=lambda m: m[-1])
+        node = {i: x for x, m in enumerate(members) for i in m}
+
+        def gap(i, j, q):
+            if calls[i][0] != calls[j][0] or calls[j][5]:
+                return q["hop"] + (calls[j][3](q) if calls[i][4][j] else 0.0)
+            return q["own"] if calls[i][0] != "P" and calls[i][4][j] else 0.0
+
+        guesses = [([sum(calls[i][2](q) for i in m) for m in members], [calls[m[0]][3](q) for m in members],
+                    [list({node[j]: gap(i, j, q) for i in m for j in calls[i][4] if node[j] != x}.items()) for x, m in enumerate(members)])
+                   for q in GUESS]
+        PLAN["order"] = [i for x in schedule([calls[m[0]][0] for m in members], guesses) for i in members[x]]
+    order = PLAN["order"]
     closes = {calls[i][6]: i for i in order if calls[i][6] is not None}
     count = {"sV": 0, "sA": 0, "sP": 0, "sG": 0}
     seen = {e: {} for e in Q}
@@ -509,7 +647,7 @@ def rank_program(g, core, T, topo):
             clock[ev] = dict(seen[e])
         event[i] = ev
 
-    g.wait_ge(T.sem["sent"], 3 * (RO - 1) * n_eng)
+    g.wait_ge(T.sem["sent"], (3 - ONE) * (RO - 1) * n_eng)
     for s in ("sV", "sA", "sP", "sG"):
         need("G", (s, count[s]))
     for s in ("dyx", "dyn0", "dyn1"):

@@ -9,18 +9,18 @@ OFF = 1536.0
 TOP = -103 * 4096
 BIG = 2097152.0
 LN2 = math.log(2.0)
-KD = 11
-KDL = 10
-NPRE = 1
+KD = 13
+KDL = 11
+NPRE = 0
 CH = ((0, 64), (64, 128), (128, 192))
 XS = ((0, 64, "V"), (64, 128, "A"), (128, 192, "A"))
 CA = ((0, 128), (128, 192))
 H = ((0, 128, 6), (128, 192, 5))
-STRIP = ("V", "V", "V", "A")
+STRIP = ("V", "V", "A", "A")
 NBP = 1
 LV = 0
 BV = 5
-YF = 1
+YF = 0
 EB = 6
 BM = 0
 SD = 0
@@ -28,14 +28,15 @@ SK = 0
 AM = 0
 ONE = 0
 WV = 2
-SV = 0
+SV = 1
 RV = 1
 EV = 0
 AV = 0
 CYC = 0.83e-3
-GUESS = ({"pe": 0.45e-3, "mm": 0.0, "act": 0.1, "gather": 1.4, "scatter": 3.8, "hop": 0.14, "own": 0.07, "far": 2.3, "dma": 1.8, "bw": 200e3},
-         {"pe": 0.43e-3, "mm": 0.0, "act": 0.1, "gather": 1.6, "scatter": 4.2, "hop": 0.11, "own": 0.1, "far": 1.6, "dma": 1.0, "bw": 400e3})
-MOVES = 30000
+GUESS = ({"pe": 0.52e-3, "mm": 0.0, "act": 0.1, "gather": 1.56, "scatter": 3.8, "hop": 0.16, "own": 0.08, "far": 2.7, "dma": 1.2, "bw": 350e3},
+         {"pe": 0.45e-3, "mm": 0.0, "act": 0.12, "gather": 1.4, "scatter": 3.5, "hop": 0.13, "own": 0.09, "far": 1.9, "dma": 0.9, "bw": 550e3},
+         {"pe": 0.5e-3, "mm": 0.0, "act": 0.12, "gather": 1.9, "scatter": 5.0, "hop": 0.11, "own": 0.06, "far": 1.6, "dma": 0.9, "bw": 400e3})
+MOVES = 50000
 SEED = 1
 
 SCRATCH = {
@@ -43,13 +44,13 @@ SCRATCH = {
     "XR": ("sbuf", [128, W], "float16"), "XO": ("sbuf", [128, W], "bfloat16"), "BT": ("sbuf", [128, M * RO], "bfloat16"),
     "ID": ("sbuf", [128, ALT + W - M], "float32"), "NB": ("sbuf", [128, V], "int32"),
     "K0": ("sbuf", [128, KK], "bfloat16"), "K1": ("sbuf", [128, KK], "bfloat16"),
-    "psi": ("sbuf", [128, 12], "int32"), "wti": ("sbuf", [128, 1], "int32"), "wf": ("sbuf", [128, 1], "float32"),
-    "J": ("sbuf", [128, M], "bfloat16"), "Jg": ("sbuf", [128, 128], "bfloat16"), "J16": ("sbuf", [128, M], "float32"),
+    "psi": ("sbuf", [128, 12], "int32"), "wti": ("sbuf", [128, 1], "int32"), "wf": ("sbuf", [128, 1], "bfloat16"),
+    "J": ("sbuf", [128, M], "bfloat16"), "Jg": ("sbuf", [128, 128], "bfloat16"), "J16": ("sbuf", [128, M], "bfloat16"),
     "pc": ("sbuf", [128, 2], "int32"), "ci": ("sbuf", [128, 4], "int32"),
-    "cf": ("sbuf", [128, 12], "float32"), "cG": ("sbuf", [128, 12], "int32"), "cGu": ("sbuf", [128, 12], "uint16"),
-    "nG": ("sbuf", [128, 12 * (RO + 1)], "float32"), "mask": ("sbuf", [128, M], "float32"), "thr": ("sbuf", [128, M], "float32"),
-    "gx": ("sbuf", [128, M], "float16"), "wG": ("sbuf", [128, 12], "float32"),
-    "hb": ("sbuf", [128, 16], "float32"), "wr": ("sbuf", [128, 16], "bfloat16"), "wm": ("sbuf", [128, 16], "float32"),
+    "cf": ("sbuf", [128, 12], "bfloat16"), "c5": ("sbuf", [128, 1], "float32"), "cG": ("sbuf", [128, 12], "int32"), "cGu": ("sbuf", [128, 12], "uint16"),
+    "nG": ("sbuf", [128, 12 * (RO + 1)], "float32"), "mask": ("sbuf", [128, M], "bfloat16"), "thr": ("sbuf", [128, M], "float32"),
+    "gx": ("sbuf", [128, M], "float16"), "pu": ("sbuf", [128, 12], "uint16"), "c15": ("sbuf", [128, 12], "bfloat16"),
+    "hb": ("sbuf", [128, 16], "bfloat16"), "wr": ("sbuf", [128, 16], "bfloat16"), "wm": ("sbuf", [128, 16], "float32"),
     "on32": ("sbuf", [128, 128], "float32"), "I32": ("sbuf", [128, 128], "float32"), "CK": ("sbuf", [128, 2 * M], "bfloat16"),
     "CKE0": ("sbuf", [128, 2 * M], "float16"), "CKE1": ("sbuf", [128, 2 * M], "float16"),
     "pGf": ("sbuf", [128, 16], "float32"), "EQ": ("sbuf", [128, 12 * M], "bfloat16"),
@@ -68,20 +69,20 @@ SCRATCH = {
     "rC": ("sbuf", [128, M], "bfloat16"), "rE": ("sbuf", [128, M], "bfloat16"), "vv": ("sbuf", [128, M], "bfloat16"),
     "ec": ("sbuf", [128, M], "float32"), "mk": ("sbuf", [128, M], "float16"),
 }
-for _n in ("I", "nI", "Ih", "I256", "IU", "nBI", "nIc", "Pm", "nPm", "Bk", "TT", "t1", "t2"):
+for _n in ("I", "nI", "Ih", "I256", "IU", "nBI", "nIc", "Pm", "nPm", "Bk", "Bw", "TT", "t1", "t2"):
     SCRATCH[_n] = ("sbuf", [128, 128], "bfloat16")
 for _n in ("Z1", "Z16", "Z8", "Zc", "Zd", "Zw", "Zb", "nZb"):
     SCRATCH[_n] = ("sbuf", [128, 144], "bfloat16")
 for _t in range(RO):
-    SCRATCH["mp%d" % _t] = ("sbuf", [128, M + 12], "uint16")
+    SCRATCH["mp%d" % _t] = ("sbuf", [128, M + 12], "float16")
     SCRATCH["mz%d" % _t] = ("sbuf", [128, M], "float16" if _t else "bfloat16")
 for _t in range(RO - 1):
-    SCRATCH["sp%d" % _t] = ("sbuf", [128, M + 12], "uint16")
+    SCRATCH["sp%d" % _t] = ("sbuf", [128, M + 12], "float16")
     SCRATCH["sz%d" % _t] = ("sbuf", [128, M], "float16")
 for _b in range(8):
     SCRATCH["P%d" % _b] = ("psum", [128, 512], "float32")
 
-DMAS = ["dps", "dwt", "dzi", "dkc", "dxc", "dyx", "dyn0", "dyn1"] + ["dnb%d" % _j for _j in range(NBP)]
+DMAS = ["dps", "dwt", "dzi", "dkc", "dxc", "dyx0", "dyx1", "dyn0", "dyn1"] + ["dnb%d" % _j for _j in range(NBP)]
 SEMAPHORES = ["sV", "sA", "sP", "sG", "sent"] + DMAS + ["ap%d" % t for t in range(1, RO)] + ["az%d" % t for t in range(1, RO)]
 PLAN = {}
 
@@ -107,20 +108,18 @@ def first_plan(queue, busy, tail, edges):
     return sorted(range(n), key=lambda i: (start[i], i))
 
 
-def replay(order, queue, busy, tail, edges):
-    end, why, free, ahead = [0.0] * len(order), [-1] * len(order), {}, {}
-    top, last = 0.0, -1
-    for i in order:
-        q = queue[i]
-        t, w = free.get(q, 0.0), ahead.get(q, -1)
+def replay(order, lo, known, ends, queue, busy, tail, edges):
+    end, why = list(known[2]), list(known[3])
+    ahead = {queue[i]: i for i in order[:lo]}
+    for i in order[lo:]:
+        w = ahead.get(queue[i], -1)
+        t = end[w] if w >= 0 else 0.0
         for j, gap in edges[i]:
             if end[j] + gap > t:
                 t, w = end[j] + gap, j
-        end[i] = free[q] = t = t + busy[i]
-        ahead[q], why[i] = i, w
-        if t + tail[i] > top:
-            top, last = t + tail[i], i
-    return top, why, last
+        end[i], why[i], ahead[queue[i]] = t + busy[i], w, i
+    last = max(ends, key=lambda i: end[i] + tail[i])
+    return end[last] + tail[last], last, end, why
 
 
 def schedule(queue, guesses):
@@ -137,11 +136,12 @@ def schedule(queue, guesses):
         return (state[0] >> 8) % k
 
     order = first_plan(queue, *guesses[0])
-    runs = [replay(order, queue, *q) for q in guesses]
+    ends = [i for i in range(n) if not behind[i]]
+    runs = [replay(order, 0, (0, 0, [0.0] * n, [-1] * n), ends, queue, *q) for q in guesses]
     best = (sum(r[0] for r in runs), order)
     now = best[0]
     for move in range(MOVES):
-        top, why, i = runs[draw(len(runs))]
+        top, i, end, why = runs[draw(len(runs))]
         pairs = []
         while i >= 0:
             j = why[i]
@@ -166,7 +166,7 @@ def schedule(queue, guesses):
         if order[lo if ahead else hi] in moved:
             continue
         new = order[:lo] + [x for x in part if (x in moved) == ahead] + [x for x in part if (x in moved) != ahead] + order[hi + 1:]
-        tried = [replay(new, queue, *q) for q in guesses]
+        tried = [replay(new, lo, r, ends, queue, *q) for r, q in zip(runs, guesses)]
         length = sum(r[0] for r in tried)
         if length < now + 0.002 * draw(100) * (1 - move / MOVES):
             now, order, runs = length, new, tried
@@ -313,23 +313,25 @@ def rank_program(g, core, T, topo):
     ts(col(6), col(1), KD - 0.5, 128.0, OP.is_ge, OP.mult, ["c1"], ["c6"])
     ts(col(7), col(1), KDL - 0.5, 128.0, OP.is_ge, OP.mult, ["c1"], ["c7"])
     for name, c, wgt in (("I", 0, 1.0), ("nI", 0, -1.0), ("Ih", 0, 0.5), ("I256", 0, 256.0), ("IU", 0, U), ("nBI", 0, -BIG),
-                         ("nIc", 0, -1.0 / 2048), ("t2", 0, -1024.0), ("I32", 0, 1.0), ("Pm", 4, 1.0), ("nPm", 4, -1.0)):
-        ts(T[name][:], J128, col(c), wgt, OP.is_equal, OP.mult, ["J", "c%d" % c], [name], 128, "" if name == "I32" else "h")
+                         ("nIc", 0, -1.0 / 2048), ("t2", 0, -1024.0), ("Pm", 4, 1.0), ("nPm", 4, -1.0)):
+        ts(T[name][:], J128, col(c), wgt, OP.is_equal, OP.mult, ["J", "c%d" % c], [name], 128, "h")
     for name, wgt in (("Z1", 1.0), ("Zd", ALT / 16.0), ("Z16", 16 * U), ("Z8", 8 * U), ("Zc", 32.0)):
         ts(T[name][:], J144, col(3), wgt, OP.is_equal, OP.mult, ["J", "c3"], [name], 144, "h")
     ts(T.Bk[:], T.Jg[:], col(2), None, OP.is_equal, None, ["Jg", "c2"], ["Bk"])
-    ts(T.mask[:], T.J16[:], col(1), None, OP.is_equal, None, ["J16", "c1"], ["mask"], M)
+    ts(T.mask[:], T.J16[:], col(1), None, OP.is_equal, None, ["J16", "c1"], ["mask"], M, "h")
     ac(T.thr[:], T.J[:], ["J"], ["thr"], AF.Exp, 96 * LN2 + math.log(1.25), -LN2, n=1800)
     ts(T.nG[:], T.nG[:], col(2), None, OP.subtract, None, ["nG", "c2"], ["nG"], 72)
-    ts(T.wG[:], T.nG[:, 0:12], -float(V), None, OP.add, None, ["nG"], ["wG"])
-    ac(T.wG[:], T.wG[:], ["wG", "thr"], ["wG"], AF.Exp, 95 * LN2, -LN2)
+    ms(T.c15[:], OFF, ["c15"])
+    ac(col(9), col(1), ["c1", "thr"], ["c9"], AF.Exp, 0.0, -LN2)
+    ts(T.Bw[:], T.Jg[:], col(2), col(9), OP.is_equal, OP.mult, ["Jg", "c2", "c9"], ["Bw"])
     if SD:
         ts(T.thm[:], T.mask[:], -1e29, 1e29, OP.mult, OP.add, ["mask"], ["thm"], M)
         tt(T.thm[:], T.thm[:], T.thr[:], OP.max, ["thm", "thr"], ["thm"], M, "d")
     ts(T.t1[:], J128, col(0), 65536.0, OP.is_gt, OP.mult, ["J", "c0"], ["t1"])
-    tt(T.t1[:], T.t1[:], T.Bk[:], OP.mult, ["t1", "Bk"], ["t1"], 128, "d")
-    tt(T.t2[:], T.t2[:], T.Bk[:], OP.add, ["t2", "Bk"], ["t2"], 128, "d")
-    tt(T.TT[:], T.t1[:], T.t2[:], OP.add, ["t1", "t2"], ["TT"], 128, "d")
+    mm(P[3][:, 0:128], T.I[:], T.t1[:], True, ["I", "t1"], "P3", 128)
+    mm(P[3][:, 0:128], T.I[:], T.Bk[:], False, ["I", "Bk"], "P3", 128)
+    mm(P[3][:, 0:128], T.I[:], T.t2[:], False, ["I", "t2"], "P3", 128)
+    tt(T.TT[:], P[3][:, 0:128], T.Bk[:], OP.mult, ["P3", "Bk"], ["TT"], 128)
     ac(T.on32[:], T.I[:], ["I"], ["on32"], AF.Identity, 1.0 / 16, 0.0, n=128)
     ms(T.CK[:, 0:M], -31.0, ["CKa"], M)
     ms(T.CK[:, M:2 * M], -32.0, ["CKb"], M)
@@ -348,7 +350,8 @@ def rank_program(g, core, T, topo):
     for j, wj in ((12, -16384.0), (13, 4.0), (14, 0.0), (15, 0.0)):
         ms(T.wr[:, j:j + 1], wj, ["wr"])
     tt(T.wm[:], T.wr[:], T.hb[:], OP.mult, ["wr", "hb"], ["wm"])
-    note("V", lambda: v.tensor_reduce(col(5), T.wm[:], AX.X, OP.add), cyc(16, ""), ["wm"], ["c5"])
+    note("V", lambda: v.tensor_reduce(T.c5[:], T.wm[:], AX.X, OP.add), cyc(16, ""), ["wm"], ["c5f"])
+    cp(col(5), T.c5[:], ["c5f"], ["c5"])
     ts(T.Zb[:], J144, col(3), col(5), OP.is_equal, OP.mult, ["J", "c3", "c5"], ["Zb"], 144, "h")
     ts(T.nZb[:], T.Zb[:], -1.0, None, OP.mult, None, ["Zb"], ["nZb"], 144, "h")
     ag(T.K1[:, 0:KK:2], T.K0[:, 1:KK:2], ["K0"], ["K1a"], 256)
@@ -356,9 +359,9 @@ def rank_program(g, core, T, topo):
     cp(T.wf[:], T.wti[:], ["wti"], ["wf"])
     ts(T.Zw[:], J144, col(3), T.wf[:], OP.is_equal, OP.mult, ["J", "c3", "wf"], ["Zw"], 144, "h")
     cp(T.cGu[:], T.cG[:], ["cG"], ["cGu"])
-    cp(T.pGf[:, 0:12], T.psi[:], ["psi"], ["pGf"])
+    ts(T.pGf[:, 0:12], T.psi[:], -OFF, None, OP.add, None, ["psi"], ["pGf"])
     tt(T.gx[:], T.pGf[:, 0:12].indirect(T.cGu[:, 0:12]), T.mask[:], OP.mult, ["pGf", "cGu", "mask"], ["gx"], M, "g")
-    cp(T.mp0[:, M:M + 12], T.psi[:], ["psi"], ["mp0g"])
+    ts(T.mp0[:, M:M + 12], T.psi[:], -OFF, None, OP.add, None, ["psi"], ["mp0g"])
     mm(P[6][:, 0:M], T.Bk[:], T.gx[:], True, ["Bk", "gx"], "P6", M)
     cp(T.mp0[:, 0:M], P[6][:, 0:M], ["P6", "mp0g"], ["mp0"], M)
     for j in range(4):
@@ -388,20 +391,19 @@ def rank_program(g, core, T, topo):
         n1 = n0 + M
         mp, mz = T["mp%d" % t], T["mz%d" % t]
         kp, kz, sp, sz = "mp%d" % t, "mz%d" % t, "sp%d" % t, "sz%d" % t
-        pG = mp[:, M:M + 12]
+        pG = T.pu[:, 0:12]
         C, E = T.CE[:, 0:M], T.CE[:, M:2 * M]
         off, offv = T.ou[:, 12:24], T.ou[:, 0:12]
         kd = KDL if last else KD
 
-        if t > 0:
-            cp(T.pGf[:, 0:12], pG, [kp, "~L0"], ["pGf"])
+        ac(pG, mp[:, M:M + 12], [kp], ["pu"], AF.Identity, OFF)
         for c in range(12):
             e0 = c * M
             unit("eq", t, c // 4)
-            ts(T.EQ[:, e0:e0 + M - 16 * c], mp[:, 16 * c:M], T.pGf[:, c:c + 1], T.wG[:, c:c + 1], OP.is_equal, OP.mult,
-               [kp, "pGf", "wG"], ["EQ%d" % c], M - 16 * c, "h")
+            ts(T.EQ[:, e0:e0 + M - 16 * c], mp[:, 16 * c:M], mp[:, M + c:M + c + 1], 2.0 ** (95 - 16 * c), OP.is_equal, OP.mult,
+               [kp] + ["~L0"] * (t > 0), ["EQ%d" % c], M - 16 * c, "h")
             unit("eq sum", t, c // 4)
-            mm(P[5][:, 16 * c:M], T.Bk[:], T.EQ[:, e0:e0 + M - 16 * c], c == 0, ["Bk", "EQ%d" % c], "P5", M - 16 * c)
+            mm(P[5][:, 16 * c:M], T.Bw[:], T.EQ[:, e0:e0 + M - 16 * c], c == 0, ["Bw", "EQ%d" % c], "P5", M - 16 * c)
         tt(T.dup[:], P[5][:, 0:M], T.thr[:], OP.is_ge, ["P5", "thr"], ["dup"], M)
         if SD:
             tt(T.og[:, 0:12], T.nG[:, 12 * RO:12 * RO + 12], T.pGf[:, 0:12], OP.subtract, ["nG", "pGf"], ["og0"])
@@ -413,7 +415,8 @@ def rank_program(g, core, T, topo):
             tt(T.og[:, 36:48], T.ds[:, 15:M:16], T.og[:, 24:36], OP.mult, ["ds", "og2"], ["og3"])
             tt(offv, T.og[:, 36:48], T.nG[:, 12 * t:12 * t + 12], OP.max, ["og3", "nG"], ["ov"])
         else:
-            mm(P[7][:, 0:12], T.I32[:], T.pGf[:, 0:12], True, ["I32", "pGf"], "P7", 256)
+            mm(P[7][:, 0:12], T.I[:], T.c15[:], True, ["I", "c15"], "P7", 12)
+            mm(P[7][:, 0:12], T.I[:], mp[:, M:M + 12], False, ["I", kp], "P7", 12)
             to_list(P[7][:, 0:12], "Zd", T.dup, ["dup"], "P7", False)
             tt(off, P[7][:, 0:12], T.nG[:, 12 * RO:12 * RO + 12], OP.min, ["P7", "nG"], ["ou"])
             tt(offv, P[7][:, 0:12], T.nG[:, 12 * t:12 * t + 12], OP.max, ["P7", "nG"], ["ov"])
@@ -421,15 +424,15 @@ def rank_program(g, core, T, topo):
         if not last:
             ac(T.spare[:], T.dup[:], ["dup"], ["cnt", "spare"], AF.Identity, 1.0, -1.0, T.cnt[:], M + 24)
         ag(P[1][:, 0:2 * M], T.Ku[:], ["Ku0", "Ku1"], ["P1"], 2 * M)
-        ac(T.xo[:], T.X[:, 0:n0].indirect(pG), ["X", "Xn", kp], ["xo"], AF.Identity, OFF - 0.25, n=M, kind="g")
+        ac(T.xo[:], T.X[:, 0:n0].indirect(pG), ["X", "Xn", "pu"], ["xo"], AF.Identity, OFF - 0.25, n=M, kind="g")
         ac(T.xp[:], T.xo[:], ["xo"], ["xp"], AF.Identity, -OFF, n=M)
         tt(C, T.xp[:], P[1][:, 0:M], OP.min, ["xp", "P1"], ["C"], M)
         tt(E, T.xp[:], P[1][:, M:2 * M], OP.min, ["xp", "P1"], ["E"], M)
         mm(P[0][:, 0:2 * M], T.nPm[:], T.CE[:], True, ["nPm", "C", "E"], "P0", 2 * M)
         if t > 0:
-            (cp if AV else ag)(T.ab[:, 0:M], T.L[:, 0:n0].indirect(pG), LK + [kp], ["a"], M, "g")
+            (cp if AV else ag)(T.ab[:, 0:M], T.L[:, 0:n0].indirect(pG), LK + ["pu"], ["a"], M, "g")
         else:
-            cp(T.ab[:, 0:M], T.NB[:].indirect(pG), ["NB0", "NB1", "NB2", "NB3", kp], ["a"], M, "g")
+            cp(T.ab[:, 0:M], T.NB[:].indirect(pG), ["NB0", "NB1", "NB2", "NB3", "pu"], ["a"], M, "g")
         ac(T.av[:], T.ab[:, 0:M], ["a"], ["av"], AF.Identity, -OFF, n=M)
         tt(T.X[:, n0:n1], E, P[3][:, 0:M], OP.mult, ["E", "P3"], ["Xn"], M)
         tt(T.X[:, 0:W + M].indirect(off), C, T.BT[:, M * t:M * t + M], OP.add, ["C", "BT", "ou"] + ["BT8", "BT9", "~Ln"] * (t > 0), ["X", "Xn"], M, "s")
@@ -476,7 +479,9 @@ def rank_program(g, core, T, topo):
                 else:
                     ac(T.XR[:, j0:j1], T.X[:, j0:j1], ["X", "Xn", "~b0"], ["XR%d" % j], AF.Identity, OFF - 0.25, n=j1 - j0)
                     ac(T.XO[:, j0:j1], T.XR[:, j0:j1], ["XR%d" % j], ["XO%d" % j], AF.Identity, -OFF, n=j1 - j0)
-            dma("S", "dyx", T.yx[:], T.XO[:], 256 * W, ["XO%d" % j for j in range(len(STRIP))], ["yx"])
+                if j % 2:
+                    dma("S", "dyx%d" % (j // 2), T.yx[:, j0 - W // 4:j1], T.XO[:, j0 - W // 4:j1], 128 * W, ["XO%d" % (j - 1), "XO%d" % j],
+                        ["yx%d" % (j // 2)])
 
         mm(P[1][:, 0:M], T.nIc[:], T.av[:], True, ["nIc", "av"], "P1", M)
         for i0, i1 in CA:
@@ -535,7 +540,7 @@ def rank_program(g, core, T, topo):
                     if h == 1:
                         to_list(P[7][:, M:M + 12], "Z1", T.mk, ["mk0", "mk1"], "P7")
                         i1 = M + 12
-                    mul, add = (-1024.0, OFF) if WV else (-2048.0, OFF - 15 * 2048)
+                    mul, add = (-1024.0, 0.0) if WV else (-2048.0, -15.0 * 2048)
                     if SV > 1 - h:
                         ts(T[sp][:, i0:i1], P[7][:, i0:i1], mul, add, OP.mult, OP.add, ["P7"], [sp + "_%d" % h], i1 - i0)
                     else:
@@ -546,7 +551,7 @@ def rank_program(g, core, T, topo):
                     send(sp, "mp%d" % (t + 1), "ap%d" % (t + 1), n_in, [sp + "_0", sp + "_1", sp + "g"], 0, i1)
         ts(T.L[:, 0:W + M].indirect(off), T.ec[:], -2048.0, OFF, OP.mult, OP.add, ["ec0", "ec1", "ou"], LK, M, "s")
         if last:
-            dma("S", "dyn0", T.yn[:, 0:n0], T.L[:, 0:n0], 512 * n0, LK[:4] + ["~yx"] * YF, [])
+            dma("S", "dyn0", T.yn[:, 0:n0], T.L[:, 0:n0], 512 * n0, LK[:4] + ["~yx%d" % j for j in range(YF)], [])
 
         PE, KE = (P[2][:, 0:M], P[EB][:, M:2 * M]), ("P2", "P%d" % EB)
         ck = T["CKE1" if last else "CKE0"]
@@ -586,7 +591,7 @@ def rank_program(g, core, T, topo):
             e_sum("Z16", ((k, 0), (k, 1)), 2 * M * k, ["cE%d_0" % k, "cE%d_1" % k])
         tt(T.k2[:], PE[0], T.NE[:], OP.max, [KE[0], "NE"], ["k2"], M)
         tt(PE[1], PE[1], T.k2[:], OP.max, [KE[1], "k2"], [KE[1]], M)
-        if EV:
+        if EV or last:
             ts(T.rE[:], PE[1], -OFF, None, OP.add, None, [KE[1]], ["rE"], M)
         else:
             ac(T.rE[:], PE[1], [KE[1]], ["rE"], AF.Identity, -OFF, n=M)
@@ -650,5 +655,5 @@ def rank_program(g, core, T, topo):
     g.wait_ge(T.sem["sent"], (3 - ONE) * (RO - 1) * n_eng)
     for s in ("sV", "sA", "sP", "sG"):
         need("G", (s, count[s]))
-    for s in ("dyx", "dyn0", "dyn1"):
+    for s in ("dyx0", "dyx1", "dyn0", "dyn1"):
         need("G", (s, 16))

import math
from concourse.mybir import AluOpType as OP, ActivationFunctionType as AF, AxisListType as AX

V, M, KK, RO, ST = 2048, 192, 512, 5, 2
W = V + M * RO
ALT = W + M
U = 4096.0
OFF = 1536.0
TOP = -103 * 4096
BIG = 2097152.0
LN2 = math.log(2.0)
KD = 13
KDL = 11
NPRE = 0
CH = ((0, 64), (64, 128), (128, 192))
XS = ((0, 64, "V"), (64, 128, "A"), (128, 192, "A"))
CA = ((0, 128), (128, 192))
H = ((0, 128, 6), (128, 192, 5))
STRIP = ("V", "V", "A", "A")
NBP = 1
LV = 0
BV = 5
YF = 0
EB = 6
BM = 0
SD = 0
SK = 0
AM = 0
ONE = 0
WV = 2
SV = 1
RV = 1
EV = 0
AV = 0
CYC = 0.83e-3
GUESS = ({"pe": 0.52e-3, "mm": 0.0, "act": 0.1, "gather": 1.56, "scatter": 3.8, "hop": 0.16, "own": 0.08, "far": 2.7, "dma": 1.2, "bw": 350e3},
         {"pe": 0.45e-3, "mm": 0.0, "act": 0.12, "gather": 1.4, "scatter": 3.5, "hop": 0.13, "own": 0.09, "far": 1.9, "dma": 0.9, "bw": 550e3},
         {"pe": 0.5e-3, "mm": 0.0, "act": 0.12, "gather": 1.9, "scatter": 5.0, "hop": 0.11, "own": 0.06, "far": 1.6, "dma": 0.9, "bw": 400e3})
MOVES = 50000
SEED = 1

SCRATCH = {
    "X": ("sbuf", [128, W + M], "bfloat16"), "L": ("sbuf", [128, W + M], "float32"),
    "XR": ("sbuf", [128, W], "float16"), "XO": ("sbuf", [128, W], "bfloat16"), "BT": ("sbuf", [128, M * RO], "bfloat16"),
    "ID": ("sbuf", [128, ALT + W - M], "float32"), "NB": ("sbuf", [128, V], "int32"),
    "K0": ("sbuf", [128, KK], "bfloat16"), "K1": ("sbuf", [128, KK], "bfloat16"),
    "psi": ("sbuf", [128, 12], "int32"), "wti": ("sbuf", [128, 1], "int32"), "wf": ("sbuf", [128, 1], "bfloat16"),
    "J": ("sbuf", [128, M], "bfloat16"), "Jg": ("sbuf", [128, 128], "bfloat16"), "J16": ("sbuf", [128, M], "bfloat16"),
    "pc": ("sbuf", [128, 2], "int32"), "ci": ("sbuf", [128, 4], "int32"),
    "cf": ("sbuf", [128, 12], "bfloat16"), "c5": ("sbuf", [128, 1], "float32"), "cG": ("sbuf", [128, 12], "int32"), "cGu": ("sbuf", [128, 12], "uint16"),
    "nG": ("sbuf", [128, 12 * (RO + 1)], "float32"), "mask": ("sbuf", [128, M], "bfloat16"), "thr": ("sbuf", [128, M], "float32"),
    "gx": ("sbuf", [128, M], "float16"), "pu": ("sbuf", [128, 12], "uint16"), "c15": ("sbuf", [128, 12], "bfloat16"),
    "hb": ("sbuf", [128, 16], "bfloat16"), "wr": ("sbuf", [128, 16], "bfloat16"), "wm": ("sbuf", [128, 16], "float32"),
    "on32": ("sbuf", [128, 128], "float32"), "I32": ("sbuf", [128, 128], "float32"), "CK": ("sbuf", [128, 2 * M], "bfloat16"),
    "CKE0": ("sbuf", [128, 2 * M], "float16"), "CKE1": ("sbuf", [128, 2 * M], "float16"),
    "pGf": ("sbuf", [128, 16], "float32"), "EQ": ("sbuf", [128, 12 * M], "bfloat16"),
    "dup": ("sbuf", [128, M], "bfloat16"), "zr": ("sbuf", [128, M], "float16"), "spare": ("sbuf", [128, M], "bfloat16"),
    "thm": ("sbuf", [128, M], "float32"), "run": ("sbuf", [128, M], "bfloat16"), "dg": ("sbuf", [128, M], "bfloat16"),
    "ds": ("sbuf", [128, M], "bfloat16"), "og": ("sbuf", [128, 48], "float32"), "pm": ("sbuf", [128, M], "float32"), "pn": ("sbuf", [128, M], "float32"),
    "cnt": ("sbuf", [128, 1], "float32"), "ou": ("sbuf", [128, 24], "uint16"),
    "ui": ("sbuf", [128, 24], "int32"), "uu": ("sbuf", [128, 12], "uint16"),
    "Ku": ("sbuf", [128, 2 * M], "bfloat16"), "CE": ("sbuf", [128, 2 * M], "bfloat16"),
    "ab": ("sbuf", [128, 2 * M], "uint16"), "bv": ("sbuf", [128, M], "float16"), "av": ("sbuf", [128, M], "float16"),
    "xo": ("sbuf", [128, M], "float16"), "xp": ("sbuf", [128, M], "bfloat16"),
    "xr": ("sbuf", [128, 16 * M], "float16"), "xab": ("sbuf", [128, 32 * M], "bfloat16"),
    "cC": ("sbuf", [128, 32 * M], "bfloat16"), "cE": ("sbuf", [128, 32 * M], "bfloat16"),
    "NC": ("sbuf", [128, M], "float32"), "NE": ("sbuf", [128, M], "float32"),
    "k1": ("sbuf", [128, M], "float32"), "k2": ("sbuf", [128, M], "float32"),
    "rC": ("sbuf", [128, M], "bfloat16"), "rE": ("sbuf", [128, M], "bfloat16"), "vv": ("sbuf", [128, M], "bfloat16"),
    "ec": ("sbuf", [128, M], "float32"), "mk": ("sbuf", [128, M], "float16"),
}
for _n in ("I", "nI", "Ih", "I256", "IU", "nBI", "nIc", "Pm", "nPm", "Bk", "Bw", "TT", "t1", "t2"):
    SCRATCH[_n] = ("sbuf", [128, 128], "bfloat16")
for _n in ("Z1", "Z16", "Z8", "Zc", "Zd", "Zw", "Zb", "nZb"):
    SCRATCH[_n] = ("sbuf", [128, 144], "bfloat16")
for _t in range(RO):
    SCRATCH["mp%d" % _t] = ("sbuf", [128, M + 12], "float16")
    SCRATCH["mz%d" % _t] = ("sbuf", [128, M], "float16" if _t else "bfloat16")
for _t in range(RO - 1):
    SCRATCH["sp%d" % _t] = ("sbuf", [128, M + 12], "float16")
    SCRATCH["sz%d" % _t] = ("sbuf", [128, M], "float16")
for _b in range(8):
    SCRATCH["P%d" % _b] = ("psum", [128, 512], "float32")

DMAS = ["dps", "dwt", "dzi", "dkc", "dxc", "dyx0", "dyx1", "dyn0", "dyn1"] + ["dnb%d" % _j for _j in range(NBP)]
SEMAPHORES = ["sV", "sA", "sP", "sG", "sent"] + DMAS + ["ap%d" % t for t in range(1, RO)] + ["az%d" % t for t in range(1, RO)]
PLAN = {}


def first_plan(queue, busy, tail, edges):
    n = len(queue)
    rest = [busy[i] + tail[i] for i in range(n)]
    for i in reversed(range(n)):
        for j, gap in edges[i]:
            rest[j] = max(rest[j], busy[j] + gap + rest[i])
    start, slots = [0.0] * n, {}
    for i in sorted(range(n), key=lambda i: (-rest[i], i)):
        t = max([0.0] + [start[j] + busy[j] + gap for j, gap in edges[i]])
        s = slots.setdefault(queue[i], [])
        at = len(s)
        while at and s[at - 1][1] > t:
            at -= 1
        while at < len(s) and s[at][0] < t + busy[i] - 1e-9:
            t = max(t, s[at][1])
            at += 1
        s.insert(at, (t, t + busy[i]))
        start[i] = t
    return sorted(range(n), key=lambda i: (start[i], i))


def replay(order, lo, known, ends, queue, busy, tail, edges):
    end, why = list(known[2]), list(known[3])
    ahead = {queue[i]: i for i in order[:lo]}
    for i in order[lo:]:
        w = ahead.get(queue[i], -1)
        t = end[w] if w >= 0 else 0.0
        for j, gap in edges[i]:
            if end[j] + gap > t:
                t, w = end[j] + gap, j
        end[i], why[i], ahead[queue[i]] = t + busy[i], w, i
    last = max(ends, key=lambda i: end[i] + tail[i])
    return end[last] + tail[last], last, end, why


def schedule(queue, guesses):
    n = len(queue)
    before = [set(j for j, gap in e) for e in guesses[0][2]]
    behind = [set() for _ in range(n)]
    for i in range(n):
        for j in before[i]:
            behind[j].add(i)
    state = [SEED]

    def draw(k):
        state[0] = (state[0] * 1103515245 + 12345) % 2147483648
        return (state[0] >> 8) % k

    order = first_plan(queue, *guesses[0])
    ends = [i for i in range(n) if not behind[i]]
    runs = [replay(order, 0, (0, 0, [0.0] * n, [-1] * n), ends, queue, *q) for q in guesses]
    best = (sum(r[0] for r in runs), order)
    now = best[0]
    for move in range(MOVES):
        top, i, end, why = runs[draw(len(runs))]
        pairs = []
        while i >= 0:
            j = why[i]
            if j >= 0 and queue[j] == queue[i] and j not in before[i]:
                pairs.append((j, i))
            i = j
        if not pairs:
            break
        j, i = pairs[draw(len(pairs))]
        lo, hi = order.index(j), order.index(i)
        ahead, step = draw(2), (0, 0, 1, 2, 5)[draw(5)]
        k = lo if ahead else hi
        while step and 0 < k < n - 1:
            k += -1 if ahead else 1
            if queue[order[k]] == queue[i]:
                lo, hi, step = min(lo, k), max(hi, k), step - 1
        part = order[lo:hi + 1]
        moved = {i if ahead else j}
        for x in (reversed(part) if ahead else part):
            if x in moved:
                moved |= before[x] if ahead else behind[x]
        if order[lo if ahead else hi] in moved:
            continue
        new = order[:lo] + [x for x in part if (x in moved) == ahead] + [x for x in part if (x in moved) != ahead] + order[hi + 1:]
        tried = [replay(new, lo, r, ends, queue, *q) for r, q in zip(runs, guesses)]
        length = sum(r[0] for r in tried)
        if length < now + 0.002 * draw(100) * (1 - move / MOVES):
            now, order, runs = length, new, tried
            if length < best[0]:
                best = (length, new)
    return best[1]


def rank_program(g, core, T, topo):
    rank = T.rank_of(core)
    if rank is None:
        return
    n_ranks = len(T.cores)
    nxt = T.cores[(rank + ST) % n_ranks]
    rid, pid, _se = topo.addr(nxt)
    emask = topo.mask(core, nxt)
    n_eng = len(topo.engines(core, nxt))
    n_in = len(topo.engines(T.cores[(rank - ST) % n_ranks], core))

    Q = {"V": g.vector, "A": g.scalar, "P": g.tensor, "G": g, "S": g.sync}
    calls = []
    wrote, read, opened, units = {}, {}, {}, {}

    def note(e, call, busy, r, w, after=lambda q: 0.0, event=None, adds=False, group=None):
        deps = {}
        for k in r:
            if k[0] == "~":
                for j in wrote.get(k[1:], []):
                    deps.setdefault(j, False)
                continue
            for j in wrote.get(k, []):
                deps[j] = True
            if k[0] == "P" and k[1:].isdigit():
                for j in read.get(k, []):
                    if calls[j][0] != e:
                        deps[j] = True
        for k in w:
            for j in (wrote[k][:1] if adds else wrote.get(k, []) + read.get(k, [])):
                if e != "G":
                    deps[j] = True
        i = len(calls)
        calls.append([e, call, busy, after, deps, event, group])
        for k in r:
            read.setdefault(k, []).append(i)
        for k in w:
            if adds:
                wrote[k].append(i)
            else:
                wrote[k] = [i]
                read[k] = []

    def unit(*name):
        units[len(calls)] = name

    def cyc(n, kind):
        if kind in ("g", "s"):
            return lambda q: 0.06 + n * q["gather" if kind == "g" else "scatter"] * CYC
        return lambda q: max(64, n * {"": 1, "h": 0.5, "d": 2}[kind]) * CYC

    def dma(e, sem, out, in_, nbytes, r, w):
        note(e, lambda: Q[e].dma_start(out, in_), lambda q: nbytes / q["bw"] + 0.2 if e == "S" else 0.05, r, w, lambda q: q["dma"], (sem, 16))

    def send(src, dst, sem, val, r, c0, c1, slack=0.0, adds=False):
        issue = 0.3 if read.get("far") else 2.3
        note("G", lambda: g.remote_dma(T[dst][:, c0:c1], T[src][:, c0:c1], T.sem[sem], T.sem["sent"], pid, rid, emask), lambda q: issue,
             r + ["far"], [dst], lambda q: q["far"] + slack + (c1 - c0) * 0.005, (sem, val), adds)

    v, a, pe = g.vector, g.scalar, g.tensor

    def ts(out, in0, s1, s2, o0, o1, r, w, n=64, kind=""):
        if s2 is None:
            note("V", lambda: v.tensor_scalar(out, in0, s1, None, o0), cyc(n, kind), r, w)
        else:
            note("V", lambda: v.tensor_scalar(out, in0, s1, s2, o0, o1), cyc(n, kind), r, w)

    def tt(out, in0, in1, o, r, w, n=64, kind=""):
        note("V", lambda: v.tensor_tensor(out, in0, in1, o), cyc(n, kind), r, w)

    def cp(out, in_, r, w, n=64, kind=""):
        note("V", lambda: v.tensor_copy(out, in_), cyc(n, kind), r, w)

    def scan(out, src, r, w, c0, c1, kind):
        note("V", lambda: v.tensor_tensor_scan(out[:, c0:c1], T.run[:, c0:c1], src[:, c0:c1], 0.0, OP.mult, OP.add), cyc(c1 - c0, kind), r + ["run"], w)

    def ms(out, val, w, n=64):
        note("V", lambda: v.memset(out, val), cyc(n, "h"), [], w)

    def ac(out, in_, r, w, f=AF.Identity, bias=0.0, scale=1.0, acc=None, n=64, kind=""):
        note("A", lambda: a.activation(out, in_, f, bias, scale, accum_out=acc), lambda q: q["act"] + cyc(n, kind)(q), r, w)

    def ag(out, in_, r, w, n=64, kind=""):
        note("A", lambda: a.activation(out, in_, AF.Copy), lambda q: q["act"] + cyc(n, kind)(q), r, w)

    def mm(out, lhsT, rhs, st, r, bank, n):
        if st:
            opened[bank] = len(calls)
        note("P", lambda stop: pe.matmul(out, lhsT, rhs, st, stop), lambda q: q["mm"] + max(64, n) * q["pe"], r, [bank], adds=not st, group=opened[bank])

    def io(out, pat, base, cm, w, n, flt=True):
        if flt:
            note("G", lambda: g.iota(out, pat, base, cm, allow_small_or_imprecise_dtypes=True), lambda q: 0.13 + 2 * n * CYC, [], w)
        else:
            note("G", lambda: g.iota(out, pat, base, cm), lambda q: 0.13 + 2 * n * CYC, [], w)

    def sel(Z, k):
        return T[Z][:, 15 - k:143 - k]

    def to_list(out, Z, src, keys, bank, first=True):
        for m in range(16):
            unit("list", len(calls) - m)
            mm(out, sel(Z, m), src[:, m:M:16], first and m == 0, keys + [Z], bank, 12)

    P = [T["P%d" % b] for b in range(8)]
    col = lambda j: T.cf[:, j:j + 1]
    J128, J144 = T.J[:, 0:128], T.J[:, 0:144]

    dma("S", "dps", T.psi[:], T.ps[:], 6144, [], ["psi"])
    dma("A", "dwt", T.wti[:], T.wt[:], 512, [], ["wti"])
    dma("A", "dzi", T.mz0[:], T.zi[:], 256 * M, [], ["mz0"])
    dma("S", "dkc", T.K0[:], T.kc[:], 256 * KK, ["~psi"], ["K0"])
    dma("S", "dxc", T.X[:, 0:V], T.xc[:], 256 * V, ["~K0"], ["X"])
    for j in range(NBP):
        w = V // NBP
        dma("S", "dnb%d" % j, T.NB[:, w * j:w * j + w], T.nb[:, w * j:w * j + w], 512 * w, ["~X"],
            ["NB%d" % q for q in range(4 * j // NBP, 4 * (j + 1) // NBP)])
    io(T.pc[:], [[1, 2]], 0, 1, ["pc"], 2, False)
    io(T.J[:], [[1, M]], 0, 0, ["J"], M)
    io(T.Jg[:], [[16, 8], [0, 16]], 0, 0, ["Jg"], 128)
    io(T.J16[:], [[0, 12], [1, 16]], 0, 0, ["J16"], M)
    io(T.cG[:], [[1, 12]], 0, 0, ["cG"], 12, False)
    io(T.nG[:], [[16, 12 * (RO + 1)]], V, 1, ["nG"], 72)
    io(T.ID[:, 0:W], [[1, W]], 0, 0, ["ID"], W)
    io(T.ID[:, W:ALT], [[0, M]], 110 * 4096, 0, ["ID2"], M)
    io(T.ID[:, ALT:ALT + V - 1], [[1, V - 1]], TOP + 1, 0, ["ALT"], V)
    io(T.ID[:, ALT + V - 1:ALT + W - M], [[1, W - M - V + 1]], TOP, 0, ["ALT2"], W - M - V)
    ts(T.ci[:, 0:1], T.pc[:, 0:1], 15, None, OP.bitwise_and, None, ["pc"], ["ci0"])
    ts(T.ci[:, 1:2], T.pc[:, 0:1], 1, None, OP.bitwise_and, None, ["pc"], ["ci1"])
    cp(col(0), T.pc[:, 0:1], ["pc"], ["c0"])
    cp(col(1), T.ci[:, 0:1], ["ci0"], ["c1"])
    ts(col(8), T.ci[:, 1:2], -2.0, 1.0, OP.mult, OP.add, ["ci1"], ["c8"])
    tt(col(2), col(0), col(1), OP.subtract, ["c0", "c1"], ["c2"])
    tt(col(4), col(0), col(8), OP.add, ["c0", "c8"], ["c4"])
    ts(col(3), col(2), 15.0, None, OP.add, None, ["c2"], ["c3"])
    ts(col(6), col(1), KD - 0.5, 128.0, OP.is_ge, OP.mult, ["c1"], ["c6"])
    ts(col(7), col(1), KDL - 0.5, 128.0, OP.is_ge, OP.mult, ["c1"], ["c7"])
    for name, c, wgt in (("I", 0, 1.0), ("nI", 0, -1.0), ("Ih", 0, 0.5), ("I256", 0, 256.0), ("IU", 0, U), ("nBI", 0, -BIG),
                         ("nIc", 0, -1.0 / 2048), ("t2", 0, -1024.0), ("Pm", 4, 1.0), ("nPm", 4, -1.0)):
        ts(T[name][:], J128, col(c), wgt, OP.is_equal, OP.mult, ["J", "c%d" % c], [name], 128, "h")
    for name, wgt in (("Z1", 1.0), ("Zd", ALT / 16.0), ("Z16", 16 * U), ("Z8", 8 * U), ("Zc", 32.0)):
        ts(T[name][:], J144, col(3), wgt, OP.is_equal, OP.mult, ["J", "c3"], [name], 144, "h")
    ts(T.Bk[:], T.Jg[:], col(2), None, OP.is_equal, None, ["Jg", "c2"], ["Bk"])
    ts(T.mask[:], T.J16[:], col(1), None, OP.is_equal, None, ["J16", "c1"], ["mask"], M, "h")
    ac(T.thr[:], T.J[:], ["J"], ["thr"], AF.Exp, 96 * LN2 + math.log(1.25), -LN2, n=1800)
    ts(T.nG[:], T.nG[:], col(2), None, OP.subtract, None, ["nG", "c2"], ["nG"], 72)
    ms(T.c15[:], OFF, ["c15"])
    ac(col(9), col(1), ["c1", "thr"], ["c9"], AF.Exp, 0.0, -LN2)
    ts(T.Bw[:], T.Jg[:], col(2), col(9), OP.is_equal, OP.mult, ["Jg", "c2", "c9"], ["Bw"])
    if SD:
        ts(T.thm[:], T.mask[:], -1e29, 1e29, OP.mult, OP.add, ["mask"], ["thm"], M)
        tt(T.thm[:], T.thm[:], T.thr[:], OP.max, ["thm", "thr"], ["thm"], M, "d")
    ts(T.t1[:], J128, col(0), 65536.0, OP.is_gt, OP.mult, ["J", "c0"], ["t1"])
    mm(P[3][:, 0:128], T.I[:], T.t1[:], True, ["I", "t1"], "P3", 128)
    mm(P[3][:, 0:128], T.I[:], T.Bk[:], False, ["I", "Bk"], "P3", 128)
    mm(P[3][:, 0:128], T.I[:], T.t2[:], False, ["I", "t2"], "P3", 128)
    tt(T.TT[:], P[3][:, 0:128], T.Bk[:], OP.mult, ["P3", "Bk"], ["TT"], 128)
    ac(T.on32[:], T.I[:], ["I"], ["on32"], AF.Identity, 1.0 / 16, 0.0, n=128)
    ms(T.CK[:, 0:M], -31.0, ["CKa"], M)
    ms(T.CK[:, M:2 * M], -32.0, ["CKb"], M)
    ts(T.CKE0[:], T.CK[:], col(6), OFF / U, OP.add, OP.add, ["CKa", "CKb", "c6"], ["CKE0"], 2 * M, "h")
    ts(T.CKE1[:], T.CK[:], col(7), OFF / U, OP.add, OP.add, ["CKa", "CKb", "c7"], ["CKE1"], 2 * M, "h")
    ts(T.hb[:], T.J[:, 0:16], col(1), 0.5, OP.is_equal, OP.mult, ["J", "c1"], ["hb"])
    cp(T.BT[:, 0:1], T.hb[:, 11:12], ["hb"], ["BT"])
    for e in range(10):
        w0, w1 = 1 << e, min(2 << e, M * RO)
        r, w = ["BT", "hb"] + ["BT8"] * (e > 8), ["BT" if e < 8 else "BT%d" % e]
        if e < BV:
            ts(T.BT[:, w0:w1], T.BT[:, 0:w1 - w0], T.hb[:, e:e + 1], None, OP.add, None, r, w, w1 - w0, "h")
        else:
            ac(T.BT[:, w0:w1], T.BT[:, 0:w1 - w0], r, w, AF.Identity, T.hb[:, e:e + 1], n=w1 - w0)
    ac(T.wr[:], T.J[:, 0:16], ["J", "thr"], ["wr"], AF.Exp, 2 * LN2, LN2)
    for j, wj in ((12, -16384.0), (13, 4.0), (14, 0.0), (15, 0.0)):
        ms(T.wr[:, j:j + 1], wj, ["wr"])
    tt(T.wm[:], T.wr[:], T.hb[:], OP.mult, ["wr", "hb"], ["wm"])
    note("V", lambda: v.tensor_reduce(T.c5[:], T.wm[:], AX.X, OP.add), cyc(16, ""), ["wm"], ["c5f"])
    cp(col(5), T.c5[:], ["c5f"], ["c5"])
    ts(T.Zb[:], J144, col(3), col(5), OP.is_equal, OP.mult, ["J", "c3", "c5"], ["Zb"], 144, "h")
    ts(T.nZb[:], T.Zb[:], -1.0, None, OP.mult, None, ["Zb"], ["nZb"], 144, "h")
    ag(T.K1[:, 0:KK:2], T.K0[:, 1:KK:2], ["K0"], ["K1a"], 256)
    ag(T.K1[:, 1:KK:2], T.K0[:, 0:KK:2], ["K0"], ["K1b"], 256)
    cp(T.wf[:], T.wti[:], ["wti"], ["wf"])
    ts(T.Zw[:], J144, col(3), T.wf[:], OP.is_equal, OP.mult, ["J", "c3", "wf"], ["Zw"], 144, "h")
    cp(T.cGu[:], T.cG[:], ["cG"], ["cGu"])
    ts(T.pGf[:, 0:12], T.psi[:], -OFF, None, OP.add, None, ["psi"], ["pGf"])
    tt(T.gx[:], T.pGf[:, 0:12].indirect(T.cGu[:, 0:12]), T.mask[:], OP.mult, ["pGf", "cGu", "mask"], ["gx"], M, "g")
    ts(T.mp0[:, M:M + 12], T.psi[:], -OFF, None, OP.add, None, ["psi"], ["mp0g"])
    mm(P[6][:, 0:M], T.Bk[:], T.gx[:], True, ["Bk", "gx"], "P6", M)
    cp(T.mp0[:, 0:M], P[6][:, 0:M], ["P6", "mp0g"], ["mp0"], M)
    for j in range(4):
        (cp if j < LV else ag)(T.L[:, 512 * j:512 * j + 512], T.NB[:, 512 * j:512 * j + 512], ["NB%d" % j], ["L%d" % j], 512)

    def cuts(t):
        if t > 0:
            mm(P[7][:, 16:17], T.on32[:], T.cnt[:], True, ["on32", "cnt"], "P7", 256)
        to_list(P[7][:, 0:12], "Zw", T["mz%d" % t], ["mz%d" % t], "P7")
        if t > 0:
            ts(T.ui[:, 0:12], P[7][:, 0:12], P[7][:, 16:17], 4194304.0, OP.add, OP.add, ["P7"], ["ui0"])
        else:
            ts(T.ui[:, 0:12], P[7][:, 0:12], 262144.0, None, OP.add, None, ["P7"], ["ui0"])
        ts(T.ui[:, 12:24], T.ui[:, 0:12], KK - 1, None, OP.bitwise_and, None, ["ui0"], ["ui1"])
        cp(T.uu[:], T.ui[:, 12:24], ["ui1"], ["uu"])
        ag(T.Ku[:, 0:M], T.K0[:].indirect(T.uu[:, 0:12]), ["K0", "uu"], ["Ku0"], M, "g")
        ag(T.Ku[:, M:2 * M], T.K1[:].indirect(T.uu[:, 0:12]), ["K1a", "K1b", "uu"], ["Ku1"], M, "g")

    cuts(0)
    XA, XB = ["xa%d" % i0 for i0, i1, e in XS], ["xb0", "xb1", "xb2"]
    xa_keys = lambda c0, c1: ["xa%d" % i0 for i0, i1, e in XS if i0 < c1 and i1 > c0]
    LK = ["L0", "L1", "L2", "L3", "Ln"]

    for t in range(RO):
        last = t == RO - 1
        n0 = V + M * t
        n1 = n0 + M
        mp, mz = T["mp%d" % t], T["mz%d" % t]
        kp, kz, sp, sz = "mp%d" % t, "mz%d" % t, "sp%d" % t, "sz%d" % t
        pG = T.pu[:, 0:12]
        C, E = T.CE[:, 0:M], T.CE[:, M:2 * M]
        off, offv = T.ou[:, 12:24], T.ou[:, 0:12]
        kd = KDL if last else KD

        ac(pG, mp[:, M:M + 12], [kp], ["pu"], AF.Identity, OFF)
        for c in range(12):
            e0 = c * M
            unit("eq", t, c // 4)
            ts(T.EQ[:, e0:e0 + M - 16 * c], mp[:, 16 * c:M], mp[:, M + c:M + c + 1], 2.0 ** (95 - 16 * c), OP.is_equal, OP.mult,
               [kp] + ["~L0"] * (t > 0), ["EQ%d" % c], M - 16 * c, "h")
            unit("eq sum", t, c // 4)
            mm(P[5][:, 16 * c:M], T.Bw[:], T.EQ[:, e0:e0 + M - 16 * c], c == 0, ["Bw", "EQ%d" % c], "P5", M - 16 * c)
        tt(T.dup[:], P[5][:, 0:M], T.thr[:], OP.is_ge, ["P5", "thr"], ["dup"], M)
        if SD:
            tt(T.og[:, 0:12], T.nG[:, 12 * RO:12 * RO + 12], T.pGf[:, 0:12], OP.subtract, ["nG", "pGf"], ["og0"])
            tt(T.dg[:], P[5][:, 0:M], T.thm[:], OP.is_ge, ["P5", "thm"], ["dg"], M)
            scan(T.ds, T.dg, ["dg"], ["ds"], 0, M, "h")
            tt(T.og[:, 12:24], T.ds[:, 15:M:16], T.og[:, 0:12], OP.mult, ["ds", "og0"], ["og1"])
            tt(off, T.og[:, 12:24], T.pGf[:, 0:12], OP.add, ["og1", "pGf"], ["ou"])
            ac(T.og[:, 24:36], T.pGf[:, 0:12], ["pGf"], ["og2"], AF.Identity, float(ALT))
            tt(T.og[:, 36:48], T.ds[:, 15:M:16], T.og[:, 24:36], OP.mult, ["ds", "og2"], ["og3"])
            tt(offv, T.og[:, 36:48], T.nG[:, 12 * t:12 * t + 12], OP.max, ["og3", "nG"], ["ov"])
        else:
            mm(P[7][:, 0:12], T.I[:], T.c15[:], True, ["I", "c15"], "P7", 12)
            mm(P[7][:, 0:12], T.I[:], mp[:, M:M + 12], False, ["I", kp], "P7", 12)
            to_list(P[7][:, 0:12], "Zd", T.dup, ["dup"], "P7", False)
            tt(off, P[7][:, 0:12], T.nG[:, 12 * RO:12 * RO + 12], OP.min, ["P7", "nG"], ["ou"])
            tt(offv, P[7][:, 0:12], T.nG[:, 12 * t:12 * t + 12], OP.max, ["P7", "nG"], ["ov"])
        ac(P[3][:, 0:M], T.dup[:], ["dup"], ["P3"], AF.Identity, 1.0, -1.0, n=M)
        if not last:
            ac(T.spare[:], T.dup[:], ["dup"], ["cnt", "spare"], AF.Identity, 1.0, -1.0, T.cnt[:], M + 24)
        ag(P[1][:, 0:2 * M], T.Ku[:], ["Ku0", "Ku1"], ["P1"], 2 * M)
        ac(T.xo[:], T.X[:, 0:n0].indirect(pG), ["X", "Xn", "pu"], ["xo"], AF.Identity, OFF - 0.25, n=M, kind="g")
        ac(T.xp[:], T.xo[:], ["xo"], ["xp"], AF.Identity, -OFF, n=M)
        tt(C, T.xp[:], P[1][:, 0:M], OP.min, ["xp", "P1"], ["C"], M)
        tt(E, T.xp[:], P[1][:, M:2 * M], OP.min, ["xp", "P1"], ["E"], M)
        mm(P[0][:, 0:2 * M], T.nPm[:], T.CE[:], True, ["nPm", "C", "E"], "P0", 2 * M)
        if t > 0:
            (cp if AV else ag)(T.ab[:, 0:M], T.L[:, 0:n0].indirect(pG), LK + ["pu"], ["a"], M, "g")
        else:
            cp(T.ab[:, 0:M], T.NB[:].indirect(pG), ["NB0", "NB1", "NB2", "NB3", "pu"], ["a"], M, "g")
        ac(T.av[:], T.ab[:, 0:M], ["a"], ["av"], AF.Identity, -OFF, n=M)
        tt(T.X[:, n0:n1], E, P[3][:, 0:M], OP.mult, ["E", "P3"], ["Xn"], M)
        tt(T.X[:, 0:W + M].indirect(off), C, T.BT[:, M * t:M * t + M], OP.add, ["C", "BT", "ou"] + ["BT8", "BT9", "~Ln"] * (t > 0), ["X", "Xn"], M, "s")
        if not last:
            mm(P[4][:, 0:M], T.nI[:], mz[:], True, ["nI", kz], "P4", M)
            mm(P[4][:, 0:M], T.I[:], C, False, ["I", "C"], "P4", M)
            mm(P[4][:, 0:M], T.nBI[:], T.dup[:], False, ["nBI", "dup"], "P4", M)
            ac(T.zr[:], P[4][:, 0:M], ["P4"], ["zr"], AF.Relu, 511.5 + (OFF if t else 0), n=M)
            mm(P[5][:, 0:M], T.I[:], mz[:], True, ["I", kz], "P5", M)
            mm(P[5][:, 0:M], T.I256[:], T.dup[:], False, ["I256", "dup"], "P5", M)
            mm(P[5][:, 0:M], T.Ih[:], T.zr[:], False, ["Ih", "zr"], "P5", M)
            ac(T[sz][:], P[5][:, 0:M], ["P5"], [sz], AF.Identity, (0 if t else OFF) - 256, n=M)
            send(sz, "mz%d" % (t + 1), "az%d" % (t + 1), n_in, [sz], 0, M, 2.5)
            cuts(t + 1)
        ac(T.NC[:], T.ID[:, 0:ALT + n0].indirect(offv), ["ID", "ID2", "ALT", "ALT2", "ov"], ["NC"], AF.Identity, 322.75, -1.0 / 2048,
           n=M, kind="g")
        ac(T.NE[:], T.ID[:, 0:ALT].indirect(off), ["ID", "ID2", "ou"], ["NE"], AF.Identity, 130 * U, n=M, kind="g")

        for i0, i1, e in XS:
            (cp if e == "V" else ag)(T.xab[:, 16 * i0:16 * i1], T.X[:, 0:n1].indirect(T.ab[:, i0:i1]), ["X", "Xn", "a"], ["xa%d" % i0],
                                     16 * (i1 - i0), "g")
        for j, (i0, i1) in enumerate(CH):
            kb, Pb, n = "P%d" % (5 + j % 2), P[5 + j % 2][:, 0:i1 - i0], i1 - i0
            ts(T.xr[:, 16 * i0:16 * i1], T.xab[:, 16 * i0:16 * i1], OFF - 0.25, None, OP.add, None, xa_keys(i0, i1), ["xr%d" % j], 16 * n, "h")
            for k in range(16):
                unit("with bits", t, j)
                mm(Pb, sel("Zb", k), T.xab[:, 16 * i0 + k:16 * i1:16], k == 0, ["Zb"] + xa_keys(i0, i1), kb, n)
            for k in range(16):
                unit("without", t, j)
                mm(Pb, sel("nZb", k), T.xr[:, 16 * i0 + k:16 * i1:16], False, ["nZb", "xr%d" % j], kb, n)
            tt(T.ab[:, M + i0:M + i1], Pb, T.ab[:, i0:i1], OP.max, [kb, "a"], ["b%d" % j], n)
            if i1 in (128, M):
                c0 = 0 if i1 == 128 else 128
                ts(T.bv[:, c0:i1], T.ab[:, M + c0:M + i1], -OFF, None, OP.add, None, ["b0", "b%d" % j],
                   ["bv%d" % x for x in range(c0 // 64, j + 1)], i1 - c0, "h")
            ag(T.xab[:, 16 * (M + i0):16 * (M + i1)], T.X[:, 0:n1].indirect(T.ab[:, M + i0:M + i1]), ["X", "Xn", "b%d" % j], ["xb%d" % j],
               16 * n, "g")
        if last:
            for j, e in enumerate(STRIP):
                j0, j1 = W // len(STRIP) * j, W // len(STRIP) * (j + 1)
                if e == "V":
                    ts(T.XR[:, j0:j1], T.X[:, j0:j1], OFF - 0.25, None, OP.add, None, ["X", "Xn", "~b0"], ["XR%d" % j], j1 - j0, "h")
                    ts(T.XO[:, j0:j1], T.XR[:, j0:j1], -OFF, None, OP.add, None, ["XR%d" % j], ["XO%d" % j], j1 - j0, "h")
                else:
                    ac(T.XR[:, j0:j1], T.X[:, j0:j1], ["X", "Xn", "~b0"], ["XR%d" % j], AF.Identity, OFF - 0.25, n=j1 - j0)
                    ac(T.XO[:, j0:j1], T.XR[:, j0:j1], ["XR%d" % j], ["XO%d" % j], AF.Identity, -OFF, n=j1 - j0)
                if j % 2:
                    dma("S", "dyx%d" % (j // 2), T.yx[:, j0 - W // 4:j1], T.XO[:, j0 - W // 4:j1], 128 * W, ["XO%d" % (j - 1), "XO%d" % j],
                        ["yx%d" % (j // 2)])

        mm(P[1][:, 0:M], T.nIc[:], T.av[:], True, ["nIc", "av"], "P1", M)
        for i0, i1 in CA:
            for k in range(16):
                o, key = 2 * M * k, "cCa%d_%d" % (k, i0)
                unit("a", t, i0, k // (4 if i0 else 2))
                tt(T.cC[:, o + i0:o + i1], T.xab[:, 16 * i0 + k:16 * i1:16], P[0][:, i0:i1], OP.is_ge, xa_keys(i0, i1) + ["P0"], [key], i1 - i0)
                if AM and i0 == 0:
                    continue
                unit("a sum", t, i0, k // 4)
                c0 = 0 if AM else i0
                mm(P[1][:, c0:i1], sel("Zc", k), T.cC[:, o + c0:o + i1], False, ["Zc", key, "cCa%d_0" % k], "P1", i1 - c0)
        tt(T.k1[:], P[1][:, 0:M], T.NC[:], OP.max, ["P1", "NC"], ["k1"], M)
        for i0, i1, b in H:
            mm(P[b][:, i0:i1], T.nIc[:], T.bv[:, i0:i1], True, ["nIc"] + (["bv0", "bv1"] if i0 == 0 else ["bv2"]), "P%d" % b, i1 - i0)
        for j, (i0, i1) in enumerate(CH):
            h = int(i0 >= H[1][0])
            b = H[h][2]
            for k in range(16):
                o, key = 2 * M * k + M, "cCb%d_%d" % (j, k)
                unit("b", t, j, k // (2 if i1 == M else 4))
                tt(T.cC[:, o + i0:o + i1], T.xab[:, 16 * (M + i0) + k:16 * (M + i1):16], P[0][:, i0:i1], OP.is_ge, ["xb%d" % j, "P0"], [key], i1 - i0)
                if BM and i1 != H[h][1]:
                    continue
                unit("b sum", t, j, k // (2 if i1 == M else 4))
                c0 = H[h][0] if BM else i0
                mm(P[b][:, c0:i1], sel("Zc", k), T.cC[:, o + c0:o + i1], False,
                   ["Zc"] + ["cCb%d_%d" % (x, k) for x in range(j + 1) if CH[x][0] >= c0], "P%d" % b, i1 - c0)
        for h, (i0, i1, b) in enumerate(H):
            kb, Pb, n = "P%d" % b, P[b][:, i0:i1], i1 - i0
            kw, Pw = "P%d" % (7 - h), P[7 - h][:, 256 + i0:256 + i1]
            tt(Pb, Pb, T.k1[:, i0:i1], OP.max, [kb, "k1"], [kb], n)
            if not last:
                ac(T.vv[:, i0:i1], Pb, [kb], ["vv%d" % h], AF.Exp, -200 * LN2, LN2 / 2, n=n)
                mm(Pw, T.TT[:], T.vv[:, i0:i1], True, ["TT", "vv%d" % h], kw, n)
            if RV > 1 - h:
                ts(T.rC[:, i0:i1], Pb, 25165824.0, 25165824.0, OP.add, OP.subtract, [kb], ["rC%d" % h], n)
            else:
                ag(T.rC[:, i0:i1], Pb, [kb], ["rC%d" % h], n)
            tt(T.ec[:, i0:i1], Pb, T.rC[:, i0:i1], OP.subtract, [kb, "rC%d" % h], ["ec%d" % h], n)
            if not last:
                if WV:
                    ts(Pw, Pw, 0.0, 2.0, OP.is_lt, OP.mult, [kw], [kw], n)
                else:
                    ac(Pw, Pw, [kw], [kw], AF.Sign, 0.0, -1.0, n=n)
                tt(T.mk[:, i0:i1], Pw, T.ec[:, i0:i1], OP.mult if WV else OP.min, [kw, "ec%d" % h], ["mk%d" % h], n)
                mm(P[7][:, i0:i1], T.Bk[:], T.mk[:, i0:i1], True, ["Bk", "mk%d" % h], "P7", n)
                if SK:
                    tt(T.pm[:, i0:i1], P[7][:, i0:i1], T.mask[:, i0:i1], OP.mult, ["P7", "mask"], ["pm%d" % h], n)
                    scan(T.pn, T.pm, ["pm%d" % h], ["pn%d" % h], i0, i1, "")
                    ac(T[sp][:, i0:i1], P[7][:, i0:i1], ["P7"], [sp + "_%d" % h], AF.Identity, OFF - 15 * 2048, -2048.0, n=i1 - i0)
                    if h == 1:
                        ac(T[sp][:, M:M + 12], T.pn[:, 15:M:16], ["pn0", "pn1"], [sp + "g"], AF.Identity, OFF - 15 * 2048, -2048.0)
                        i1 = M + 12
                else:
                    if h == 1:
                        to_list(P[7][:, M:M + 12], "Z1", T.mk, ["mk0", "mk1"], "P7")
                        i1 = M + 12
                    mul, add = (-1024.0, 0.0) if WV else (-2048.0, -15.0 * 2048)
                    if SV > 1 - h:
                        ts(T[sp][:, i0:i1], P[7][:, i0:i1], mul, add, OP.mult, OP.add, ["P7"], [sp + "_%d" % h], i1 - i0)
                    else:
                        ac(T[sp][:, i0:i1], P[7][:, i0:i1], ["P7"], [sp + "_%d" % h], AF.Identity, add, mul, n=i1 - i0)
                if not ONE:
                    send(sp, "mp%d" % (t + 1), "ap%d" % (t + 1), 2 * n_in, [sp + "_%d" % h] + [sp + "g"] * h, i0, i1, 0.0, h == 1)
                elif h == 1:
                    send(sp, "mp%d" % (t + 1), "ap%d" % (t + 1), n_in, [sp + "_0", sp + "_1", sp + "g"], 0, i1)
        ts(T.L[:, 0:W + M].indirect(off), T.ec[:], -2048.0, OFF, OP.mult, OP.add, ["ec0", "ec1", "ou"], LK, M, "s")
        if last:
            dma("S", "dyn0", T.yn[:, 0:n0], T.L[:, 0:n0], 512 * n0, LK[:4] + ["~yx%d" % j for j in range(YF)], [])

        PE, KE = (P[2][:, 0:M], P[EB][:, M:2 * M]), ("P2", "P%d" % EB)
        ck = T["CKE1" if last else "CKE0"]
        if EB == 2:
            mm(P[2][:, 0:2 * M], T.IU[:], ck[:], True, ["IU", "CKE0", "CKE1"], "P2", 2 * M)
        for s, val, keys in ((0, T.av, ["av"]), (1, T.bv, ["bv%d" % j for j in range(len(CH))])):
            if EB != 2:
                mm(PE[s], T.IU[:], ck[:, M * s:M * s + M], True, ["IU", "CKE0", "CKE1"], KE[s], M)
            mm(PE[s], T.I[:], val[:], False, ["I"] + keys, KE[s], M)

        def e_sum(Z, pair, o, keys):
            if EB == 2 and pair[0][0] == pair[1][0]:
                mm(P[2][:, 0:2 * M], sel(Z, pair[0][0]), T.cE[:, o:o + 2 * M], False, [Z] + keys, "P2", 2 * M)
            else:
                for h, (k, s) in enumerate(pair):
                    mm(PE[s], sel(Z, k), T.cE[:, o + M * h:o + M * h + M], False, [Z] + keys[h % len(keys):h % len(keys) + 1], KE[s], M)

        halves = [(k, s) for s in (0, 1) for k in range(kd, kd + 2 * NPRE)] + [(k, s) for k in range(kd + 2 * NPRE, 16) for s in (0, 1)]
        for u in range(len(halves) // 2):
            kb, o, pair, Pb = "P%d" % (3 + u % 2), 2 * M * (kd + u), halves[2 * u:2 * u + 2], P[3 + u % 2]
            whole = pair[0][0] == pair[1][0]
            if whole:
                unit("lay", t, u)
                mm(Pb[:, 0:2 * M], T.I[:], T.xab[:, pair[0][0]:32 * M:16], True, ["I"] + XA + XB, kb, 2 * M)
            for h, (k, s) in enumerate(pair):
                unit("lay", t, u)
                mm(Pb[:, M * h:M * h + M], T.Pm[:], E, not whole, ["Pm", "E"], kb, M)
                if not whole:
                    unit("lay", t, u)
                    mm(Pb[:, M * h:M * h + M], T.I[:], T.xab[:, 16 * M * s + k:16 * M * (s + 1):16], False, ["I"] + (XB if s else XA), kb, M)
            ac(T.cE[:, o:o + 2 * M], Pb[:, 0:2 * M], [kb], ["cEs%d" % u], AF.Sign, 0.25, n=2 * M)
            e_sum("Z8", pair, o, ["cEs%d" % u])
        for k in range(kd):
            for s in (0, 1):
                o, key = 2 * M * k + M * s, "cE%d_%d" % (k, s)
                tt(T.cE[:, o:o + M], T.xab[:, 16 * M * s + k:16 * M * (s + 1):16], P[0][:, M:2 * M], OP.is_ge, (XB if s else XA) + ["P0"], [key], M)
            e_sum("Z16", ((k, 0), (k, 1)), 2 * M * k, ["cE%d_0" % k, "cE%d_1" % k])
        tt(T.k2[:], PE[0], T.NE[:], OP.max, [KE[0], "NE"], ["k2"], M)
        tt(PE[1], PE[1], T.k2[:], OP.max, [KE[1], "k2"], [KE[1]], M)
        if EV or last:
            ts(T.rE[:], PE[1], -OFF, None, OP.add, None, [KE[1]], ["rE"], M)
        else:
            ac(T.rE[:], PE[1], [KE[1]], ["rE"], AF.Identity, -OFF, n=M)
        tt(T.L[:, n0:n1], PE[1], T.rE[:], OP.subtract, [KE[1], "rE"], ["Ln"], M)
        if last:
            dma("A", "dyn1", T.yn[:, n0:n1], T.L[:, n0:n1], 512 * M, ["Ln"], [])

    if not PLAN:
        members = {}
        for i in range(len(calls)):
            members.setdefault(units.get(i, i), []).append(i)
        members = sorted(members.values(), key=lambda m: m[-1])
        node = {i: x for x, m in enumerate(members) for i in m}

        def gap(i, j, q):
            if calls[i][0] != calls[j][0] or calls[j][5]:
                return q["hop"] + (calls[j][3](q) if calls[i][4][j] else 0.0)
            return q["own"] if calls[i][0] != "P" and calls[i][4][j] else 0.0

        guesses = [([sum(calls[i][2](q) for i in m) for m in members], [calls[m[0]][3](q) for m in members],
                    [list({node[j]: gap(i, j, q) for i in m for j in calls[i][4] if node[j] != x}.items()) for x, m in enumerate(members)])
                   for q in GUESS]
        PLAN["order"] = [i for x in schedule([calls[m[0]][0] for m in members], guesses) for i in members[x]]
    order = PLAN["order"]
    closes = {calls[i][6]: i for i in order if calls[i][6] is not None}
    count = {"sV": 0, "sA": 0, "sP": 0, "sG": 0}
    seen = {e: {} for e in Q}
    clock, event = {}, {}

    def need(e, ev):
        s, val = ev
        if seen[e].get(s, 0) >= val:
            return
        Q[e].wait_ge(T.sem[s], val)
        for s2, v2 in clock.get(ev, {}).items():
            if seen[e].get(s2, 0) < v2:
                seen[e][s2] = v2
        seen[e][s] = val

    for i in order:
        e, call, _, _, deps, ev, group = calls[i]
        evs = {}
        for j in deps:
            s, val = event[j]
            if deps[j] and (s != "sP" or e != "P"):
                evs[s] = max(evs.get(s, 0), val)
        for s in sorted(evs, key=lambda s: s == "s" + e):
            need(e, (s, evs[s]))
        if ev is None:
            count["s" + e] += 1
            ev = ("s" + e, count["s" + e])
            (call() if group is None else call(closes[group] == i)).then_inc(T.sem[ev[0]], 1)
            clock[ev] = dict(seen[e])
        elif e == "G":
            call()
        else:
            call().then_inc(T.sem[ev[0]], 16)
            clock[ev] = dict(seen[e])
        event[i] = ev

    g.wait_ge(T.sem["sent"], (3 - ONE) * (RO - 1) * n_eng)
    for s in ("sV", "sA", "sP", "sG"):
        need("G", (s, count[s]))
    for s in ("dyx0", "dyx1", "dyn0", "dyn1"):
        need("G", (s, 16))
